import numpy as np
import ml_dtypes


def mxq(x, axis, fmt="e4m3"):
    dtype, down = {"e4m3": (ml_dtypes.float8_e4m3fn, 7), "e5m2": (ml_dtypes.float8_e5m2, 14)}[fmt]
    v = np.moveaxis(np.asarray(x, np.float32).astype(ml_dtypes.bfloat16).astype(np.float64), axis, -1)
    blocks = v.reshape(v.shape[:-1] + (-1, 32))
    amax = np.abs(blocks).max(-1, keepdims=True)
    byte = np.maximum(np.where(amax > 0, np.frexp(amax)[1] - 1 + 127, 0) - down, 1)
    scale = np.exp2(byte - 127.0)
    codes = (blocks / scale).astype(np.float32).astype(dtype).astype(np.float64)
    return np.moveaxis((codes * scale).reshape(v.shape), -1, axis)


WIDE = False


def mx_kscale(k):
    if not WIDE:
        return np.ones(k)
    levels = np.array([10, -10, 5, -5, 0])
    if k % 512:
        return np.exp2(np.random.permutation(np.resize(levels, k // 32))).repeat(32)
    a = np.empty((k // 512, 16))
    for p in range(k // 512):
        a[p, :8] = np.random.permutation(np.resize(levels, 8))
        for g in range(8):
            far = levels[np.abs(levels - a[p, g]) >= 10]
            a[p, g + 8] = far[np.random.randint(len(far))]
    return np.exp2(a.ravel()).repeat(32)


def f64(x):
    return np.asarray(x).astype(np.float64)


def striped(idx):
    return np.tile(idx.reshape(-1, 16).T, (8, 1)).astype(np.uint16)


def unstriped(offs):
    return offs[:16].T.reshape(-1).astype(np.int64)


E2M1 = np.array([0.0, 0.5, 1.0, 1.5, 2.0, 3.0, 4.0, 6.0, -0.0, -0.5, -1.0, -1.5, -2.0, -3.0, -4.0, -6.0])


def pack_weight(w, fmt):
    k, n = w.shape
    w = f64(np.asarray(w, np.float32).astype(ml_dtypes.bfloat16)).reshape(k // 32, 32, n)
    amax = np.abs(w).max(1)
    if fmt == "e4m3":
        byte = np.frexp(amax)[1] - 1 + 127 - 7
    else:
        mant, ex = np.frexp(amax / 6.0)
        byte = np.where(mant > 0.5, ex, ex - 1) + 127
    byte = np.clip(np.where(amax > 0, byte, 1), 1, 254)
    scaled = (w * np.exp2(127.0 - byte)[:, None, :]).reshape(k, n).astype(np.float32)
    by_word = np.ascontiguousarray(scaled.reshape(k // 512, 128, 4, n).transpose(0, 1, 3, 2))
    if fmt == "e4m3":
        words = by_word.astype(ml_dtypes.float8_e4m3fn).view(np.uint8)
    else:
        c = by_word.astype(ml_dtypes.float4_e2m1fn).view(np.uint8) & 0xF
        words = (c[..., 0::2] | (c[..., 1::2] << 4)).reshape(k // 512, 128, 2 * n)
    return np.ascontiguousarray(words), np.ascontiguousarray(byte.astype(np.uint8).reshape(k // 512, 16, n))


def unpack_weight(words, scales, fmt):
    g, _, n = scales.shape
    words = np.ascontiguousarray(words).reshape(g, 128, n, -1)
    if fmt == "e4m3":
        vals = words.view(ml_dtypes.float8_e4m3fn).astype(np.float64)
    else:
        nib = np.empty((g, 128, n, 4), np.uint8)
        nib[..., 0::2] = words & 0xF
        nib[..., 1::2] = words >> 4
        vals = E2M1[nib]
    vals = vals * np.repeat(np.exp2(scales.astype(np.float64) - 127.0), 8, axis=1)[..., None]
    return vals.transpose(0, 1, 3, 2).reshape(g * 512, n)


def gelu(v):
    return 0.5 * v * (1.0 + np.tanh(np.sqrt(2.0 / np.pi) * (v + 0.044715 * v**3)))


K, H, N, T, S, T2, P = 1024, 512, 768, 2048, 1024, 2048, 1024

def setup_inputs():
    n = np.random.standard_normal
    s = mx_kscale(K)[:, None]
    u = mx_kscale(H)[:, None]
    tab_words, tab_scales = pack_weight(n((K, T)) * s, "e4m3")
    w2_words, w2_scales = pack_weight(n((K, H)) / np.sqrt(K) / s, "e4m3")
    w3_words, w3_scales = pack_weight(n((K, H)) / np.sqrt(K) / s, "e2m1")
    return {
        "tab_words": tab_words, "tab_scales": tab_scales,
        "offs": striped(np.random.permutation(T)[:S]),
        "offs2": striped(np.random.permutation(T2)[:S]),
        "offs3": striped(np.random.permutation(T2)[:P]),
        "w1": (n((K, H)) / np.sqrt(K) / s).astype(np.float32),
        "w2_words": w2_words, "w2_scales": w2_scales,
        "w3_words": w3_words, "w3_scales": w3_scales,
        "wgs": np.exp(0.3 * n((128, S))).astype(np.float32),
        "load": (n((H, P)) * u).astype(np.float32),
        "wo": (n((H, N)) / np.sqrt(H) / u).astype(np.float32),
    }

def reference(tab_words, tab_scales, offs, offs2, offs3, w1, w2_words, w2_scales,
              w3_words, w3_scales, wgs, load, wo):
    v = unpack_weight(tab_words, tab_scales, "e4m3")[:, unstriped(offs)]
    w2 = unpack_weight(w2_words, w2_scales, "e4m3")
    w3 = unpack_weight(w3_words, w3_scales, "e2m1")
    e1 = mxq(f64(w1), 0, "e4m3").T @ v
    e2 = w2.T @ v
    e3 = w3.T @ v
    h = np.maximum(e1, e2) - np.minimum(e2, e3)
    page = np.zeros((H, T2))
    page[:, unstriped(offs2)] = np.tile(f64(wgs), (H // 128, 1)) * h
    x = page[:, unstriped(offs3)]
    z = np.exp(-x) * f64(load)
    return mxq(f64(wo), 0, "e4m3").T @ mxq(z, 0, "e4m3")

@@ -1,0 +1,293 @@
+from contextlib import ExitStack
+
+import concourse.mybir as mybir
+from concourse.masks import make_identity
+
+K, H, N, T, S, T2, M = 1024, 512, 768, 2048, 1024, 2048, 1024
+FLOPS = 2 * K * H * S * 3 + 2 * H * N * M
+
+F32 = mybir.dt.float32
+BF16 = mybir.dt.bfloat16
+I32 = mybir.dt.int32
+U32 = mybir.dt.uint32
+U16 = mybir.dt.uint16
+U8 = mybir.dt.uint8
+FP8X4 = mybir.dt.float8_e4m3fn_x4
+FP4X4 = mybir.dt.float4_e2m1fn_x4
+ALU = mybir.AluOpType
+ACT = mybir.ActivationFunctionType
+
+P = 128
+PACK = 4
+PASSES = K // (P * PACK)
+BLOCKS = H // P
+BANK = 512
+FIRST = 256
+CHUNK = 256
+
+
+def interleave(engine_copy, dst, src):
+    engine_copy(
+        out=dst.rearrange("p (c e) i -> p c i e", e=4),
+        in_=src.rearrange("p i (c e) -> p c i e", e=4),
+    )
+
+
+def tile_list_latency_envelopes_kernel(
+    tc, tab_words, tab_scales, offs, offs2, offs3, w1, w2_words, w2_scales,
+    w3_words, w3_scales, wgs, load, wo, out,
+):
+    nc = tc.nc
+    with ExitStack() as ctx:
+        keep = ctx.enter_context(tc.tile_pool(name="keep", bufs=1))
+        ring = ctx.enter_context(tc.tile_pool(name="ring", bufs=2))
+        psum = ctx.enter_context(tc.psum_pool(name="psum", bufs=4))
+
+        idx1 = keep.tile([P, S // 16], U16, name="idx1")
+        idx2 = keep.tile([P, S // 16], U16, name="idx2")
+        idx3 = keep.tile([P, M // 16], U16, name="idx3")
+
+        tab_s = keep.tile([P, PASSES * T], U8, name="tab_s", align_bytes=64)
+        w_s = keep.tile([P, 2, PASSES, H], U8, name="w_s", align_bytes=64)
+        nc.vector.memset(tab_s[:].bitcast(I32), 0)
+        nc.gpsimd.memset(w_s[:].rearrange("p w a c -> p (w a c)").bitcast(I32), 0)
+        pages = [keep.tile([P, T2], F32, name="page%d" % b) for b in range(2)]
+        for b in range(2):
+            nc.vector.memset(pages[b][:], 0.0)
+
+        warm = keep.tile([P, 2], F32, name="warm")
+        nc.gpsimd.memset(warm[:, 0:1], 0.0)
+
+        nc.sync.dma_start(idx1[:], offs)
+        tab_w = [keep.tile([P, T], I32, name="tab_w%d" % a, tag="late%d" % a) for a in range(PASSES)]
+        nc.sync.dma_start(tab_w[0][:], tab_words[0].rearrange("p t i -> p (t i)").bitcast(I32))
+        tab_s_words = tab_s[:].bitcast(I32).rearrange("p (a t) -> p a t", a=PASSES)
+        for q in range(4):
+            nc.sync.dma_start(
+                tab_s_words[32 * q : 32 * q + 4, :, :],
+                tab_scales.bitcast(I32)[:, 4 * q : 4 * q + 4, :].rearrange("a r t -> r a t"),
+            )
+        ident = keep.tile([P, P], F32, name="ident")
+        make_identity(nc, ident[:])
+        nc.scalar.activation(warm[:, 1:2], warm[:, 0:1], ACT.Exp)
+
+        nc.sync.dma_start(tab_w[1][:], tab_words[1].rearrange("p t i -> p (t i)").bitcast(I32))
+
+        w1_rows = w1.rearrange("(a p i) c -> a p i c", a=PASSES, i=PACK)
+        w2_hbm = w2_words.rearrange("a p c i -> p a (c i)")
+        w3_hbm = w3_words.rearrange("a p c -> p a c")
+        w1_raw, w2_c, w3_c = {}, {}, {}
+
+        def load_weights(b0, b1):
+            width = (b1 - b0) * P
+            raws = []
+            for a in range(PASSES):
+                raw = keep.tile([P, PACK, width], F32, name="w1_raw%d_%d" % (b0, a))
+                nc.sync.dma_start(raw[:], w1_rows[a][:, :, b0 * P : b1 * P])
+                raws.append(raw)
+            c2 = keep.tile([P, PASSES, width], U32, name="w2_c%d" % b0, align_bytes=64)
+            nc.sync.dma_start(c2[:].bitcast(I32), w2_hbm[:, :, 4 * b0 * P : 4 * b1 * P].bitcast(I32))
+            c3 = keep.tile([P, PASSES, 2 * width], U8, name="w3_c%d" % b0, align_bytes=64)
+            nc.sync.dma_start(c3[:].bitcast(I32), w3_hbm[:, :, 2 * b0 * P : 2 * b1 * P].bitcast(I32))
+            for b in range(b0, b1):
+                o = (b - b0) * P
+                for a in range(PASSES):
+                    w1_raw[b, a] = raws[a][:, :, o : o + P]
+                    w2_c[b, a] = c2[:, a, o : o + P].bitcast(FP8X4)
+                    w3_c[b, a] = c3[:, a, 2 * o : 2 * (o + P)].bitcast(FP4X4)
+
+        load_weights(0, 1)
+        for w, scales in enumerate((w2_scales, w3_scales)):
+            for q in range(4):
+                nc.sync.dma_start(
+                    w_s[32 * q : 32 * q + 4, w, :, :].bitcast(I32),
+                    scales.bitcast(I32)[:, 4 * q : 4 * q + 4, :].rearrange("a r t -> r a t"),
+                )
+        nc.sync.dma_start(idx2[:], offs2)
+        wgs_sb = keep.tile([P, S], F32, name="wgs_sb")
+        nc.sync.dma_start(wgs_sb[:], wgs)
+        load_weights(1, BLOCKS)
+        nc.sync.dma_start(idx3[:], offs3)
+        wo_raw = keep.tile([P, PACK, N], F32, name="wo_raw")
+        nc.sync.dma_start(wo_raw[:], wo.rearrange("(p i) n -> p i n", i=PACK))
+        load_raw = [keep.tile([P, PACK, CHUNK], F32, name="load_raw%d" % c) for c in range(M // CHUNK)]
+        load_rows = load.rearrange("(p i) m -> p i m", i=PACK)
+        for c in range(M // CHUNK):
+            nc.sync.dma_start(load_raw[c][:], load_rows[:, :, c * CHUNK : (c + 1) * CHUNK])
+
+        v_w = [keep.tile([P, S], U32, name="v_w%d" % a, align_bytes=64) for a in range(PASSES)]
+        v_s = [keep.tile([P, S], U8, name="v_s%d" % a, align_bytes=64) for a in range(PASSES)]
+
+        def gather_table(j0, j1):
+            picks = idx1[:, j0 // 16 : j1 // 16]
+            nc.vector.tensor_copy(v_w[0][:, j0:j1], tab_w[0][:].bitcast(U32).indirect(picks))
+            for a in range(PASSES):
+                nc.vector.tensor_copy(v_s[a][:, j0:j1], tab_s[:, a * T : (a + 1) * T].indirect(picks))
+            nc.vector.tensor_copy(v_w[1][:, j0:j1], tab_w[1][:].bitcast(U32).indirect(picks))
+
+        w1_c, w1_s = {}, {}
+        w1_bf = [keep.tile([P, PASSES, P, PACK], BF16, name="w1_bf%d" % b, align_bytes=64) for b in range(BLOCKS)]
+
+        def quantize_w1(b):
+            for a in range(PASSES):
+                interleave(nc.scalar.copy, w1_bf[b][:, a, :, :], w1_raw[b, a])
+            codes = keep.tile([P, PASSES * P], U32, name="w1_c%d" % b, align_bytes=64)
+            scales = keep.tile([P, PASSES * P], U8, name="w1_s%d" % b, align_bytes=64)
+            nc.vector.quantize_mx(
+                out=codes[:].bitcast(FP8X4), scales=scales[:],
+                in_=w1_bf[b][:].rearrange("p a c i -> p (a c i)"),
+            )
+            for a in range(PASSES):
+                w1_c[b, a] = codes[:, a * P : (a + 1) * P].bitcast(FP8X4)
+                w1_s[b, a] = scales[:, a * P : (a + 1) * P]
+
+        gather_table(0, FIRST)
+        quantize_w1(0)
+        gather_table(FIRST, S)
+        for b in range(2, BLOCKS):
+            page = keep.tile([P, T2], F32, name="page%d" % b, tag="late%d" % (b - 2))
+            nc.gpsimd.memset(page[:], 0.0)
+            pages.append(page)
+
+        wo_bf = [keep.tile([P, 2 * P, PACK], BF16, name="wo_bf%d" % k, align_bytes=64) for k in range(N // (2 * P))]
+        wo_c = keep.tile([P, N], U32, name="wo_c", align_bytes=64)
+        wo_s = keep.tile([P, N], U8, name="wo_s", align_bytes=64)
+        load_il = [keep.tile([P, CHUNK, PACK], F32, name="load_il%d" % c) for c in range(M // CHUNK)]
+
+        def quantize_wo(k):
+            cols = slice(2 * P * k, 2 * P * (k + 1))
+            interleave(nc.scalar.copy, wo_bf[k][:], wo_raw[:, :, cols])
+            nc.vector.quantize_mx(
+                out=wo_c[:, cols].bitcast(FP8X4), scales=wo_s[:, cols],
+                in_=wo_bf[k][:].rearrange("p n i -> p (n i)"),
+            )
+
+        def weave_load(c):
+            interleave(nc.scalar.copy, load_il[c][:], load_raw[c][:])
+
+        stage = [keep.tile([P, BLOCKS * CHUNK], F32, name="stage%d" % i) for i in range(2)]
+
+        def product(b, j0, j1, codes, scales):
+            bank = psum.tile([P, BANK], F32, name="e_bank", tag="e")
+            for jt in range(j0, j1, P):
+                for a in range(PASSES):
+                    nc.tensor.matmul_mx(
+                        out=bank[:, jt - j0 : jt - j0 + P],
+                        lhsT=v_w[a][:, jt : jt + P].bitcast(FP8X4),
+                        lhsT_scale=v_s[a][:, jt : jt + P],
+                        rhs=codes[b, a],
+                        rhs_scale=scales[a],
+                        start=(a == 0),
+                        stop=(a == PASSES - 1),
+                    )
+            return bank
+
+        def difference(width, plus, minus):
+            bank = psum.tile([P, BANK], F32, name="d_bank", tag="d")
+            for o in range(0, width, P):
+                nc.tensor.matmul(bank[:, o : o + P], plus[:, o : o + P], ident[:],
+                                 start=True, stop=False, is_transpose=True)
+                nc.tensor.matmul(bank[:, o : o + P], minus[:, o : o + P], ident[:],
+                                 start=False, stop=True, is_transpose=True)
+            return bank
+
+        def envelope(u, b, j0, j1, above, neg3):
+            width = j1 - j0
+            cols = slice(b * P, (b + 1) * P)
+            e2 = product(b, j0, j1, w2_c, [w_s[:, 0, a, cols] for a in range(PASSES)])
+            e1 = product(b, j0, j1, w1_c, [w1_s[b, a] for a in range(PASSES)])
+            e3 = product(b, j0, j1, w3_c, [w_s[:, 1, a, cols] for a in range(PASSES)])
+            pos2 = ring.tile([P, BANK], F32, name="pos2")
+            nc.scalar.copy(pos2[:, :width], e2[:, :width])
+            neg1 = ring.tile([P, BANK], F32, name="neg1")
+            nc.scalar.activation(neg1[:, :width], e1[:, :width], ACT.Copy, scale=-1.0)
+            nc.scalar.activation(neg3[:, :width], e3[:, :width], ACT.Copy, scale=-1.0)
+            d21 = difference(width, pos2, neg1)
+            d23 = difference(width, pos2, neg3)
+            nc.scalar.activation(above[:, :width], d21[:, :width], ACT.Relu, scale=-1.0)
+            h = stage[u % 2][:, :width]
+            nc.vector.scalar_tensor_tensor(h, d23[:, :width], 0.0, above[:, :width], ALU.max, ALU.add)
+            nc.vector.tensor_tensor(
+                pages[b][:].indirect(idx2[:, j0 // 16 : j1 // 16]), h, wgs_sb[:, j0:j1], ALU.mult
+            )
+
+        units = [(0, 0, FIRST), (0, FIRST, BANK), (0, BANK, S)]
+        units = units + [(b, j0, j0 + BANK) for b in range(1, BLOCKS) for j0 in range(0, S, BANK)]
+        side = [(w1_bf[b][:].rearrange("p a c i -> p (a c i)").bitcast(F32), quantize_w1, b) for b in range(1, BLOCKS)]
+        side = side + [(t[:].rearrange("p n i -> p (n i)").bitcast(F32), quantize_wo, k) for k, t in enumerate(wo_bf)]
+        side = side + [(t[:].rearrange("p n i -> p (n i)"), weave_load, c) for c, t in enumerate(load_il)]
+        for u, (b, j0, j1) in enumerate(units):
+            spare, job, arg = side[u]
+            if u == len(units) - 1:
+                neg3 = side[u + 1][0]
+            else:
+                neg3 = ring.tile([P, BANK], F32, name="neg3")
+            envelope(u, b, j0, j1, spare, neg3)
+            job(arg)
+        weave_load(M // CHUNK - 1)
+
+        out_rows = out.rearrange("(i p) m -> p i m", p=P)
+        chunks = M // CHUNK
+        picked = [t[:] for t in stage] + [t[:].rearrange("p m i -> p (m i)") for t in load_il[: chunks - 2]]
+        damp = {}
+
+        def fetch(c, b):
+            nc.vector.tensor_copy(
+                picked[c][:, b * CHUNK : (b + 1) * CHUNK],
+                pages[b][:].indirect(idx3[:, c * CHUNK // 16 : (c + 1) * CHUNK // 16]),
+            )
+
+        def damping(c):
+            for half in range(CHUNK // P):
+                x_t = psum.tile([P, BANK], F32, name="x_t", tag="e")
+                for b in range(BLOCKS):
+                    o = b * CHUNK + half * P
+                    nc.tensor.transpose(x_t[:, b * P : (b + 1) * P], picked[c][:, o : o + P], ident[:])
+                ex_t = ring.tile([P, PACK, P], F32, name="ex_t")
+                nc.scalar.activation(ex_t[:], x_t[:].rearrange("m (q i) -> m i q", i=PACK), ACT.Exp, scale=-1.0)
+                ex = psum.tile([P, PACK, P], F32, name="ex", tag="d")
+                for i in range(PACK):
+                    nc.tensor.transpose(ex[:, i, :], ex_t[:, i, :], ident[:])
+                damp[c, half] = ex
+
+        def signal(c):
+            z = ring.tile([P, CHUNK, PACK], BF16, name="z", align_bytes=64)
+            for half in range(CHUNK // P):
+                cols = slice(half * P, (half + 1) * P)
+                nc.vector.tensor_tensor(
+                    z[:, cols, :], damp[c, half][:].rearrange("q i m -> q m i"), load_il[c][:, cols, :], ALU.mult
+                )
+            return z
+
+        def finish(c, z):
+            z_c = ring.tile([P, CHUNK], U32, name="z_c", align_bytes=64)
+            z_s = ring.tile([P, CHUNK], U8, name="z_s", align_bytes=64)
+            nc.vector.quantize_mx(out=z_c[:].bitcast(FP8X4), scales=z_s[:], in_=z[:].rearrange("p m i -> p (m i)"))
+            for pair in range(N // (2 * P)):
+                acc = psum.tile([P, 2, CHUNK], F32, name="acc", tag="e")
+                for k in range(2):
+                    n0 = (2 * pair + k) * P
+                    nc.tensor.matmul_mx(
+                        out=acc[:, k, :], lhsT=wo_c[:, n0 : n0 + P].bitcast(FP8X4), lhsT_scale=wo_s[:, n0 : n0 + P],
+                        rhs=z_c[:].bitcast(FP8X4), rhs_scale=z_s[:], start=True, stop=True,
+                    )
+                res = ring.tile([P, 2, CHUNK], F32, name="res", bufs=4)
+                if c == chunks - 1 and pair == 1:
+                    nc.vector.tensor_copy(res[:], acc[:])
+                else:
+                    nc.scalar.copy(res[:], acc[:])
+                nc.sync.dma_start(out_rows[:, 2 * pair : 2 * pair + 2, c * CHUNK : (c + 1) * CHUNK], res[:])
+
+        for c in range(2):
+            for b in range(BLOCKS):
+                fetch(c, b)
+            damping(c)
+        for c in range(chunks):
+            z = signal(c)
+            if c + 2 < chunks:
+                fetch(c + 2, 0)
+            finish(c, z)
+            if c + 2 < chunks:
+                for b in range(1, BLOCKS):
+                    fetch(c + 2, b)
+                damping(c + 2)

@@ -47,44 +47,41 @@ def tile_list_latency_envelopes_kernel(
         idx2 = keep.tile([P, S // 16], U16, name="idx2")
         idx3 = keep.tile([P, M // 16], U16, name="idx3")
 
-        tab_s = keep.tile([P, PASSES * T], U8, name="tab_s", align_bytes=64)
+        tab_s = keep.tile([P, PASSES * T], U8, name="tab_s", tag="page1", align_bytes=64)
         w_s = keep.tile([P, 2, PASSES, H], U8, name="w_s", align_bytes=64)
-        nc.vector.memset(tab_s[:].bitcast(I32), 0)
-        nc.gpsimd.memset(w_s[:].rearrange("p w a c -> p (w a c)").bitcast(I32), 0)
-        pages = [keep.tile([P, T2], F32, name="page%d" % b) for b in range(2)]
-        for b in range(2):
-            nc.vector.memset(pages[b][:], 0.0)
+        nc.gpsimd.memset(tab_s[:].bitcast(I32), 0)
+        nc.vector.memset(w_s[:].rearrange("p w a c -> p (w a c)").bitcast(I32), 0)
+        pages = [keep.tile([P, T2], F32, name="page0")]
+        nc.vector.memset(pages[0][:], 0.0)
+
+        def open_page():
+            page = keep.tile([P, T2], F32, name="page", tag="page%d" % len(pages), align_bytes=64)
+            nc.gpsimd.memset(page[:], 0.0)
+            pages.append(page)
 
         warm = keep.tile([P, 2], F32, name="warm")
-        nc.gpsimd.memset(warm[:, 0:1], 0.0)
+        nc.vector.memset(warm[:, 0:1], 0.0)
 
         nc.sync.dma_start(idx1[:], offs)
-        tab_w = [keep.tile([P, T], I32, name="tab_w%d" % a, tag="late%d" % a) for a in range(PASSES)]
-        nc.sync.dma_start(tab_w[0][:], tab_words[0].rearrange("p t i -> p (t i)").bitcast(I32))
-        tab_s_words = tab_s[:].bitcast(I32).rearrange("p (a t) -> p a t", a=PASSES)
-        for q in range(4):
-            nc.sync.dma_start(
-                tab_s_words[32 * q : 32 * q + 4, :, :],
-                tab_scales.bitcast(I32)[:, 4 * q : 4 * q + 4, :].rearrange("a r t -> r a t"),
-            )
-        ident = keep.tile([P, P], F32, name="ident")
-        make_identity(nc, ident[:])
+        tab_w = [keep.tile([P, T], I32, name="tab_w%d" % a, tag="late%d" % a, align_bytes=64) for a in range(PASSES)]
         nc.scalar.activation(warm[:, 1:2], warm[:, 0:1], ACT.Exp)
-
-        nc.sync.dma_start(tab_w[1][:], tab_words[1].rearrange("p t i -> p (t i)").bitcast(I32))
 
         w1_rows = w1.rearrange("(a p i) c -> a p i c", a=PASSES, i=PACK)
         w2_hbm = w2_words.rearrange("a p c i -> p a (c i)")
         w3_hbm = w3_words.rearrange("a p c -> p a c")
         w1_raw, w2_c, w3_c = {}, {}, {}
 
-        def load_weights(b0, b1):
+        def load_w1(a, b0, b1):
+            raw = keep.tile([P, PACK, (b1 - b0) * P], F32, name="w1_raw%d_%d" % (b0, a))
+            nc.sync.dma_start(raw[:], w1_rows[a][:, :, b0 * P : b1 * P])
+            for b in range(b0, b1):
+                w1_raw[b, a] = raw[:, :, (b - b0) * P : (b - b0 + 1) * P]
+
+        def load_table(a):
+            nc.sync.dma_start(tab_w[a][:], tab_words[a].rearrange("p t i -> p (t i)").bitcast(I32))
+
+        def load_packed(b0, b1):
             width = (b1 - b0) * P
-            raws = []
-            for a in range(PASSES):
-                raw = keep.tile([P, PACK, width], F32, name="w1_raw%d_%d" % (b0, a))
-                nc.sync.dma_start(raw[:], w1_rows[a][:, :, b0 * P : b1 * P])
-                raws.append(raw)
             c2 = keep.tile([P, PASSES, width], U32, name="w2_c%d" % b0, align_bytes=64)
             nc.sync.dma_start(c2[:].bitcast(I32), w2_hbm[:, :, 4 * b0 * P : 4 * b1 * P].bitcast(I32))
             c3 = keep.tile([P, PASSES, 2 * width], U8, name="w3_c%d" % b0, align_bytes=64)
@@ -92,21 +89,37 @@ def tile_list_latency_envelopes_kernel(
             for b in range(b0, b1):
                 o = (b - b0) * P
                 for a in range(PASSES):
-                    w1_raw[b, a] = raws[a][:, :, o : o + P]
                     w2_c[b, a] = c2[:, a, o : o + P].bitcast(FP8X4)
                     w3_c[b, a] = c3[:, a, 2 * o : 2 * (o + P)].bitcast(FP4X4)
 
-        load_weights(0, 1)
-        for w, scales in enumerate((w2_scales, w3_scales)):
+        def load_scales(queue, w, scales):
             for q in range(4):
-                nc.sync.dma_start(
+                queue.dma_start(
                     w_s[32 * q : 32 * q + 4, w, :, :].bitcast(I32),
                     scales.bitcast(I32)[:, 4 * q : 4 * q + 4, :].rearrange("a r t -> r a t"),
                 )
+
+        load_scales(nc.gpsimd, 1, w3_scales)
+        ident = keep.tile([P, P], F32, name="ident")
+        make_identity(nc, ident[:])
+        load_w1(0, 0, 2)
+        tab_s_words = tab_s[:].bitcast(I32).rearrange("p (a t) -> p a t", a=PASSES)
+        for q in range(4):
+            nc.sync.dma_start(
+                tab_s_words[32 * q : 32 * q + 4, :, :],
+                tab_scales.bitcast(I32)[:, 4 * q : 4 * q + 4, :].rearrange("a r t -> r a t"),
+            )
+        load_w1(1, 0, 2)
+        load_table(0)
+        load_table(1)
+        load_scales(nc.sync, 0, w2_scales)
+        load_packed(0, 2)
         nc.sync.dma_start(idx2[:], offs2)
         wgs_sb = keep.tile([P, S], F32, name="wgs_sb")
         nc.sync.dma_start(wgs_sb[:], wgs)
-        load_weights(1, BLOCKS)
+        load_w1(0, 2, BLOCKS)
+        load_w1(1, 2, BLOCKS)
+        load_packed(2, BLOCKS)
         nc.sync.dma_start(idx3[:], offs3)
         wo_raw = keep.tile([P, PACK, N], F32, name="wo_raw")
         nc.sync.dma_start(wo_raw[:], wo.rearrange("(p i) n -> p i n", i=PACK))
@@ -115,18 +128,23 @@ def tile_list_latency_envelopes_kernel(
         for c in range(M // CHUNK):
             nc.sync.dma_start(load_raw[c][:], load_rows[:, :, c * CHUNK : (c + 1) * CHUNK])
 
-        v_w = [keep.tile([P, S], U32, name="v_w%d" % a, align_bytes=64) for a in range(PASSES)]
-        v_s = [keep.tile([P, S], U8, name="v_s%d" % a, align_bytes=64) for a in range(PASSES)]
+        v_w, v_s = {}, {}
 
-        def gather_table(j0, j1):
-            picks = idx1[:, j0 // 16 : j1 // 16]
-            nc.vector.tensor_copy(v_w[0][:, j0:j1], tab_w[0][:].bitcast(U32).indirect(picks))
+        def gather_words(a, j0, j1):
+            words = keep.tile([P, j1 - j0], U32, name="v_w%d_%d" % (a, j0), align_bytes=64)
+            nc.vector.tensor_copy(words[:], tab_w[a][:].bitcast(U32).indirect(idx1[:, j0 // 16 : j1 // 16]))
+            for jt in range(j0, j1, P):
+                v_w[a, jt] = words[:, jt - j0 : jt - j0 + P].bitcast(FP8X4)
+
+        def gather_scales(j0, j1, tag):
+            held = keep.tile([P, PASSES, j1 - j0], U8, name="v_s", tag=tag, align_bytes=64)
             for a in range(PASSES):
-                nc.vector.tensor_copy(v_s[a][:, j0:j1], tab_s[:, a * T : (a + 1) * T].indirect(picks))
-            nc.vector.tensor_copy(v_w[1][:, j0:j1], tab_w[1][:].bitcast(U32).indirect(picks))
+                nc.vector.tensor_copy(held[:, a, :], tab_s[:, a * T : (a + 1) * T].indirect(idx1[:, j0 // 16 : j1 // 16]))
+                for jt in range(j0, j1, P):
+                    v_s[a, jt] = held[:, a, jt - j0 : jt - j0 + P]
 
         w1_c, w1_s = {}, {}
-        w1_bf = [keep.tile([P, PASSES, P, PACK], BF16, name="w1_bf%d" % b, align_bytes=64) for b in range(BLOCKS)]
+        w1_bf = [keep.tile([P, PASSES, P, PACK], BF16, name="w1_bf", tag=("page%d" if b >= 2 else "w1_bf%d") % b, align_bytes=64) for b in range(BLOCKS)]
 
         def quantize_w1(b):
             for a in range(PASSES):
@@ -141,13 +159,15 @@ def tile_list_latency_envelopes_kernel(
                 w1_c[b, a] = codes[:, a * P : (a + 1) * P].bitcast(FP8X4)
                 w1_s[b, a] = scales[:, a * P : (a + 1) * P]
 
-        gather_table(0, FIRST)
+        gather_scales(0, BANK, "v_s")
         quantize_w1(0)
-        gather_table(FIRST, S)
-        for b in range(2, BLOCKS):
-            page = keep.tile([P, T2], F32, name="page%d" % b, tag="late%d" % (b - 2))
-            nc.gpsimd.memset(page[:], 0.0)
-            pages.append(page)
+        quantize_w1(1)
+        gather_words(0, 0, S)
+        gather_words(1, 0, FIRST)
+        gather_words(1, FIRST, BANK)
+        gather_words(1, BANK, S)
+        gather_scales(BANK, S, "late1")
+        open_page()
 
         wo_bf = [keep.tile([P, 2 * P, PACK], BF16, name="wo_bf%d" % k, align_bytes=64) for k in range(N // (2 * P))]
         wo_c = keep.tile([P, N], U32, name="wo_c", align_bytes=64)
@@ -168,22 +188,22 @@ def tile_list_latency_envelopes_kernel(
         stage = [keep.tile([P, BLOCKS * CHUNK], F32, name="stage%d" % i) for i in range(2)]
 
         def product(b, j0, j1, codes, scales):
-            bank = psum.tile([P, BANK], F32, name="e_bank", tag="e")
-            for jt in range(j0, j1, P):
-                for a in range(PASSES):
+            bank = psum.tile([P, BANK], F32, name="e_bank", tag="e", bufs=2)
+            for a in range(PASSES):
+                for jt in range(j0, j1, P):
                     nc.tensor.matmul_mx(
                         out=bank[:, jt - j0 : jt - j0 + P],
-                        lhsT=v_w[a][:, jt : jt + P].bitcast(FP8X4),
-                        lhsT_scale=v_s[a][:, jt : jt + P],
+                        lhsT=v_w[a, jt],
+                        lhsT_scale=v_s[a, jt],
                         rhs=codes[b, a],
                         rhs_scale=scales[a],
-                        start=(a == 0),
-                        stop=(a == PASSES - 1),
+                        start=(a == 0 and jt == j0),
+                        stop=(a == PASSES - 1 and jt == j1 - P),
                     )
             return bank
 
         def difference(width, plus, minus):
-            bank = psum.tile([P, BANK], F32, name="d_bank", tag="d")
+            bank = psum.tile([P, BANK], F32, name="d_bank", tag="d", bufs=6)
             for o in range(0, width, P):
                 nc.tensor.matmul(bank[:, o : o + P], plus[:, o : o + P], ident[:],
                                  start=True, stop=False, is_transpose=True)
@@ -191,44 +211,75 @@ def tile_list_latency_envelopes_kernel(
                                  start=False, stop=True, is_transpose=True)
             return bank
 
-        def envelope(u, b, j0, j1, above, neg3):
-            width = j1 - j0
-            cols = slice(b * P, (b + 1) * P)
-            e2 = product(b, j0, j1, w2_c, [w_s[:, 0, a, cols] for a in range(PASSES)])
-            e1 = product(b, j0, j1, w1_c, [w1_s[b, a] for a in range(PASSES)])
-            e3 = product(b, j0, j1, w3_c, [w_s[:, 1, a, cols] for a in range(PASSES)])
-            pos2 = ring.tile([P, BANK], F32, name="pos2")
-            nc.scalar.copy(pos2[:, :width], e2[:, :width])
-            neg1 = ring.tile([P, BANK], F32, name="neg1")
-            nc.scalar.activation(neg1[:, :width], e1[:, :width], ACT.Copy, scale=-1.0)
-            nc.scalar.activation(neg3[:, :width], e3[:, :width], ACT.Copy, scale=-1.0)
-            d21 = difference(width, pos2, neg1)
-            d23 = difference(width, pos2, neg3)
-            nc.scalar.activation(above[:, :width], d21[:, :width], ACT.Relu, scale=-1.0)
-            h = stage[u % 2][:, :width]
-            nc.vector.scalar_tensor_tensor(h, d23[:, :width], 0.0, above[:, :width], ALU.max, ALU.add)
-            nc.vector.tensor_tensor(
-                pages[b][:].indirect(idx2[:, j0 // 16 : j1 // 16]), h, wgs_sb[:, j0:j1], ALU.mult
-            )
+        def copy_out(name, bank, width, scale, into=None):
+            held = ring.tile([P, BANK], F32, name=name, bufs=3) if into is None else into
+            nc.scalar.activation(held[:, :width], bank[:, :width], ACT.Copy, scale=scale)
+            return held
 
-        units = [(0, 0, FIRST), (0, FIRST, BANK), (0, BANK, S)]
-        units = units + [(b, j0, j0 + BANK) for b in range(1, BLOCKS) for j0 in range(0, S, BANK)]
-        side = [(w1_bf[b][:].rearrange("p a c i -> p (a c i)").bitcast(F32), quantize_w1, b) for b in range(1, BLOCKS)]
-        side = side + [(t[:].rearrange("p n i -> p (n i)").bitcast(F32), quantize_wo, k) for k, t in enumerate(wo_bf)]
-        side = side + [(t[:].rearrange("p n i -> p (n i)"), weave_load, c) for c, t in enumerate(load_il)]
-        for u, (b, j0, j1) in enumerate(units):
-            spare, job, arg = side[u]
-            if u == len(units) - 1:
-                neg3 = side[u + 1][0]
-            else:
-                neg3 = ring.tile([P, BANK], F32, name="neg3")
-            envelope(u, b, j0, j1, spare, neg3)
-            job(arg)
-        weave_load(M // CHUNK - 1)
+        units = [(0, 0, FIRST), (0, FIRST, BANK), (1, 0, BANK), (0, BANK, S), (1, BANK, S)]
+        units = units + [(b, j0, j0 + BANK) for b in range(2, BLOCKS) for j0 in range(0, S, BANK)]
+        last = len(units) - 1
+        jobs = [(w1_bf[b][:].rearrange("p a c i -> p (a c i)").bitcast(F32), quantize_w1, b) for b in range(2, BLOCKS)]
+        jobs = jobs + [(t[:].rearrange("p n i -> p (n i)").bitcast(F32), quantize_wo, k) for k, t in enumerate(wo_bf)]
+        jobs = jobs + [(t[:].rearrange("p n i -> p (n i)"), weave_load, c) for c, t in enumerate(load_il)]
+        pos2, neg1, neg3, above = {}, {}, {}, {}
+
+        def estimate2(u):
+            b, j0, j1 = units[u]
+            bank = product(b, j0, j1, w2_c, [w_s[:, 0, a, b * P : (b + 1) * P] for a in range(PASSES)])
+            pos2[u] = copy_out("pos2", bank, j1 - j0, 1.0)
+
+        def estimate1(u):
+            b, j0, j1 = units[u]
+            bank = product(b, j0, j1, w1_c, [w1_s[b, a] for a in range(PASSES)])
+            neg1[u] = copy_out("neg1", bank, j1 - j0, -1.0, jobs[-2][0] if u == last else None)
+
+        def estimate3(u):
+            b, j0, j1 = units[u]
+            bank = product(b, j0, j1, w3_c, [w_s[:, 1, a, b * P : (b + 1) * P] for a in range(PASSES)])
+            neg3[u] = copy_out("neg3", bank, j1 - j0, -1.0, jobs[-1][0] if u == last else None)
+
+        def upper(u):
+            b, j0, j1 = units[u]
+            width = j1 - j0
+            bank = difference(width, pos2[u], neg1[u])
+            above[u] = jobs[u - 2][0] if u >= 2 else ring.tile([P, BANK], F32, name="above")
+            nc.scalar.activation(above[u][:, :width], bank[:, :width], ACT.Relu, scale=-1.0)
+
+        def lower_and_put(u):
+            b, j0, j1 = units[u]
+            width = j1 - j0
+            bank = difference(width, pos2[u], neg3[u])
+            h = stage[u % 2][:, :width]
+            nc.vector.scalar_tensor_tensor(h, bank[:, :width], 0.0, above[u][:, :width], ALU.max, ALU.add)
+            nc.vector.tensor_tensor(pages[b][:].indirect(idx2[:, j0 // 16 : j1 // 16]), h, wgs_sb[:, j0:j1], ALU.mult)
+            if u >= 2:
+                jobs[u - 2][1](jobs[u - 2][2])
+
+        estimate2(0)
+        estimate1(0)
+        estimate3(0)
+        upper(0)
+        lower_and_put(0)
+        estimate2(1)
+        estimate1(1)
+        estimate3(1)
+        for u in range(1, last):
+            estimate2(u + 1)
+            upper(u)
+            estimate1(u + 1)
+            lower_and_put(u)
+            estimate3(u + 1)
+            if u in (2, 3):
+                open_page()
+        upper(last)
+        lower_and_put(last)
+        weave_load(2)
+        weave_load(3)
 
         out_rows = out.rearrange("(i p) m -> p i m", p=P)
         chunks = M // CHUNK
-        picked = [t[:] for t in stage] + [t[:].rearrange("p m i -> p (m i)") for t in load_il[: chunks - 2]]
+        picked = [t[:] for t in reversed(stage)] + [t[:].rearrange("p m i -> p (m i)") for t in load_il[: chunks - 2]]
         damp = {}
 
         def fetch(c, b):
@@ -239,13 +290,13 @@ def tile_list_latency_envelopes_kernel(
 
         def damping(c):
             for half in range(CHUNK // P):
-                x_t = psum.tile([P, BANK], F32, name="x_t", tag="e")
+                x_t = psum.tile([P, BANK], F32, name="x_t", tag="e", bufs=2)
                 for b in range(BLOCKS):
                     o = b * CHUNK + half * P
                     nc.tensor.transpose(x_t[:, b * P : (b + 1) * P], picked[c][:, o : o + P], ident[:])
                 ex_t = ring.tile([P, PACK, P], F32, name="ex_t")
                 nc.scalar.activation(ex_t[:], x_t[:].rearrange("m (q i) -> m i q", i=PACK), ACT.Exp, scale=-1.0)
-                ex = psum.tile([P, PACK, P], F32, name="ex", tag="d")
+                ex = psum.tile([P, PACK, P], F32, name="ex", tag="d", bufs=6)
                 for i in range(PACK):
                     nc.tensor.transpose(ex[:, i, :], ex_t[:, i, :], ident[:])
                 damp[c, half] = ex
@@ -259,19 +310,22 @@ def tile_list_latency_envelopes_kernel(
                 )
             return z
 
-        def finish(c, z):
+        def quantize_z(z):
             z_c = ring.tile([P, CHUNK], U32, name="z_c", align_bytes=64)
             z_s = ring.tile([P, CHUNK], U8, name="z_s", align_bytes=64)
             nc.vector.quantize_mx(out=z_c[:].bitcast(FP8X4), scales=z_s[:], in_=z[:].rearrange("p m i -> p (m i)"))
+            return z_c, z_s
+
+        def project(c, z_c, z_s):
             for pair in range(N // (2 * P)):
-                acc = psum.tile([P, 2, CHUNK], F32, name="acc", tag="e")
+                acc = psum.tile([P, 2, CHUNK], F32, name="acc", tag="d", bufs=6)
                 for k in range(2):
                     n0 = (2 * pair + k) * P
                     nc.tensor.matmul_mx(
                         out=acc[:, k, :], lhsT=wo_c[:, n0 : n0 + P].bitcast(FP8X4), lhsT_scale=wo_s[:, n0 : n0 + P],
                         rhs=z_c[:].bitcast(FP8X4), rhs_scale=z_s[:], start=True, stop=True,
                     )
-                res = ring.tile([P, 2, CHUNK], F32, name="res", bufs=4)
+                res = ring.tile([P, 2, CHUNK], F32, name="res", bufs=12)
                 if c == chunks - 1 and pair == 1:
                     nc.vector.tensor_copy(res[:], acc[:])
                 else:
@@ -286,8 +340,9 @@ def tile_list_latency_envelopes_kernel(
             z = signal(c)
             if c + 2 < chunks:
                 fetch(c + 2, 0)
-            finish(c, z)
+            z_c, z_s = quantize_z(z)
             if c + 2 < chunks:
                 for b in range(1, BLOCKS):
                     fetch(c + 2, b)
                 damping(c + 2)
+            project(c, z_c, z_s)

@@ -24,13 +24,11 @@ BLOCKS = H // P
 BANK = 512
 FIRST = 256
 CHUNK = 256
+EB = 2
 
 
 def interleave(engine_copy, dst, src):
-    engine_copy(
-        out=dst.rearrange("p (c e) i -> p c i e", e=4),
-        in_=src.rearrange("p i (c e) -> p c i e", e=4),
-    )
+    engine_copy(out=dst, in_=src.rearrange("p i c -> p c i"))
 
 
 def tile_list_latency_envelopes_kernel(
@@ -47,23 +45,25 @@ def tile_list_latency_envelopes_kernel(
         idx2 = keep.tile([P, S // 16], U16, name="idx2")
         idx3 = keep.tile([P, M // 16], U16, name="idx3")
 
-        tab_s = keep.tile([P, PASSES * T], U8, name="tab_s", tag="page1", align_bytes=64)
+        tab_s = keep.tile([P, T], U8, name="tab_s", align_bytes=64)
+        v_s1 = keep.tile([P, S], U8, name="v_s1", align_bytes=64)
         w_s = keep.tile([P, 2, PASSES, H], U8, name="w_s", align_bytes=64)
         nc.gpsimd.memset(tab_s[:].bitcast(I32), 0)
         nc.vector.memset(w_s[:].rearrange("p w a c -> p (w a c)").bitcast(I32), 0)
+        nc.vector.memset(v_s1[:].bitcast(I32), 0)
         pages = [keep.tile([P, T2], F32, name="page0")]
-        nc.vector.memset(pages[0][:], 0.0)
+        nc.vector.memset(pages[0][:].bitcast(I32), 0)
 
         def open_page():
             page = keep.tile([P, T2], F32, name="page", tag="page%d" % len(pages), align_bytes=64)
-            nc.gpsimd.memset(page[:], 0.0)
+            nc.gpsimd.memset(page[:].bitcast(I32), 0)
             pages.append(page)
 
         warm = keep.tile([P, 2], F32, name="warm")
         nc.vector.memset(warm[:, 0:1], 0.0)
 
         nc.sync.dma_start(idx1[:], offs)
-        tab_w = [keep.tile([P, T], I32, name="tab_w%d" % a, tag="late%d" % a, align_bytes=64) for a in range(PASSES)]
+        tab_w = [keep.tile([P, T], I32, name="tab_w%d" % a, tag=("page1", "late1")[a], align_bytes=64) for a in range(PASSES)]
         nc.scalar.activation(warm[:, 1:2], warm[:, 0:1], ACT.Exp)
 
         w1_rows = w1.rearrange("(a p i) c -> a p i c", a=PASSES, i=PACK)
@@ -93,27 +93,26 @@ def tile_list_latency_envelopes_kernel(
                     w3_c[b, a] = c3[:, a, 2 * o : 2 * (o + P)].bitcast(FP4X4)
 
         def load_scales(queue, w, scales):
-            for q in range(4):
+            for r in range(4):
                 queue.dma_start(
-                    w_s[32 * q : 32 * q + 4, w, :, :].bitcast(I32),
-                    scales.bitcast(I32)[:, 4 * q : 4 * q + 4, :].rearrange("a r t -> r a t"),
+                    w_s[r:P:32, w, :, :].bitcast(I32),
+                    scales.bitcast(I32)[:, r:16:4, :].rearrange("a q t -> q a t"),
                 )
 
-        load_scales(nc.gpsimd, 1, w3_scales)
         ident = keep.tile([P, P], F32, name="ident")
         make_identity(nc, ident[:])
         load_w1(0, 0, 2)
-        tab_s_words = tab_s[:].bitcast(I32).rearrange("p (a t) -> p a t", a=PASSES)
         for q in range(4):
             nc.sync.dma_start(
-                tab_s_words[32 * q : 32 * q + 4, :, :],
-                tab_scales.bitcast(I32)[:, 4 * q : 4 * q + 4, :].rearrange("a r t -> r a t"),
+                tab_s[32 * q : 32 * q + 4 * PASSES, :].bitcast(I32),
+                tab_scales.bitcast(I32)[:, 4 * q : 4 * q + 4, :],
             )
         load_w1(1, 0, 2)
         load_table(0)
         load_table(1)
         load_scales(nc.sync, 0, w2_scales)
         load_packed(0, 2)
+        load_scales(nc.sync, 1, w3_scales)
         nc.sync.dma_start(idx2[:], offs2)
         wgs_sb = keep.tile([P, S], F32, name="wgs_sb")
         nc.sync.dma_start(wgs_sb[:], wgs)
@@ -123,25 +122,23 @@ def tile_list_latency_envelopes_kernel(
         nc.sync.dma_start(idx3[:], offs3)
         wo_raw = keep.tile([P, PACK, N], F32, name="wo_raw")
         nc.sync.dma_start(wo_raw[:], wo.rearrange("(p i) n -> p i n", i=PACK))
-        load_raw = [keep.tile([P, PACK, CHUNK], F32, name="load_raw%d" % c) for c in range(M // CHUNK)]
-        load_rows = load.rearrange("(p i) m -> p i m", i=PACK)
-        for c in range(M // CHUNK):
-            nc.sync.dma_start(load_raw[c][:], load_rows[:, :, c * CHUNK : (c + 1) * CHUNK])
+        load_raw = [keep.tile([P, M], F32, name="load_raw%d" % b) for b in range(BLOCKS)]
+        for b in range(BLOCKS):
+            nc.sync.dma_start(load_raw[b][:], load[b * P : (b + 1) * P, :])
 
-        v_w, v_s = {}, {}
+        v_w = {}
 
-        def gather_words(a, j0, j1):
-            words = keep.tile([P, j1 - j0], U32, name="v_w%d_%d" % (a, j0), align_bytes=64)
-            nc.vector.tensor_copy(words[:], tab_w[a][:].bitcast(U32).indirect(idx1[:, j0 // 16 : j1 // 16]))
-            for jt in range(j0, j1, P):
-                v_w[a, jt] = words[:, jt - j0 : jt - j0 + P].bitcast(FP8X4)
+        def gather_words(a, half, j0, j1):
+            nc.vector.tensor_copy(
+                v_w[a, half][:, j0:j1],
+                tab_w[a][:].bitcast(U32).indirect(idx1[:, (half * BANK + j0) // 16 : (half * BANK + j1) // 16]),
+            )
 
-        def gather_scales(j0, j1, tag):
-            held = keep.tile([P, PASSES, j1 - j0], U8, name="v_s", tag=tag, align_bytes=64)
-            for a in range(PASSES):
-                nc.vector.tensor_copy(held[:, a, :], tab_s[:, a * T : (a + 1) * T].indirect(idx1[:, j0 // 16 : j1 // 16]))
-                for jt in range(j0, j1, P):
-                    v_s[a, jt] = held[:, a, jt - j0 : jt - j0 + P]
+        v_s = keep.tile([P, S], U8, name="v_s", align_bytes=64)
+        nc.vector.tensor_copy(v_s[:], tab_s[:].indirect(idx1[:]))
+        nc.gpsimd.dma_start(v_s1[0:112, :].bitcast(I32), v_s[4:116, :].bitcast(I32))
+        packed_planes = [v_s[4 * a : P, :] for a in range(PASSES)]
+        planes_at_zero = [v_s[:], v_s1[:]]
 
         w1_c, w1_s = {}, {}
         w1_bf = [keep.tile([P, PASSES, P, PACK], BF16, name="w1_bf", tag=("page%d" if b >= 2 else "w1_bf%d") % b, align_bytes=64) for b in range(BLOCKS)]
@@ -159,20 +156,21 @@ def tile_list_latency_envelopes_kernel(
                 w1_c[b, a] = codes[:, a * P : (a + 1) * P].bitcast(FP8X4)
                 w1_s[b, a] = scales[:, a * P : (a + 1) * P]
 
-        gather_scales(0, BANK, "v_s")
         quantize_w1(0)
         quantize_w1(1)
-        gather_words(0, 0, S)
-        gather_words(1, 0, FIRST)
-        gather_words(1, FIRST, BANK)
-        gather_words(1, BANK, S)
-        gather_scales(BANK, S, "late1")
+        for a, half in ((0, 0), (1, 0), (1, 1)):
+            v_w[a, half] = keep.tile([P, BANK], U32, name="v_w%d_%d" % (a, half), align_bytes=64)
+        gather_words(0, 0, 0, BANK)
+        gather_words(1, 0, 0, BANK)
+        gather_words(1, 1, 0, BANK)
+        v_w[0, 1] = keep.tile([P, BANK], U32, name="v_w0_1", tag="late1", align_bytes=64)
+        gather_words(0, 1, 0, BANK)
         open_page()
 
         wo_bf = [keep.tile([P, 2 * P, PACK], BF16, name="wo_bf%d" % k, align_bytes=64) for k in range(N // (2 * P))]
         wo_c = keep.tile([P, N], U32, name="wo_c", align_bytes=64)
         wo_s = keep.tile([P, N], U8, name="wo_s", align_bytes=64)
-        load_il = [keep.tile([P, CHUNK, PACK], F32, name="load_il%d" % c) for c in range(M // CHUNK)]
+        load_t = [keep.tile([P, CHUNK // P, H], F32, name="load_t%d" % c) for c in range(M // CHUNK)]
 
         def quantize_wo(k):
             cols = slice(2 * P * k, 2 * P * (k + 1))
@@ -182,28 +180,47 @@ def tile_list_latency_envelopes_kernel(
                 in_=wo_bf[k][:].rearrange("p n i -> p (n i)"),
             )
 
-        def weave_load(c):
-            interleave(nc.scalar.copy, load_il[c][:], load_raw[c][:])
+        def by_words(rows):
+            return rows.rearrange("m (q u e) -> m u q e", u=2, e=2)
+
+        def in_words(rows):
+            return rows.rearrange("m (u q e) -> m u q e", u=2, e=2)
+
+        def turn_load(c, half):
+            bank = psum.tile([P, BANK], F32, name="load_bank", tag="d", bufs=8 - EB)
+            m0 = c * CHUNK + half * P
+            for b in range(BLOCKS):
+                nc.tensor.transpose(bank[:, b * P : (b + 1) * P], load_raw[b][:, m0 : m0 + P], ident[:])
+            nc.scalar.copy(in_words(load_t[c][:, half, :]), by_words(bank[:]))
 
         stage = [keep.tile([P, BLOCKS * CHUNK], F32, name="stage%d" % i) for i in range(2)]
 
-        def product(b, j0, j1, codes, scales):
-            bank = psum.tile([P, BANK], F32, name="e_bank", tag="e", bufs=2)
+        def product(u, planes, codes, scales):
+            b, j0, j1 = units[u]
+            half, o = divmod(j0, BANK)
+            bank = psum.tile([P, BANK], F32, name="e_bank", tag="e", bufs=EB)
             for a in range(PASSES):
-                for jt in range(j0, j1, P):
+                if u == 0:
                     nc.tensor.matmul_mx(
-                        out=bank[:, jt - j0 : jt - j0 + P],
-                        lhsT=v_w[a, jt],
-                        lhsT_scale=v_s[a, jt],
+                        out=bank[:], lhsT=codes[b, a], lhsT_scale=scales[a],
+                        rhs=v_w[a, half][:].bitcast(FP8X4), rhs_scale=planes[a][:, j0:j1],
+                        start=(a == 0), stop=(a == PASSES - 1),
+                    )
+                    continue
+                for k in range(0, j1 - j0, P):
+                    nc.tensor.matmul_mx(
+                        out=bank[:, k : k + P],
+                        lhsT=v_w[a, half][:, o + k : o + k + P].bitcast(FP8X4),
+                        lhsT_scale=planes[a][:, j0 + k : j0 + k + P],
                         rhs=codes[b, a],
                         rhs_scale=scales[a],
-                        start=(a == 0 and jt == j0),
-                        stop=(a == PASSES - 1 and jt == j1 - P),
+                        start=(a == 0 and k == 0),
+                        stop=(a == PASSES - 1 and k == j1 - j0 - P),
                     )
             return bank
 
         def difference(width, plus, minus):
-            bank = psum.tile([P, BANK], F32, name="d_bank", tag="d", bufs=6)
+            bank = psum.tile([P, BANK], F32, name="d_bank", tag="d", bufs=8 - EB)
             for o in range(0, width, P):
                 nc.tensor.matmul(bank[:, o : o + P], plus[:, o : o + P], ident[:],
                                  start=True, stop=False, is_transpose=True)
@@ -216,51 +233,55 @@ def tile_list_latency_envelopes_kernel(
             nc.scalar.activation(held[:, :width], bank[:, :width], ACT.Copy, scale=scale)
             return held
 
-        units = [(0, 0, FIRST), (0, FIRST, BANK), (1, 0, BANK), (0, BANK, S), (1, BANK, S)]
+        units = [(0, 0, BANK), (1, 0, BANK), (0, BANK, S), (1, BANK, S)]
         units = units + [(b, j0, j0 + BANK) for b in range(2, BLOCKS) for j0 in range(0, S, BANK)]
         last = len(units) - 1
         jobs = [(w1_bf[b][:].rearrange("p a c i -> p (a c i)").bitcast(F32), quantize_w1, b) for b in range(2, BLOCKS)]
         jobs = jobs + [(t[:].rearrange("p n i -> p (n i)").bitcast(F32), quantize_wo, k) for k, t in enumerate(wo_bf)]
-        jobs = jobs + [(t[:].rearrange("p n i -> p (n i)"), weave_load, c) for c, t in enumerate(load_il)]
         pos2, neg1, neg3, above = {}, {}, {}, {}
 
         def estimate2(u):
             b, j0, j1 = units[u]
-            bank = product(b, j0, j1, w2_c, [w_s[:, 0, a, b * P : (b + 1) * P] for a in range(PASSES)])
+            bank = product(u, packed_planes, w2_c, [w_s[:, 0, a, b * P : (b + 1) * P] for a in range(PASSES)])
             pos2[u] = copy_out("pos2", bank, j1 - j0, 1.0)
 
         def estimate1(u):
             b, j0, j1 = units[u]
-            bank = product(b, j0, j1, w1_c, [w1_s[b, a] for a in range(PASSES)])
-            neg1[u] = copy_out("neg1", bank, j1 - j0, -1.0, jobs[-2][0] if u == last else None)
+            bank = product(u, packed_planes, w1_c, [w1_s[b, a] for a in range(PASSES)])
+            neg1[u] = copy_out("neg1", bank, j1 - j0, -1.0)
 
         def estimate3(u):
             b, j0, j1 = units[u]
-            bank = product(b, j0, j1, w3_c, [w_s[:, 1, a, b * P : (b + 1) * P] for a in range(PASSES)])
-            neg3[u] = copy_out("neg3", bank, j1 - j0, -1.0, jobs[-1][0] if u == last else None)
+            bank = product(u, planes_at_zero, w3_c, [w_s[:, 1, a, b * P : (b + 1) * P] for a in range(PASSES)])
+            neg3[u] = copy_out("neg3", bank, j1 - j0, -1.0)
 
         def upper(u):
             b, j0, j1 = units[u]
             width = j1 - j0
             bank = difference(width, pos2[u], neg1[u])
-            above[u] = jobs[u - 2][0] if u >= 2 else ring.tile([P, BANK], F32, name="above")
+            above[u] = jobs[u - 1][0] if u <= len(jobs) else ring.tile([P, BANK], F32, name="above")
             nc.scalar.activation(above[u][:, :width], bank[:, :width], ACT.Relu, scale=-1.0)
 
         def lower_and_put(u):
             b, j0, j1 = units[u]
             width = j1 - j0
             bank = difference(width, pos2[u], neg3[u])
-            h = stage[u % 2][:, :width]
+            h = stage[(u - last - 1) % 2][:, :width]
             nc.vector.scalar_tensor_tensor(h, bank[:, :width], 0.0, above[u][:, :width], ALU.max, ALU.add)
             nc.vector.tensor_tensor(pages[b][:].indirect(idx2[:, j0 // 16 : j1 // 16]), h, wgs_sb[:, j0:j1], ALU.mult)
-            if u >= 2:
-                jobs[u - 2][1](jobs[u - 2][2])
+            if u <= len(jobs):
+                jobs[u - 1][1](jobs[u - 1][2])
 
         estimate2(0)
-        estimate1(0)
-        estimate3(0)
-        upper(0)
-        lower_and_put(0)
+        e1 = product(0, packed_planes, w1_c, [w1_s[0, a] for a in range(PASSES)])
+        high = ring.tile([P, BANK], F32, name="neg1", bufs=3)
+        nc.vector.tensor_tensor(high[:], e1[:], pos2[0][:], ALU.max)
+        e3 = product(0, planes_at_zero, w3_c, [w_s[:, 1, a, 0:P] for a in range(PASSES)])
+        low = ring.tile([P, BANK], F32, name="neg3", bufs=3)
+        nc.vector.tensor_tensor(low[:], e3[:], pos2[0][:], ALU.min)
+        h = stage[(0 - last - 1) % 2][:, :BANK]
+        nc.vector.tensor_tensor(h, high[:], low[:], ALU.subtract)
+        nc.vector.tensor_tensor(pages[0][:].indirect(idx2[:, 0 : BANK // 16]), h, wgs_sb[:, 0:BANK], ALU.mult)
         estimate2(1)
         estimate1(1)
         estimate3(1)
@@ -270,16 +291,17 @@ def tile_list_latency_envelopes_kernel(
             estimate1(u + 1)
             lower_and_put(u)
             estimate3(u + 1)
-            if u in (2, 3):
+            if u in (1, 2):
                 open_page()
         upper(last)
         lower_and_put(last)
-        weave_load(2)
-        weave_load(3)
+        for c in range(M // CHUNK):
+            for half in range(CHUNK // P):
+                turn_load(c, half)
 
         out_rows = out.rearrange("(i p) m -> p i m", p=P)
         chunks = M // CHUNK
-        picked = [t[:] for t in reversed(stage)] + [t[:].rearrange("p m i -> p (m i)") for t in load_il[: chunks - 2]]
+        picked = [t[:] for t in stage] + [t[:].rearrange("p h r -> p (h r)") for t in load_t[0:chunks:2]]
         damp = {}
 
         def fetch(c, b):
@@ -290,59 +312,66 @@ def tile_list_latency_envelopes_kernel(
 
         def damping(c):
             for half in range(CHUNK // P):
-                x_t = psum.tile([P, BANK], F32, name="x_t", tag="e", bufs=2)
+                x_t = psum.tile([P, BANK], F32, name="x_t", tag="e", bufs=EB)
                 for b in range(BLOCKS):
                     o = b * CHUNK + half * P
                     nc.tensor.transpose(x_t[:, b * P : (b + 1) * P], picked[c][:, o : o + P], ident[:])
-                ex_t = ring.tile([P, PACK, P], F32, name="ex_t")
-                nc.scalar.activation(ex_t[:], x_t[:].rearrange("m (q i) -> m i q", i=PACK), ACT.Exp, scale=-1.0)
-                ex = psum.tile([P, PACK, P], F32, name="ex", tag="d", bufs=6)
-                for i in range(PACK):
-                    nc.tensor.transpose(ex[:, i, :], ex_t[:, i, :], ident[:])
-                damp[c, half] = ex
+                ex_t = ring.tile([P, H], F32, name="ex_t", bufs=4)
+                nc.scalar.activation(in_words(ex_t[:]), by_words(x_t[:]), ACT.Exp, scale=-1.0)
+                damp[c, half] = ex_t
 
         def signal(c):
-            z = ring.tile([P, CHUNK, PACK], BF16, name="z", align_bytes=64)
-            for half in range(CHUNK // P):
-                cols = slice(half * P, (half + 1) * P)
-                nc.vector.tensor_tensor(
-                    z[:, cols, :], damp[c, half][:].rearrange("q i m -> q m i"), load_il[c][:, cols, :], ALU.mult
-                )
-            return z
+            parts = [(0, 1), (1, 2)] if c == 3 else [(0, 2)]
+            made = []
+            for h0, h1 in parts:
+                bank = psum.tile([P, h1 - h0, 2, P], F32, name="z_bank", tag="d", bufs=8 - EB)
+                for half in range(h0, h1):
+                    z_t = ring.tile([P, H], BF16, name="z_t", bufs=4)
+                    nc.vector.tensor_tensor(z_t[:], damp[c, half][:], load_t[c][:, half, :], ALU.mult)
+                    for u in range(2):
+                        nc.tensor.transpose(bank[:, half - h0, u, :], z_t[:].bitcast(F32)[:, u * P : (u + 1) * P], ident[:])
+                made.append((c * CHUNK + h0 * P, (h1 - h0) * P, bank))
+            return made
 
-        def quantize_z(z):
-            z_c = ring.tile([P, CHUNK], U32, name="z_c", align_bytes=64)
-            z_s = ring.tile([P, CHUNK], U8, name="z_s", align_bytes=64)
+        def project(c, m0, width, bank):
+            z = ring.tile([P, width, PACK], BF16, name="z", align_bytes=64)
+            (nc.vector.tensor_copy if c >= 2 else nc.scalar.copy)(
+                z[:].bitcast(F32).rearrange("q (h m) u -> q h m u", m=P), bank[:].rearrange("q h u m -> q h m u")
+            )
+            z_c = ring.tile([P, width], U32, name="z_c", align_bytes=64)
+            z_s = ring.tile([P, width], U8, name="z_s", align_bytes=64)
             nc.vector.quantize_mx(out=z_c[:].bitcast(FP8X4), scales=z_s[:], in_=z[:].rearrange("p m i -> p (m i)"))
-            return z_c, z_s
-
-        def project(c, z_c, z_s):
-            for pair in range(N // (2 * P)):
-                acc = psum.tile([P, 2, CHUNK], F32, name="acc", tag="d", bufs=6)
-                for k in range(2):
-                    n0 = (2 * pair + k) * P
+            group = 2 if width == CHUNK else 3
+            for pair in range(N // (group * P)):
+                acc = psum.tile([P, group, width], F32, name="acc", tag="d", bufs=8 - EB)
+                for k in range(group):
+                    n0 = (group * pair + k) * P
                     nc.tensor.matmul_mx(
                         out=acc[:, k, :], lhsT=wo_c[:, n0 : n0 + P].bitcast(FP8X4), lhsT_scale=wo_s[:, n0 : n0 + P],
                         rhs=z_c[:].bitcast(FP8X4), rhs_scale=z_s[:], start=True, stop=True,
                     )
-                res = ring.tile([P, 2, CHUNK], F32, name="res", bufs=12)
-                if c == chunks - 1 and pair == 1:
-                    nc.vector.tensor_copy(res[:], acc[:])
-                else:
-                    nc.scalar.copy(res[:], acc[:])
-                nc.sync.dma_start(out_rows[:, 2 * pair : 2 * pair + 2, c * CHUNK : (c + 1) * CHUNK], res[:])
+                res = ring.tile([P, group, width], F32, name="res", bufs=12)
+                (nc.vector.tensor_copy if c == 3 and pair == 1 else nc.scalar.copy)(res[:], acc[:])
+                nc.sync.dma_start(out_rows[:, group * pair : group * pair + group, m0 : m0 + width], res[:])
 
-        for c in range(2):
+        def gather_chunk(c):
             for b in range(BLOCKS):
                 fetch(c, b)
             damping(c)
-        for c in range(chunks):
-            z = signal(c)
-            if c + 2 < chunks:
-                fetch(c + 2, 0)
-            z_c, z_s = quantize_z(z)
-            if c + 2 < chunks:
-                for b in range(1, BLOCKS):
-                    fetch(c + 2, b)
-                damping(c + 2)
-            project(c, z_c, z_s)
+
+        gather_chunk(0)
+        gather_chunk(1)
+        z = signal(0)
+        gather_chunk(2)
+        for part in z:
+            project(0, *part)
+        z = signal(1)
+        for part in z:
+            project(1, *part)
+        z = signal(2)
+        gather_chunk(3)
+        for part in z:
+            project(2, *part)
+        z = signal(3)
+        for part in z:
+            project(3, *part)

@@ -19,16 +19,32 @@ ACT = mybir.ActivationFunctionType
 
 P = 128
 PACK = 4
+STRIPE = 16
+PLANE_ROWS = 4
 PASSES = K // (P * PACK)
-BLOCKS = H // P
+PASS_BLOCKS = P * PACK // 32
+PAGES = H // P
 BANK = 512
-FIRST = 256
+EARLY_PAGES = 2
 CHUNK = 256
-EB = 2
+CHUNKS = M // CHUNK
+WO_PIECE = 256
+SHORT_BANKS = 2
+LONG_BANKS = 6
+UNIT_BUFS = 3
+RESULT_BUFS = 12
 
 
-def interleave(engine_copy, dst, src):
-    engine_copy(out=dst, in_=src.rearrange("p i c -> p c i"))
+def interleave(nc, dst, src):
+    nc.scalar.copy(out=dst, in_=src.rearrange("p i c -> p c i"))
+
+
+def in_pair_order(natural):
+    return natural.rearrange("m (q u e) -> m u q e", u=2, e=2)
+
+
+def as_pairs(ordered):
+    return ordered.rearrange("m (u q e) -> m u q e", u=2, e=2)
 
 
 def tile_list_latency_envelopes_kernel(
@@ -39,11 +55,23 @@ def tile_list_latency_envelopes_kernel(
     with ExitStack() as ctx:
         keep = ctx.enter_context(tc.tile_pool(name="keep", bufs=1))
         ring = ctx.enter_context(tc.tile_pool(name="ring", bufs=2))
-        psum = ctx.enter_context(tc.psum_pool(name="psum", bufs=4))
+        psum = ctx.enter_context(tc.psum_pool(name="psum", bufs=1))
 
-        idx1 = keep.tile([P, S // 16], U16, name="idx1")
-        idx2 = keep.tile([P, S // 16], U16, name="idx2")
-        idx3 = keep.tile([P, M // 16], U16, name="idx3")
+        def short_bank(shape):
+            return psum.tile(shape, F32, name="short_bank", bufs=SHORT_BANKS)
+
+        def long_bank(shape):
+            return psum.tile(shape, F32, name="long_bank", bufs=LONG_BANKS)
+
+        def unit_tile(name):
+            return ring.tile([P, BANK], F32, name=name, bufs=UNIT_BUFS)
+
+        idx1 = keep.tile([P, S // STRIPE], U16, name="idx1")
+        idx2 = keep.tile([P, S // STRIPE], U16, name="idx2")
+        idx3 = keep.tile([P, M // STRIPE], U16, name="idx3")
+
+        def entries(idx, j0, j1):
+            return idx[:, j0 // STRIPE : j1 // STRIPE]
 
         tab_s = keep.tile([P, T], U8, name="tab_s", align_bytes=64)
         v_s1 = keep.tile([P, S], U8, name="v_s1", align_bytes=64)
@@ -59,16 +87,13 @@ def tile_list_latency_envelopes_kernel(
             nc.gpsimd.memset(page[:].bitcast(I32), 0)
             pages.append(page)
 
-        warm = keep.tile([P, 2], F32, name="warm")
-        nc.vector.memset(warm[:, 0:1], 0.0)
-
-        nc.sync.dma_start(idx1[:], offs)
-        tab_w = [keep.tile([P, T], I32, name="tab_w%d" % a, tag=("page1", "late1")[a], align_bytes=64) for a in range(PASSES)]
-        nc.scalar.activation(warm[:, 1:2], warm[:, 0:1], ACT.Exp)
-
+        tab_w = [
+            keep.tile([P, T], I32, name="tab_w0", tag="page1", align_bytes=64),
+            keep.tile([P, T], I32, name="tab_w1", tag="tab_w1", align_bytes=64),
+        ]
         w1_rows = w1.rearrange("(a p i) c -> a p i c", a=PASSES, i=PACK)
-        w2_hbm = w2_words.rearrange("a p c i -> p a (c i)")
-        w3_hbm = w3_words.rearrange("a p c -> p a c")
+        w2_rows = w2_words.rearrange("a p c i -> p a (c i)")
+        w3_rows = w3_words.rearrange("a p c -> p a c")
         w1_raw, w2_c, w3_c = {}, {}, {}
 
         def load_w1(a, b0, b1):
@@ -77,301 +102,301 @@ def tile_list_latency_envelopes_kernel(
             for b in range(b0, b1):
                 w1_raw[b, a] = raw[:, :, (b - b0) * P : (b - b0 + 1) * P]
 
-        def load_table(a):
-            nc.sync.dma_start(tab_w[a][:], tab_words[a].rearrange("p t i -> p (t i)").bitcast(I32))
-
         def load_packed(b0, b1):
             width = (b1 - b0) * P
-            c2 = keep.tile([P, PASSES, width], U32, name="w2_c%d" % b0, align_bytes=64)
-            nc.sync.dma_start(c2[:].bitcast(I32), w2_hbm[:, :, 4 * b0 * P : 4 * b1 * P].bitcast(I32))
-            c3 = keep.tile([P, PASSES, 2 * width], U8, name="w3_c%d" % b0, align_bytes=64)
-            nc.sync.dma_start(c3[:].bitcast(I32), w3_hbm[:, :, 2 * b0 * P : 2 * b1 * P].bitcast(I32))
+            words2 = keep.tile([P, PASSES, width], U32, name="w2_c%d" % b0, align_bytes=64)
+            nc.sync.dma_start(words2[:].bitcast(I32), w2_rows[:, :, 4 * b0 * P : 4 * b1 * P].bitcast(I32))
+            words3 = keep.tile([P, PASSES, 2 * width], U8, name="w3_c%d" % b0, align_bytes=64)
+            nc.sync.dma_start(words3[:].bitcast(I32), w3_rows[:, :, 2 * b0 * P : 2 * b1 * P].bitcast(I32))
             for b in range(b0, b1):
-                o = (b - b0) * P
+                c0 = (b - b0) * P
                 for a in range(PASSES):
-                    w2_c[b, a] = c2[:, a, o : o + P].bitcast(FP8X4)
-                    w3_c[b, a] = c3[:, a, 2 * o : 2 * (o + P)].bitcast(FP4X4)
+                    w2_c[b, a] = words2[:, a, c0 : c0 + P].bitcast(FP8X4)
+                    w3_c[b, a] = words3[:, a, 2 * c0 : 2 * (c0 + P)].bitcast(FP4X4)
 
-        def load_scales(queue, w, scales):
-            for r in range(4):
-                queue.dma_start(
-                    w_s[r:P:32, w, :, :].bitcast(I32),
-                    scales.bitcast(I32)[:, r:16:4, :].rearrange("a q t -> q a t"),
+        def load_weight_scales(w, scales):
+            for row in range(PLANE_ROWS):
+                nc.sync.dma_start(
+                    w_s[row:P:32, w, :, :].bitcast(I32),
+                    scales.bitcast(I32)[:, row:PASS_BLOCKS:PLANE_ROWS, :].rearrange("a q c -> q a c"),
                 )
 
+        nc.sync.dma_start(idx1[:], offs)
         ident = keep.tile([P, P], F32, name="ident")
         make_identity(nc, ident[:])
-        load_w1(0, 0, 2)
-        for q in range(4):
+        load_w1(0, 0, EARLY_PAGES)
+        for q in range(P // 32):
             nc.sync.dma_start(
-                tab_s[32 * q : 32 * q + 4 * PASSES, :].bitcast(I32),
-                tab_scales.bitcast(I32)[:, 4 * q : 4 * q + 4, :],
+                tab_s[32 * q : 32 * q + PASSES * PLANE_ROWS, :].bitcast(I32),
+                tab_scales.bitcast(I32)[:, PLANE_ROWS * q : PLANE_ROWS * (q + 1), :],
             )
-        load_w1(1, 0, 2)
-        load_table(0)
-        load_table(1)
-        load_scales(nc.sync, 0, w2_scales)
-        load_packed(0, 2)
-        load_scales(nc.sync, 1, w3_scales)
+        load_w1(1, 0, EARLY_PAGES)
+        for a in range(PASSES):
+            nc.sync.dma_start(tab_w[a][:], tab_words[a].rearrange("p t i -> p (t i)").bitcast(I32))
+        load_weight_scales(0, w2_scales)
+        load_packed(0, EARLY_PAGES)
+        load_weight_scales(1, w3_scales)
         nc.sync.dma_start(idx2[:], offs2)
         wgs_sb = keep.tile([P, S], F32, name="wgs_sb")
         nc.sync.dma_start(wgs_sb[:], wgs)
-        load_w1(0, 2, BLOCKS)
-        load_w1(1, 2, BLOCKS)
-        load_packed(2, BLOCKS)
+        for a in range(PASSES):
+            load_w1(a, EARLY_PAGES, PAGES)
+        load_packed(EARLY_PAGES, PAGES)
         nc.sync.dma_start(idx3[:], offs3)
         wo_raw = keep.tile([P, PACK, N], F32, name="wo_raw")
         nc.sync.dma_start(wo_raw[:], wo.rearrange("(p i) n -> p i n", i=PACK))
-        load_raw = [keep.tile([P, M], F32, name="load_raw%d" % b) for b in range(BLOCKS)]
-        for b in range(BLOCKS):
+        load_raw = [keep.tile([P, M], F32, name="load_raw%d" % b) for b in range(PAGES)]
+        for b in range(PAGES):
             nc.sync.dma_start(load_raw[b][:], load[b * P : (b + 1) * P, :])
-
-        v_w = {}
-
-        def gather_words(a, half, j0, j1):
-            nc.vector.tensor_copy(
-                v_w[a, half][:, j0:j1],
-                tab_w[a][:].bitcast(U32).indirect(idx1[:, (half * BANK + j0) // 16 : (half * BANK + j1) // 16]),
-            )
 
         v_s = keep.tile([P, S], U8, name="v_s", align_bytes=64)
         nc.vector.tensor_copy(v_s[:], tab_s[:].indirect(idx1[:]))
-        nc.gpsimd.dma_start(v_s1[0:112, :].bitcast(I32), v_s[4:116, :].bitcast(I32))
-        packed_planes = [v_s[4 * a : P, :] for a in range(PASSES)]
+        plane_span = P - 32 + PLANE_ROWS
+        nc.gpsimd.dma_start(
+            v_s1[0:plane_span, :].bitcast(I32), v_s[PLANE_ROWS : PLANE_ROWS + plane_span, :].bitcast(I32)
+        )
+        planes_packed = [v_s[PLANE_ROWS * a : P, :] for a in range(PASSES)]
         planes_at_zero = [v_s[:], v_s1[:]]
 
+        v_w = {}
+
+        def gather_words(a, half, tag):
+            v_w[a, half] = keep.tile([P, BANK], U32, name="v_w", tag=tag, align_bytes=64)
+            nc.vector.tensor_copy(
+                v_w[a, half][:], tab_w[a][:].bitcast(U32).indirect(entries(idx1, half * BANK, (half + 1) * BANK))
+            )
+
         w1_c, w1_s = {}, {}
-        w1_bf = [keep.tile([P, PASSES, P, PACK], BF16, name="w1_bf", tag=("page%d" if b >= 2 else "w1_bf%d") % b, align_bytes=64) for b in range(BLOCKS)]
+        w1_bf = [
+            keep.tile([P, PASSES, P, PACK], BF16, name="w1_bf", align_bytes=64,
+                      tag=("w1_bf%d" if b < EARLY_PAGES else "page%d") % b)
+            for b in range(PAGES)
+        ]
 
         def quantize_w1(b):
             for a in range(PASSES):
-                interleave(nc.scalar.copy, w1_bf[b][:, a, :, :], w1_raw[b, a])
+                interleave(nc, w1_bf[b][:, a, :, :], w1_raw[b, a])
             codes = keep.tile([P, PASSES * P], U32, name="w1_c%d" % b, align_bytes=64)
             scales = keep.tile([P, PASSES * P], U8, name="w1_s%d" % b, align_bytes=64)
             nc.vector.quantize_mx(
-                out=codes[:].bitcast(FP8X4), scales=scales[:],
-                in_=w1_bf[b][:].rearrange("p a c i -> p (a c i)"),
+                out=codes[:].bitcast(FP8X4), scales=scales[:], in_=w1_bf[b][:].rearrange("p a c i -> p (a c i)")
             )
             for a in range(PASSES):
                 w1_c[b, a] = codes[:, a * P : (a + 1) * P].bitcast(FP8X4)
                 w1_s[b, a] = scales[:, a * P : (a + 1) * P]
 
-        quantize_w1(0)
-        quantize_w1(1)
-        for a, half in ((0, 0), (1, 0), (1, 1)):
-            v_w[a, half] = keep.tile([P, BANK], U32, name="v_w%d_%d" % (a, half), align_bytes=64)
-        gather_words(0, 0, 0, BANK)
-        gather_words(1, 0, 0, BANK)
-        gather_words(1, 1, 0, BANK)
-        v_w[0, 1] = keep.tile([P, BANK], U32, name="v_w0_1", tag="late1", align_bytes=64)
-        gather_words(0, 1, 0, BANK)
+        for b in range(EARLY_PAGES):
+            quantize_w1(b)
+        gather_words(0, 0, "v_w00")
+        gather_words(1, 0, "v_w10")
+        gather_words(1, 1, "v_w11")
+        gather_words(0, 1, "tab_w1")
         open_page()
 
-        wo_bf = [keep.tile([P, 2 * P, PACK], BF16, name="wo_bf%d" % k, align_bytes=64) for k in range(N // (2 * P))]
+        wo_bf = [keep.tile([P, WO_PIECE, PACK], BF16, name="wo_bf%d" % k, align_bytes=64) for k in range(N // WO_PIECE)]
         wo_c = keep.tile([P, N], U32, name="wo_c", align_bytes=64)
         wo_s = keep.tile([P, N], U8, name="wo_s", align_bytes=64)
-        load_t = [keep.tile([P, CHUNK // P, H], F32, name="load_t%d" % c) for c in range(M // CHUNK)]
 
         def quantize_wo(k):
-            cols = slice(2 * P * k, 2 * P * (k + 1))
-            interleave(nc.scalar.copy, wo_bf[k][:], wo_raw[:, :, cols])
+            cols = slice(WO_PIECE * k, WO_PIECE * (k + 1))
+            interleave(nc, wo_bf[k][:], wo_raw[:, :, cols])
             nc.vector.quantize_mx(
-                out=wo_c[:, cols].bitcast(FP8X4), scales=wo_s[:, cols],
-                in_=wo_bf[k][:].rearrange("p n i -> p (n i)"),
+                out=wo_c[:, cols].bitcast(FP8X4), scales=wo_s[:, cols], in_=wo_bf[k][:].rearrange("p n i -> p (n i)")
             )
 
-        def by_words(rows):
-            return rows.rearrange("m (q u e) -> m u q e", u=2, e=2)
+        units = [(b, half) for half in range(2) for b in range(EARLY_PAGES)]
+        units = units + [(b, half) for b in range(EARLY_PAGES, PAGES) for half in range(2)]
+        last = len(units) - 1
 
-        def in_words(rows):
-            return rows.rearrange("m (u q e) -> m u q e", u=2, e=2)
+        def turned_twice(u):
+            return units[u][0] == PAGES - 1
 
-        def turn_load(c, half):
-            bank = psum.tile([P, BANK], F32, name="load_bank", tag="d", bufs=8 - EB)
-            m0 = c * CHUNK + half * P
-            for b in range(BLOCKS):
-                nc.tensor.transpose(bank[:, b * P : (b + 1) * P], load_raw[b][:, m0 : m0 + P], ident[:])
-            nc.scalar.copy(in_words(load_t[c][:, half, :]), by_words(bank[:]))
-
-        stage = [keep.tile([P, BLOCKS * CHUNK], F32, name="stage%d" % i) for i in range(2)]
-
-        def product(u, planes, codes, scales):
-            b, j0, j1 = units[u]
-            half, o = divmod(j0, BANK)
-            bank = psum.tile([P, BANK], F32, name="e_bank", tag="e", bufs=EB)
+        def estimate(u, bank, planes, codes, scales):
+            b, half = units[u]
+            j0 = half * BANK
             for a in range(PASSES):
-                if u == 0:
+                if u == 0 or turned_twice(u):
                     nc.tensor.matmul_mx(
                         out=bank[:], lhsT=codes[b, a], lhsT_scale=scales[a],
-                        rhs=v_w[a, half][:].bitcast(FP8X4), rhs_scale=planes[a][:, j0:j1],
+                        rhs=v_w[a, half][:].bitcast(FP8X4), rhs_scale=planes[a][:, j0 : j0 + BANK],
                         start=(a == 0), stop=(a == PASSES - 1),
                     )
-                    continue
-                for k in range(0, j1 - j0, P):
-                    nc.tensor.matmul_mx(
-                        out=bank[:, k : k + P],
-                        lhsT=v_w[a, half][:, o + k : o + k + P].bitcast(FP8X4),
-                        lhsT_scale=planes[a][:, j0 + k : j0 + k + P],
-                        rhs=codes[b, a],
-                        rhs_scale=scales[a],
-                        start=(a == 0 and k == 0),
-                        stop=(a == PASSES - 1 and k == j1 - j0 - P),
-                    )
+                else:
+                    for c0 in range(0, BANK, P):
+                        nc.tensor.matmul_mx(
+                            out=bank[:, c0 : c0 + P],
+                            lhsT=v_w[a, half][:, c0 : c0 + P].bitcast(FP8X4),
+                            lhsT_scale=planes[a][:, j0 + c0 : j0 + c0 + P],
+                            rhs=codes[b, a], rhs_scale=scales[a],
+                            start=(a == 0 and c0 == 0), stop=(a == PASSES - 1 and c0 == BANK - P),
+                        )
             return bank
 
-        def difference(width, plus, minus):
-            bank = psum.tile([P, BANK], F32, name="d_bank", tag="d", bufs=8 - EB)
-            for o in range(0, width, P):
-                nc.tensor.matmul(bank[:, o : o + P], plus[:, o : o + P], ident[:],
+        def e1(u, bank):
+            return estimate(u, bank, planes_packed, w1_c, [w1_s[units[u][0], a] for a in range(PASSES)])
+
+        def e2(u, bank):
+            c0 = units[u][0] * P
+            return estimate(u, bank, planes_packed, w2_c, [w_s[:, 0, a, c0 : c0 + P] for a in range(PASSES)])
+
+        def e3(u, bank):
+            c0 = units[u][0] * P
+            return estimate(u, bank, planes_at_zero, w3_c, [w_s[:, 1, a, c0 : c0 + P] for a in range(PASSES)])
+
+        def turned_sum(first, second):
+            bank = long_bank([P, BANK])
+            for c0 in range(0, BANK, P):
+                nc.tensor.matmul(bank[:, c0 : c0 + P], first[:, c0 : c0 + P], ident[:],
                                  start=True, stop=False, is_transpose=True)
-                nc.tensor.matmul(bank[:, o : o + P], minus[:, o : o + P], ident[:],
+                nc.tensor.matmul(bank[:, c0 : c0 + P], second[:, c0 : c0 + P], ident[:],
                                  start=False, stop=True, is_transpose=True)
             return bank
 
-        def copy_out(name, bank, width, scale, into=None):
-            held = ring.tile([P, BANK], F32, name=name, bufs=3) if into is None else into
-            nc.scalar.activation(held[:, :width], bank[:, :width], ACT.Copy, scale=scale)
-            return held
+        def put(u, h):
+            b, half = units[u]
+            j0 = half * BANK
+            nc.vector.tensor_tensor(
+                pages[b][:].indirect(entries(idx2, j0, j0 + BANK)), h, wgs_sb[:, j0 : j0 + BANK], ALU.mult
+            )
 
-        units = [(0, 0, BANK), (1, 0, BANK), (0, BANK, S), (1, BANK, S)]
-        units = units + [(b, j0, j0 + BANK) for b in range(2, BLOCKS) for j0 in range(0, S, BANK)]
-        last = len(units) - 1
-        jobs = [(w1_bf[b][:].rearrange("p a c i -> p (a c i)").bitcast(F32), quantize_w1, b) for b in range(2, BLOCKS)]
-        jobs = jobs + [(t[:].rearrange("p n i -> p (n i)").bitcast(F32), quantize_wo, k) for k, t in enumerate(wo_bf)]
+        pieces = [
+            (w1_bf[b][:].rearrange("p a c i -> p (a c i)").bitcast(F32), quantize_w1, b)
+            for b in range(EARLY_PAGES, PAGES)
+        ]
+        pieces = pieces + [
+            (tile[:].rearrange("p n i -> p (n i)").bitcast(F32), quantize_wo, k) for k, tile in enumerate(wo_bf)
+        ]
+        first_x = [keep.tile([P, PAGES * CHUNK], F32, name="first_x%d" % c) for c in range(2)]
         pos2, neg1, neg3, above = {}, {}, {}, {}
 
-        def estimate2(u):
-            b, j0, j1 = units[u]
-            bank = product(u, packed_planes, w2_c, [w_s[:, 0, a, b * P : (b + 1) * P] for a in range(PASSES)])
-            pos2[u] = copy_out("pos2", bank, j1 - j0, 1.0)
+        def copy_e2(u):
+            bank = e2(u, short_bank([P, BANK]))
+            pos2[u] = unit_tile("pos2")
+            nc.scalar.activation(pos2[u][:], bank[:], ACT.Copy, scale=1.0)
 
-        def estimate1(u):
-            b, j0, j1 = units[u]
-            bank = product(u, packed_planes, w1_c, [w1_s[b, a] for a in range(PASSES)])
-            neg1[u] = copy_out("neg1", bank, j1 - j0, -1.0)
+        def negate_e1(u):
+            bank = e1(u, short_bank([P, BANK]))
+            neg1[u] = unit_tile("neg1")
+            nc.scalar.activation(neg1[u][:], bank[:], ACT.Copy, scale=-1.0)
 
-        def estimate3(u):
-            b, j0, j1 = units[u]
-            bank = product(u, planes_at_zero, w3_c, [w_s[:, 1, a, b * P : (b + 1) * P] for a in range(PASSES)])
-            neg3[u] = copy_out("neg3", bank, j1 - j0, -1.0)
+        def negate_e3(u):
+            bank = e3(u, short_bank([P, BANK]))
+            neg3[u] = pieces[u - 1][0] if u <= len(pieces) else unit_tile("neg3")
+            nc.scalar.activation(neg3[u][:], bank[:], ACT.Copy, scale=-1.0)
 
-        def upper(u):
-            b, j0, j1 = units[u]
-            width = j1 - j0
-            bank = difference(width, pos2[u], neg1[u])
-            above[u] = jobs[u - 1][0] if u <= len(jobs) else ring.tile([P, BANK], F32, name="above")
-            nc.scalar.activation(above[u][:, :width], bank[:, :width], ACT.Relu, scale=-1.0)
+        def upper_part(u):
+            bank = turned_sum(pos2[u], neg1[u])
+            above[u] = unit_tile("above")
+            nc.scalar.activation(above[u][:], bank[:], ACT.Relu, scale=-1.0)
 
-        def lower_and_put(u):
-            b, j0, j1 = units[u]
-            width = j1 - j0
-            bank = difference(width, pos2[u], neg3[u])
-            h = stage[(u - last - 1) % 2][:, :width]
-            nc.vector.scalar_tensor_tensor(h, bank[:, :width], 0.0, above[u][:, :width], ALU.max, ALU.add)
-            nc.vector.tensor_tensor(pages[b][:].indirect(idx2[:, j0 // 16 : j1 // 16]), h, wgs_sb[:, j0:j1], ALU.mult)
-            if u <= len(jobs):
-                jobs[u - 1][1](jobs[u - 1][2])
+        def lower_part_and_put(u):
+            bank = turned_sum(pos2[u], neg3[u])
+            h = first_x[u - last + 1][:, :BANK] if u >= last - 1 else unit_tile("h")[:]
+            if turned_twice(u):
+                below = ring.tile([P, BANK], F32, name="below")
+                nc.scalar.activation(below[:], bank[:], ACT.Relu)
+                nc.scalar.copy(h, turned_sum(above[u], below)[:])
+            else:
+                nc.vector.scalar_tensor_tensor(h, bank[:], 0.0, above[u][:], ALU.max, ALU.add)
+            put(u, h)
+            if u <= len(pieces):
+                pieces[u - 1][1](pieces[u - 1][2])
 
-        estimate2(0)
-        e1 = product(0, packed_planes, w1_c, [w1_s[0, a] for a in range(PASSES)])
-        high = ring.tile([P, BANK], F32, name="neg1", bufs=3)
-        nc.vector.tensor_tensor(high[:], e1[:], pos2[0][:], ALU.max)
-        e3 = product(0, planes_at_zero, w3_c, [w_s[:, 1, a, 0:P] for a in range(PASSES)])
-        low = ring.tile([P, BANK], F32, name="neg3", bufs=3)
-        nc.vector.tensor_tensor(low[:], e3[:], pos2[0][:], ALU.min)
-        h = stage[(0 - last - 1) % 2][:, :BANK]
-        nc.vector.tensor_tensor(h, high[:], low[:], ALU.subtract)
-        nc.vector.tensor_tensor(pages[0][:].indirect(idx2[:, 0 : BANK // 16]), h, wgs_sb[:, 0:BANK], ALU.mult)
-        estimate2(1)
-        estimate1(1)
-        estimate3(1)
+        copy_e2(0)
+        high_bank = e1(0, long_bank([P, BANK]))
+        high = unit_tile("neg1")
+        nc.vector.tensor_tensor(high[:], high_bank[:], pos2[0][:], ALU.max)
+        low_bank = e3(0, long_bank([P, BANK]))
+        low = unit_tile("neg3")
+        nc.vector.tensor_tensor(low[:], low_bank[:], pos2[0][:], ALU.min)
+        spread = unit_tile("h")
+        nc.vector.tensor_tensor(spread[:], high[:], low[:], ALU.subtract)
+        put(0, spread[:])
+
+        copy_e2(1)
+        negate_e1(1)
+        negate_e3(1)
         for u in range(1, last):
-            estimate2(u + 1)
-            upper(u)
-            estimate1(u + 1)
-            lower_and_put(u)
-            estimate3(u + 1)
-            if u in (1, 2):
+            copy_e2(u + 1)
+            upper_part(u)
+            negate_e1(u + 1)
+            lower_part_and_put(u)
+            negate_e3(u + 1)
+            if len(pages) < PAGES:
                 open_page()
-        upper(last)
-        lower_and_put(last)
-        for c in range(M // CHUNK):
-            for half in range(CHUNK // P):
-                turn_load(c, half)
+        upper_part(last)
+        lower_part_and_put(last)
 
+        load_t = [keep.tile([P, CHUNK // P, H], F32, name="load_t%d" % c) for c in range(CHUNKS)]
+        for c in range(CHUNKS):
+            for part in range(CHUNK // P):
+                bank = long_bank([P, H])
+                m0 = c * CHUNK + part * P
+                for b in range(PAGES):
+                    nc.tensor.transpose(bank[:, b * P : (b + 1) * P], load_raw[b][:, m0 : m0 + P], ident[:])
+                nc.scalar.copy(as_pairs(load_t[c][:, part, :]), in_pair_order(bank[:]))
+
+        x_tiles = [tile[:] for tile in first_x] + [tile[:].rearrange("m a r -> m (a r)") for tile in load_t[0::2]]
         out_rows = out.rearrange("(i p) m -> p i m", p=P)
-        chunks = M // CHUNK
-        picked = [t[:] for t in stage] + [t[:].rearrange("p h r -> p (h r)") for t in load_t[0:chunks:2]]
-        damp = {}
+        damping = {}
 
-        def fetch(c, b):
-            nc.vector.tensor_copy(
-                picked[c][:, b * CHUNK : (b + 1) * CHUNK],
-                pages[b][:].indirect(idx3[:, c * CHUNK // 16 : (c + 1) * CHUNK // 16]),
-            )
+        def fetch(c):
+            for b in range(PAGES):
+                nc.vector.tensor_copy(
+                    x_tiles[c][:, b * CHUNK : (b + 1) * CHUNK],
+                    pages[b][:].indirect(entries(idx3, c * CHUNK, (c + 1) * CHUNK)),
+                )
+            for part in range(CHUNK // P):
+                bank = short_bank([P, H])
+                for b in range(PAGES):
+                    c0 = b * CHUNK + part * P
+                    nc.tensor.transpose(bank[:, b * P : (b + 1) * P], x_tiles[c][:, c0 : c0 + P], ident[:])
+                damping[c, part] = ring.tile([P, H], F32, name="damping", bufs=2 * CHUNK // P)
+                nc.scalar.activation(as_pairs(damping[c, part][:]), in_pair_order(bank[:]), ACT.Exp, scale=-1.0)
 
-        def damping(c):
-            for half in range(CHUNK // P):
-                x_t = psum.tile([P, BANK], F32, name="x_t", tag="e", bufs=EB)
-                for b in range(BLOCKS):
-                    o = b * CHUNK + half * P
-                    nc.tensor.transpose(x_t[:, b * P : (b + 1) * P], picked[c][:, o : o + P], ident[:])
-                ex_t = ring.tile([P, H], F32, name="ex_t", bufs=4)
-                nc.scalar.activation(in_words(ex_t[:]), by_words(x_t[:]), ACT.Exp, scale=-1.0)
-                damp[c, half] = ex_t
-
-        def signal(c):
-            parts = [(0, 1), (1, 2)] if c == 3 else [(0, 2)]
-            made = []
-            for h0, h1 in parts:
-                bank = psum.tile([P, h1 - h0, 2, P], F32, name="z_bank", tag="d", bufs=8 - EB)
-                for half in range(h0, h1):
-                    z_t = ring.tile([P, H], BF16, name="z_t", bufs=4)
-                    nc.vector.tensor_tensor(z_t[:], damp[c, half][:], load_t[c][:, half, :], ALU.mult)
+        def damp(c):
+            spans = [(0, 1), (1, 2)] if c == CHUNKS - 1 else [(0, 2)]
+            banks = []
+            for part0, part1 in spans:
+                bank = long_bank([P, part1 - part0, 2, P])
+                for part in range(part0, part1):
+                    z_t = ring.tile([P, H], BF16, name="z_t", bufs=2 * CHUNK // P)
+                    nc.vector.tensor_tensor(z_t[:], damping[c, part][:], load_t[c][:, part, :], ALU.mult)
                     for u in range(2):
-                        nc.tensor.transpose(bank[:, half - h0, u, :], z_t[:].bitcast(F32)[:, u * P : (u + 1) * P], ident[:])
-                made.append((c * CHUNK + h0 * P, (h1 - h0) * P, bank))
-            return made
+                        nc.tensor.transpose(
+                            bank[:, part - part0, u, :], z_t[:].bitcast(F32)[:, u * P : (u + 1) * P], ident[:]
+                        )
+                banks.append((c * CHUNK + part0 * P, (part1 - part0) * P, bank))
+            return banks
 
-        def project(c, m0, width, bank):
-            z = ring.tile([P, width, PACK], BF16, name="z", align_bytes=64)
-            (nc.vector.tensor_copy if c >= 2 else nc.scalar.copy)(
-                z[:].bitcast(F32).rearrange("q (h m) u -> q h m u", m=P), bank[:].rearrange("q h u m -> q h m u")
-            )
-            z_c = ring.tile([P, width], U32, name="z_c", align_bytes=64)
-            z_s = ring.tile([P, width], U8, name="z_s", align_bytes=64)
-            nc.vector.quantize_mx(out=z_c[:].bitcast(FP8X4), scales=z_s[:], in_=z[:].rearrange("p m i -> p (m i)"))
-            group = 2 if width == CHUNK else 3
-            for pair in range(N // (group * P)):
-                acc = psum.tile([P, group, width], F32, name="acc", tag="d", bufs=8 - EB)
-                for k in range(group):
-                    n0 = (group * pair + k) * P
-                    nc.tensor.matmul_mx(
-                        out=acc[:, k, :], lhsT=wo_c[:, n0 : n0 + P].bitcast(FP8X4), lhsT_scale=wo_s[:, n0 : n0 + P],
-                        rhs=z_c[:].bitcast(FP8X4), rhs_scale=z_s[:], start=True, stop=True,
-                    )
-                res = ring.tile([P, group, width], F32, name="res", bufs=12)
-                (nc.vector.tensor_copy if c == 3 and pair == 1 else nc.scalar.copy)(res[:], acc[:])
-                nc.sync.dma_start(out_rows[:, group * pair : group * pair + group, m0 : m0 + width], res[:])
+        def project(c, banks):
+            for m0, width, bank in banks:
+                z = ring.tile([P, width, PACK], BF16, name="z", align_bytes=64)
+                move_words = nc.vector.tensor_copy if c >= CHUNKS // 2 else nc.scalar.copy
+                move_words(
+                    z[:].bitcast(F32).rearrange("q (a m) u -> q a m u", m=P), bank[:].rearrange("q a u m -> q a m u")
+                )
+                z_c = ring.tile([P, width], U32, name="z_c", align_bytes=64)
+                z_s = ring.tile([P, width], U8, name="z_s", align_bytes=64)
+                nc.vector.quantize_mx(out=z_c[:].bitcast(FP8X4), scales=z_s[:], in_=z[:].rearrange("p m i -> p (m i)"))
+                group = 2 if width == CHUNK else 3
+                for g in range(N // (group * P)):
+                    acc = long_bank([P, group, width])
+                    for k in range(group):
+                        n0 = (group * g + k) * P
+                        nc.tensor.matmul_mx(
+                            out=acc[:, k, :], lhsT=wo_c[:, n0 : n0 + P].bitcast(FP8X4), lhsT_scale=wo_s[:, n0 : n0 + P],
+                            rhs=z_c[:].bitcast(FP8X4), rhs_scale=z_s[:], start=True, stop=True,
+                        )
+                    result = ring.tile([P, group, width], F32, name="result", bufs=RESULT_BUFS)
+                    copy_out = nc.vector.tensor_copy if c == CHUNKS - 1 and g == 1 else nc.scalar.copy
+                    copy_out(result[:], acc[:])
+                    nc.sync.dma_start(out_rows[:, group * g : group * (g + 1), m0 : m0 + width], result[:])
 
-        def gather_chunk(c):
-            for b in range(BLOCKS):
-                fetch(c, b)
-            damping(c)
-
-        gather_chunk(0)
-        gather_chunk(1)
-        z = signal(0)
-        gather_chunk(2)
-        for part in z:
-            project(0, *part)
-        z = signal(1)
-        for part in z:
-            project(1, *part)
-        z = signal(2)
-        gather_chunk(3)
-        for part in z:
-            project(2, *part)
-        z = signal(3)
-        for part in z:
-            project(3, *part)
+        fetch(0)
+        fetch(1)
+        for c in range(CHUNKS):
+            banks = damp(c)
+            if c % 2 == 0:
+                fetch(2 + c // 2)
+            project(c, banks)

@@ -21,30 +21,24 @@ P = 128
 PACK = 4
 STRIPE = 16
 PLANE_ROWS = 4
+QUADS = P // 32
 PASSES = K // (P * PACK)
-PASS_BLOCKS = P * PACK // 32
 PAGES = H // P
 BANK = 512
-EARLY_PAGES = 2
 CHUNK = 256
 CHUNKS = M // CHUNK
 WO_PIECE = 256
-SHORT_BANKS = 2
-LONG_BANKS = 6
-UNIT_BUFS = 3
-RESULT_BUFS = 12
+KINDS = "EAAAAAAA"
+E_BANKS = 3
+LONG_BANKS = 4
 
 
-def interleave(nc, dst, src):
-    nc.scalar.copy(out=dst, in_=src.rearrange("p i c -> p c i"))
+def woven(planes):
+    return planes.rearrange("p i (c e) -> p c i e", e=2)
 
 
-def in_pair_order(natural):
-    return natural.rearrange("m (q u e) -> m u q e", u=2, e=2)
-
-
-def as_pairs(ordered):
-    return ordered.rearrange("m (u q e) -> m u q e", u=2, e=2)
+def woven_out(words):
+    return words.rearrange("p (c e) i -> p c i e", e=2)
 
 
 def tile_list_latency_envelopes_kernel(
@@ -58,13 +52,16 @@ def tile_list_latency_envelopes_kernel(
         psum = ctx.enter_context(tc.psum_pool(name="psum", bufs=1))
 
         def short_bank(shape):
-            return psum.tile(shape, F32, name="short_bank", bufs=SHORT_BANKS)
+            return psum.tile(shape, F32, name="short_bank", bufs=E_BANKS)
+
+        def upper_bank(shape):
+            return psum.tile(shape, F32, name="upper_bank", bufs=1)
 
         def long_bank(shape):
             return psum.tile(shape, F32, name="long_bank", bufs=LONG_BANKS)
 
         def unit_tile(name):
-            return ring.tile([P, BANK], F32, name=name, bufs=UNIT_BUFS)
+            return ring.tile([P, BANK], F32, name=name, bufs=4)
 
         idx1 = keep.tile([P, S // STRIPE], U16, name="idx1")
         idx2 = keep.tile([P, S // STRIPE], U16, name="idx2")
@@ -75,9 +72,11 @@ def tile_list_latency_envelopes_kernel(
 
         tab_s = keep.tile([P, T], U8, name="tab_s", align_bytes=64)
         v_s1 = keep.tile([P, S], U8, name="v_s1", align_bytes=64)
-        w_s = keep.tile([P, 2, PASSES, H], U8, name="w_s", align_bytes=64)
+        w2_s = keep.tile([P, H], U8, name="w2_s", align_bytes=64)
+        w3_s = keep.tile([P, PASSES, H], U8, name="w3_s", align_bytes=64)
         nc.gpsimd.memset(tab_s[:].bitcast(I32), 0)
-        nc.vector.memset(w_s[:].rearrange("p w a c -> p (w a c)").bitcast(I32), 0)
+        nc.vector.memset(w2_s[:].bitcast(I32), 0)
+        nc.vector.memset(w3_s[:].rearrange("p a c -> p (a c)").bitcast(I32), 0)
         nc.vector.memset(v_s1[:].bitcast(I32), 0)
         pages = [keep.tile([P, T2], F32, name="page0")]
         nc.vector.memset(pages[0][:].bitcast(I32), 0)
@@ -87,10 +86,7 @@ def tile_list_latency_envelopes_kernel(
             nc.gpsimd.memset(page[:].bitcast(I32), 0)
             pages.append(page)
 
-        tab_w = [
-            keep.tile([P, T], I32, name="tab_w0", tag="page1", align_bytes=64),
-            keep.tile([P, T], I32, name="tab_w1", tag="tab_w1", align_bytes=64),
-        ]
+        tab_w = [keep.tile([P, T], I32, name="tab_w", tag="page%d" % (2 + a), align_bytes=64) for a in range(PASSES)]
         w1_rows = w1.rearrange("(a p i) c -> a p i c", a=PASSES, i=PACK)
         w2_rows = w2_words.rearrange("a p c i -> p a (c i)")
         w3_rows = w3_words.rearrange("a p c -> p a c")
@@ -114,108 +110,101 @@ def tile_list_latency_envelopes_kernel(
                     w2_c[b, a] = words2[:, a, c0 : c0 + P].bitcast(FP8X4)
                     w3_c[b, a] = words3[:, a, 2 * c0 : 2 * (c0 + P)].bitcast(FP4X4)
 
-        def load_weight_scales(w, scales):
-            for row in range(PLANE_ROWS):
+        def load_packed_planes(tile, scales):
+            for q in range(QUADS):
                 nc.sync.dma_start(
-                    w_s[row:P:32, w, :, :].bitcast(I32),
-                    scales.bitcast(I32)[:, row:PASS_BLOCKS:PLANE_ROWS, :].rearrange("a q c -> q a c"),
+                    tile[32 * q : 32 * q + PASSES * PLANE_ROWS, :].bitcast(I32),
+                    scales.bitcast(I32)[:, PLANE_ROWS * q : PLANE_ROWS * (q + 1), :],
                 )
 
-        nc.sync.dma_start(idx1[:], offs)
-        ident = keep.tile([P, P], F32, name="ident")
-        make_identity(nc, ident[:])
-        load_w1(0, 0, EARLY_PAGES)
-        for q in range(P // 32):
-            nc.sync.dma_start(
-                tab_s[32 * q : 32 * q + PASSES * PLANE_ROWS, :].bitcast(I32),
-                tab_scales.bitcast(I32)[:, PLANE_ROWS * q : PLANE_ROWS * (q + 1), :],
-            )
-        load_w1(1, 0, EARLY_PAGES)
-        for a in range(PASSES):
+        def load_table_words(a):
             nc.sync.dma_start(tab_w[a][:], tab_words[a].rearrange("p t i -> p (t i)").bitcast(I32))
-        load_weight_scales(0, w2_scales)
-        load_packed(0, EARLY_PAGES)
-        load_weight_scales(1, w3_scales)
-        nc.sync.dma_start(idx2[:], offs2)
-        wgs_sb = keep.tile([P, S], F32, name="wgs_sb")
-        nc.sync.dma_start(wgs_sb[:], wgs)
-        for a in range(PASSES):
-            load_w1(a, EARLY_PAGES, PAGES)
-        load_packed(EARLY_PAGES, PAGES)
-        nc.sync.dma_start(idx3[:], offs3)
-        wo_raw = keep.tile([P, PACK, N], F32, name="wo_raw")
-        nc.sync.dma_start(wo_raw[:], wo.rearrange("(p i) n -> p i n", i=PACK))
-        load_raw = [keep.tile([P, M], F32, name="load_raw%d" % b) for b in range(PAGES)]
-        for b in range(PAGES):
-            nc.sync.dma_start(load_raw[b][:], load[b * P : (b + 1) * P, :])
 
+        nc.sync.dma_start(idx1[:], offs)
+        nc.sync.dma_start(idx2[:], offs2)
+        load_packed_planes(tab_s, tab_scales)
+        load_table_words(0)
+        load_w1(0, 0, 1)
+        load_w1(1, 0, 1)
+        load_packed_planes(w2_s, w2_scales)
+        load_table_words(1)
+        load_packed(0, 1)
+        for q in range(QUADS):
+            nc.gpsimd.dma_start(
+                w3_s[32 * q : 32 * q + PLANE_ROWS, :, :].bitcast(I32),
+                w3_scales.bitcast(I32)[:, PLANE_ROWS * q : PLANE_ROWS * (q + 1), :].rearrange("a r c -> r a c"),
+            )
         v_s = keep.tile([P, S], U8, name="v_s", align_bytes=64)
         nc.vector.tensor_copy(v_s[:], tab_s[:].indirect(idx1[:]))
         plane_span = P - 32 + PLANE_ROWS
-        nc.gpsimd.dma_start(
+        nc.sync.dma_start(
             v_s1[0:plane_span, :].bitcast(I32), v_s[PLANE_ROWS : PLANE_ROWS + plane_span, :].bitcast(I32)
         )
-        planes_packed = [v_s[PLANE_ROWS * a : P, :] for a in range(PASSES)]
-        planes_at_zero = [v_s[:], v_s1[:]]
+        wgs_sb = [keep.tile([P, BANK], F32, name="wgs_sb%d" % half) for half in range(2)]
+        nc.sync.dma_start(wgs_sb[0][:], wgs[:, :BANK])
+        for a in range(PASSES):
+            load_w1(a, 1, 2)
+        load_packed(1, 2)
+        nc.sync.dma_start(wgs_sb[1][:], wgs[:, BANK:])
+        for a in range(PASSES):
+            load_w1(a, 2, PAGES)
+        load_packed(2, PAGES)
+        nc.sync.dma_start(idx3[:], offs3)
+        wo_raw = keep.tile([P, PACK, N], F32, name="wo_raw")
+        nc.sync.dma_start(wo_raw[:], wo.rearrange("(p i) n -> p i n", i=PACK))
+        load_sb = keep.tile([P, PACK, M], F32, name="load_sb")
+        nc.sync.dma_start(load_sb[:], load.rearrange("(p i) m -> p i m", i=PACK))
+
+        planes = [v_s[:], v_s1[:]]
+        ident = keep.tile([P, P], F32, name="ident")
+        if KINDS.count("E") < len(KINDS):
+            make_identity(nc, ident[:])
 
         v_w = {}
 
-        def gather_words(a, half, tag):
-            v_w[a, half] = keep.tile([P, BANK], U32, name="v_w", tag=tag, align_bytes=64)
+        def gather_words(a, half):
+            v_w[a, half] = keep.tile([P, BANK], U32, name="v_w%d%d" % (a, half), align_bytes=64)
             nc.vector.tensor_copy(
                 v_w[a, half][:], tab_w[a][:].bitcast(U32).indirect(entries(idx1, half * BANK, (half + 1) * BANK))
             )
 
         w1_c, w1_s = {}, {}
-        w1_bf = [
-            keep.tile([P, PASSES, P, PACK], BF16, name="w1_bf", align_bytes=64,
-                      tag=("w1_bf%d" if b < EARLY_PAGES else "page%d") % b)
-            for b in range(PAGES)
-        ]
 
         def quantize_w1(b):
+            rounded = keep.tile([P, PASSES, P, PACK], BF16, name="w1_bf", tag="page1" if b == 0 else "piece%d" % (b - 1), align_bytes=64)
             for a in range(PASSES):
-                interleave(nc, w1_bf[b][:, a, :, :], w1_raw[b, a])
+                nc.scalar.copy(out=woven_out(rounded[:, a, :, :]), in_=woven(w1_raw[b, a]))
             codes = keep.tile([P, PASSES * P], U32, name="w1_c%d" % b, align_bytes=64)
             scales = keep.tile([P, PASSES * P], U8, name="w1_s%d" % b, align_bytes=64)
             nc.vector.quantize_mx(
-                out=codes[:].bitcast(FP8X4), scales=scales[:], in_=w1_bf[b][:].rearrange("p a c i -> p (a c i)")
+                out=codes[:].bitcast(FP8X4), scales=scales[:], in_=rounded[:].rearrange("p a c i -> p (a c i)")
             )
             for a in range(PASSES):
                 w1_c[b, a] = codes[:, a * P : (a + 1) * P].bitcast(FP8X4)
                 w1_s[b, a] = scales[:, a * P : (a + 1) * P]
 
-        for b in range(EARLY_PAGES):
-            quantize_w1(b)
-        gather_words(0, 0, "v_w00")
-        gather_words(1, 0, "v_w10")
-        gather_words(1, 1, "v_w11")
-        gather_words(0, 1, "tab_w1")
-        open_page()
+        gather_words(0, 0)
+        quantize_w1(0)
+        gather_words(1, 0)
+        gather_words(0, 1)
+        gather_words(1, 1)
+        for b in range(1, PAGES):
+            open_page()
 
-        wo_bf = [keep.tile([P, WO_PIECE, PACK], BF16, name="wo_bf%d" % k, align_bytes=64) for k in range(N // WO_PIECE)]
-        wo_c = keep.tile([P, N], U32, name="wo_c", align_bytes=64)
-        wo_s = keep.tile([P, N], U8, name="wo_s", align_bytes=64)
 
-        def quantize_wo(k):
-            cols = slice(WO_PIECE * k, WO_PIECE * (k + 1))
-            interleave(nc, wo_bf[k][:], wo_raw[:, :, cols])
-            nc.vector.quantize_mx(
-                out=wo_c[:, cols].bitcast(FP8X4), scales=wo_s[:, cols], in_=wo_bf[k][:].rearrange("p n i -> p (n i)")
-            )
+        wo_bf = {}
 
-        units = [(b, half) for half in range(2) for b in range(EARLY_PAGES)]
-        units = units + [(b, half) for b in range(EARLY_PAGES, PAGES) for half in range(2)]
-        last = len(units) - 1
+        def round_wo(k):
+            wo_bf[k] = keep.tile([P, WO_PIECE, PACK], BF16, name="wo_bf", tag="piece%d" % (PAGES - 1 + k), align_bytes=64)
+            nc.scalar.copy(out=woven_out(wo_bf[k][:]), in_=woven(wo_raw[:, :, WO_PIECE * k : WO_PIECE * (k + 1)]))
 
-        def turned_twice(u):
-            return units[u][0] == PAGES - 1
+        units = [(b, half) for b in range(PAGES) for half in range(2)]
 
-        def estimate(u, bank, planes, codes, scales):
+        def estimate(u, bank, codes, scales):
             b, half = units[u]
             j0 = half * BANK
             for a in range(PASSES):
-                if u == 0 or turned_twice(u):
+                if KINDS[u] != "A":
                     nc.tensor.matmul_mx(
                         out=bank[:], lhsT=codes[b, a], lhsT_scale=scales[a],
                         rhs=v_w[a, half][:].bitcast(FP8X4), rhs_scale=planes[a][:, j0 : j0 + BANK],
@@ -233,18 +222,17 @@ def tile_list_latency_envelopes_kernel(
             return bank
 
         def e1(u, bank):
-            return estimate(u, bank, planes_packed, w1_c, [w1_s[units[u][0], a] for a in range(PASSES)])
+            return estimate(u, bank, w1_c, [w1_s[units[u][0], a] for a in range(PASSES)])
 
         def e2(u, bank):
             c0 = units[u][0] * P
-            return estimate(u, bank, planes_packed, w2_c, [w_s[:, 0, a, c0 : c0 + P] for a in range(PASSES)])
+            return estimate(u, bank, w2_c, [w2_s[PLANE_ROWS * a : P, c0 : c0 + P] for a in range(PASSES)])
 
         def e3(u, bank):
             c0 = units[u][0] * P
-            return estimate(u, bank, planes_at_zero, w3_c, [w_s[:, 1, a, c0 : c0 + P] for a in range(PASSES)])
+            return estimate(u, bank, w3_c, [w3_s[:, a, c0 : c0 + P] for a in range(PASSES)])
 
-        def turned_sum(first, second):
-            bank = long_bank([P, BANK])
+        def turned_sum(first, second, bank):
             for c0 in range(0, BANK, P):
                 nc.tensor.matmul(bank[:, c0 : c0 + P], first[:, c0 : c0 + P], ident[:],
                                  start=True, stop=False, is_transpose=True)
@@ -254,149 +242,121 @@ def tile_list_latency_envelopes_kernel(
 
         def put(u, h):
             b, half = units[u]
-            j0 = half * BANK
             nc.vector.tensor_tensor(
-                pages[b][:].indirect(entries(idx2, j0, j0 + BANK)), h, wgs_sb[:, j0 : j0 + BANK], ALU.mult
+                pages[b][:].indirect(entries(idx2, half * BANK, (half + 1) * BANK)), h, wgs_sb[half][:], ALU.mult
             )
 
-        pieces = [
-            (w1_bf[b][:].rearrange("p a c i -> p (a c i)").bitcast(F32), quantize_w1, b)
-            for b in range(EARLY_PAGES, PAGES)
-        ]
-        pieces = pieces + [
-            (tile[:].rearrange("p n i -> p (n i)").bitcast(F32), quantize_wo, k) for k, tile in enumerate(wo_bf)
-        ]
-        first_x = [keep.tile([P, PAGES * CHUNK], F32, name="first_x%d" % c) for c in range(2)]
-        pos2, neg1, neg3, above = {}, {}, {}, {}
+        def scaled_copy(name, bank, func, scale):
+            tile = unit_tile(name) if isinstance(name, str) else name
+            nc.scalar.activation(tile[:], bank[:], func, scale=scale)
+            return tile
 
-        def copy_e2(u):
-            bank = e2(u, short_bank([P, BANK]))
-            pos2[u] = unit_tile("pos2")
-            nc.scalar.activation(pos2[u][:], bank[:], ACT.Copy, scale=1.0)
+        pos2, neg1, neg3 = {}, {}, {}
 
-        def negate_e1(u):
-            bank = e1(u, short_bank([P, BANK]))
-            neg1[u] = unit_tile("neg1")
-            nc.scalar.activation(neg1[u][:], bank[:], ACT.Copy, scale=-1.0)
-
-        def negate_e3(u):
-            bank = e3(u, short_bank([P, BANK]))
-            neg3[u] = pieces[u - 1][0] if u <= len(pieces) else unit_tile("neg3")
-            nc.scalar.activation(neg3[u][:], bank[:], ACT.Copy, scale=-1.0)
-
-        def upper_part(u):
-            bank = turned_sum(pos2[u], neg1[u])
-            above[u] = unit_tile("above")
-            nc.scalar.activation(above[u][:], bank[:], ACT.Relu, scale=-1.0)
-
-        def lower_part_and_put(u):
-            bank = turned_sum(pos2[u], neg3[u])
-            h = first_x[u - last + 1][:, :BANK] if u >= last - 1 else unit_tile("h")[:]
-            if turned_twice(u):
-                below = ring.tile([P, BANK], F32, name="below")
-                nc.scalar.activation(below[:], bank[:], ACT.Relu)
-                nc.scalar.copy(h, turned_sum(above[u], below)[:])
+        def estimates(u):
+            place = "pos2"
+            if u < PAGES - 1 + N // WO_PIECE:
+                place = keep.tile([P, BANK], F32, name="pos2", tag="piece%d" % u, align_bytes=64)
+            if KINDS[u] == "E":
+                pos2[u] = scaled_copy(place, e2(u, short_bank([P, BANK])), ACT.Copy, 1.0)
+                neg1[u] = e1(u, long_bank([P, BANK]))
+                neg3[u] = e3(u, long_bank([P, BANK]))
             else:
-                nc.vector.scalar_tensor_tensor(h, bank[:], 0.0, above[u][:], ALU.max, ALU.add)
-            put(u, h)
-            if u <= len(pieces):
-                pieces[u - 1][1](pieces[u - 1][2])
+                neg3[u] = scaled_copy("neg3", e3(u, short_bank([P, BANK])), ACT.Copy, -1.0)
+                pos2[u] = scaled_copy(place, e2(u, short_bank([P, BANK])), ACT.Copy, 1.0)
+                neg1[u] = scaled_copy("neg1", e1(u, short_bank([P, BANK])), ACT.Copy, -1.0)
 
-        copy_e2(0)
-        high_bank = e1(0, long_bank([P, BANK]))
-        high = unit_tile("neg1")
-        nc.vector.tensor_tensor(high[:], high_bank[:], pos2[0][:], ALU.max)
-        low_bank = e3(0, long_bank([P, BANK]))
-        low = unit_tile("neg3")
-        nc.vector.tensor_tensor(low[:], low_bank[:], pos2[0][:], ALU.min)
-        spread = unit_tile("h")
-        nc.vector.tensor_tensor(spread[:], high[:], low[:], ALU.subtract)
-        put(0, spread[:])
+        def envelope(u):
+            h = unit_tile("h") if u < len(units) - 1 else keep.tile([P, BANK], F32, name="h", tag="wo_c", align_bytes=64)
+            spare = neg3[u]
+            if KINDS[u] == "E":
+                high = unit_tile("neg1")
+                nc.vector.tensor_tensor(high[:], neg1[u][:], pos2[u][:], ALU.max)
+                low = unit_tile("neg3")
+                nc.vector.tensor_tensor(low[:], neg3[u][:], pos2[u][:], ALU.min)
+                nc.vector.tensor_tensor(h[:], high[:], low[:], ALU.subtract)
+                spare = low
+            else:
+                bank = turned_sum(pos2[u], neg3[u], long_bank([P, BANK]))
+                above = scaled_copy("above", turned_sum(pos2[u], neg1[u], upper_bank([P, BANK])), ACT.Relu, -1.0)
+                if KINDS[u] == "A":
+                    nc.vector.scalar_tensor_tensor(h[:], bank[:], 0.0, above[:], ALU.max, ALU.add)
+                else:
+                    below = scaled_copy("below", bank, ACT.Relu, 1.0)
+                    nc.scalar.copy(h[:], turned_sum(above, below, long_bank([P, BANK]))[:])
+            return h, spare
 
-        copy_e2(1)
-        negate_e1(1)
-        negate_e3(1)
-        for u in range(1, last):
-            copy_e2(u + 1)
-            upper_part(u)
-            negate_e1(u + 1)
-            lower_part_and_put(u)
-            negate_e3(u + 1)
-            if len(pages) < PAGES:
-                open_page()
-        upper_part(last)
-        lower_part_and_put(last)
+        damping = keep.tile([P, CHUNKS, PACK, CHUNK], F32, name="damping")
 
-        load_t = [keep.tile([P, CHUNK // P, H], F32, name="load_t%d" % c) for c in range(CHUNKS)]
-        for c in range(CHUNKS):
-            for part in range(CHUNK // P):
-                bank = long_bank([P, H])
-                m0 = c * CHUNK + part * P
-                for b in range(PAGES):
-                    nc.tensor.transpose(bank[:, b * P : (b + 1) * P], load_raw[b][:, m0 : m0 + P], ident[:])
-                nc.scalar.copy(as_pairs(load_t[c][:, part, :]), in_pair_order(bank[:]))
+        def fetch(b, c0, c1, x):
+            nc.vector.tensor_copy(x, pages[b][:].indirect(entries(idx3, c0 * CHUNK, c1 * CHUNK)))
 
-        x_tiles = [tile[:] for tile in first_x] + [tile[:].rearrange("m a r -> m (a r)") for tile in load_t[0::2]]
-        out_rows = out.rearrange("(i p) m -> p i m", p=P)
-        damping = {}
-
-        def fetch(c):
-            for b in range(PAGES):
-                nc.vector.tensor_copy(
-                    x_tiles[c][:, b * CHUNK : (b + 1) * CHUNK],
-                    pages[b][:].indirect(entries(idx3, c * CHUNK, (c + 1) * CHUNK)),
+        def spread(b, c0, c1, x, e):
+            nc.scalar.activation(e[:], x, ACT.Exp, scale=-1.0)
+            for i in range(PACK):
+                nc.sync.dma_start(
+                    damping[32 * b : 32 * (b + 1), c0:c1, i, :], e[i:P:PACK, :].rearrange("p (c m) -> p c m", m=CHUNK)
                 )
-            for part in range(CHUNK // P):
-                bank = short_bank([P, H])
-                for b in range(PAGES):
-                    c0 = b * CHUNK + part * P
-                    nc.tensor.transpose(bank[:, b * P : (b + 1) * P], x_tiles[c][:, c0 : c0 + P], ident[:])
-                damping[c, part] = ring.tile([P, H], F32, name="damping", bufs=2 * CHUNK // P)
-                nc.scalar.activation(as_pairs(damping[c, part][:]), in_pair_order(bank[:]), ACT.Exp, scale=-1.0)
+
+        fetched = {}
+        for u in range(len(units)):
+            b, half = units[u]
+            if u <= 2:
+                estimates(u)
+            if 2 <= u < len(units) - 1:
+                estimates(u + 1)
+            h, spare = envelope(u)
+            if b > 0:
+                fetched[u] = (b - 1, 2 * half, 2 * half + 2, spare[:])
+                fetch(*fetched[u])
+            put(u, h[:])
+            if u - 1 in fetched:
+                spread(*fetched[u - 1], neg1[u])
+            if u < PAGES - 1:
+                quantize_w1(u + 1)
+            elif u < PAGES - 1 + N // WO_PIECE:
+                round_wo(u - PAGES + 1)
+
+        last_x = keep.tile([P, M], F32, name="last_x")
+        spread(*fetched[len(units) - 1], unit_tile("neg1"))
+        for c in range(CHUNKS):
+            fetch(PAGES - 1, c, c + 1, last_x[:, c * CHUNK : (c + 1) * CHUNK])
+            last_e = ring.tile([P, CHUNK], F32, name="last_e", bufs=CHUNKS)
+            spread(PAGES - 1, c, c + 1, last_x[:, c * CHUNK : (c + 1) * CHUNK], last_e)
+        wo_c = keep.tile([P, N], U32, name="wo_c", tag="wo_c", align_bytes=64)
+        wo_s = keep.tile([P, N], U8, name="wo_s", align_bytes=64)
+        for k in range(N // WO_PIECE):
+            cols = slice(WO_PIECE * k, WO_PIECE * (k + 1))
+            nc.vector.quantize_mx(
+                out=wo_c[:, cols].bitcast(FP8X4), scales=wo_s[:, cols], in_=wo_bf[k][:].rearrange("p n i -> p (n i)")
+            )
+        out_rows = out.rearrange("(i p) m -> p i m", p=P)
+        z = {}
 
         def damp(c):
-            spans = [(0, 1), (1, 2)] if c == CHUNKS - 1 else [(0, 2)]
-            banks = []
-            for part0, part1 in spans:
-                bank = long_bank([P, part1 - part0, 2, P])
-                for part in range(part0, part1):
-                    z_t = ring.tile([P, H], BF16, name="z_t", bufs=2 * CHUNK // P)
-                    nc.vector.tensor_tensor(z_t[:], damping[c, part][:], load_t[c][:, part, :], ALU.mult)
-                    for u in range(2):
-                        nc.tensor.transpose(
-                            bank[:, part - part0, u, :], z_t[:].bitcast(F32)[:, u * P : (u + 1) * P], ident[:]
-                        )
-                banks.append((c * CHUNK + part0 * P, (part1 - part0) * P, bank))
-            return banks
+            z[c] = ring.tile([P, CHUNK, PACK], BF16, name="z", align_bytes=64, bufs=3)
+            nc.vector.tensor_tensor(
+                woven_out(z[c][:]), woven(damping[:, c, :, :]), woven(load_sb[:, :, c * CHUNK : (c + 1) * CHUNK]),
+                ALU.mult,
+            )
 
-        def project(c, banks):
-            for m0, width, bank in banks:
-                z = ring.tile([P, width, PACK], BF16, name="z", align_bytes=64)
-                move_words = nc.vector.tensor_copy if c >= CHUNKS // 2 else nc.scalar.copy
-                move_words(
-                    z[:].bitcast(F32).rearrange("q (a m) u -> q a m u", m=P), bank[:].rearrange("q a u m -> q a m u")
-                )
-                z_c = ring.tile([P, width], U32, name="z_c", align_bytes=64)
-                z_s = ring.tile([P, width], U8, name="z_s", align_bytes=64)
-                nc.vector.quantize_mx(out=z_c[:].bitcast(FP8X4), scales=z_s[:], in_=z[:].rearrange("p m i -> p (m i)"))
-                group = 2 if width == CHUNK else 3
-                for g in range(N // (group * P)):
-                    acc = long_bank([P, group, width])
-                    for k in range(group):
-                        n0 = (group * g + k) * P
-                        nc.tensor.matmul_mx(
-                            out=acc[:, k, :], lhsT=wo_c[:, n0 : n0 + P].bitcast(FP8X4), lhsT_scale=wo_s[:, n0 : n0 + P],
-                            rhs=z_c[:].bitcast(FP8X4), rhs_scale=z_s[:], start=True, stop=True,
-                        )
-                    result = ring.tile([P, group, width], F32, name="result", bufs=RESULT_BUFS)
-                    copy_out = nc.vector.tensor_copy if c == CHUNKS - 1 and g == 1 else nc.scalar.copy
-                    copy_out(result[:], acc[:])
-                    nc.sync.dma_start(out_rows[:, group * g : group * (g + 1), m0 : m0 + width], result[:])
+        def project(c):
+            z_c = ring.tile([P, CHUNK], U32, name="z_c", align_bytes=64)
+            z_s = ring.tile([P, CHUNK], U8, name="z_s", align_bytes=64)
+            nc.vector.quantize_mx(out=z_c[:].bitcast(FP8X4), scales=z_s[:], in_=z[c][:].rearrange("p m i -> p (m i)"))
+            for g in range(N // (2 * P)):
+                acc = (long_bank if g % 2 == 0 else short_bank)([P, 2, CHUNK])
+                for k in range(2):
+                    n0 = (2 * g + k) * P
+                    nc.tensor.matmul_mx(
+                        out=acc[:, k, :], lhsT=wo_c[:, n0 : n0 + P].bitcast(FP8X4), lhsT_scale=wo_s[:, n0 : n0 + P],
+                        rhs=z_c[:].bitcast(FP8X4), rhs_scale=z_s[:], start=True, stop=True,
+                    )
+                result = ring.tile([P, 2, CHUNK], F32, name="result", bufs=12)
+                copy_out = nc.vector.tensor_copy if c == CHUNKS - 1 and g == 1 else nc.scalar.copy
+                copy_out(result[:], acc[:])
+                nc.sync.dma_start(out_rows[:, 2 * g : 2 * (g + 1), c * CHUNK : (c + 1) * CHUNK], result[:])
 
-        fetch(0)
-        fetch(1)
         for c in range(CHUNKS):
-            banks = damp(c)
-            if c % 2 == 0:
-                fetch(2 + c // 2)
-            project(c, banks)
+            damp(c)
+            project(c)

@@ -28,7 +28,7 @@ BANK = 512
 CHUNK = 256
 CHUNKS = M // CHUNK
 WO_PIECE = 256
-KINDS = "EAAAAAAA"
+KINDS = "EAABBBBB"
 E_BANKS = 3
 LONG_BANKS = 4
 
@@ -121,16 +121,15 @@ def tile_list_latency_envelopes_kernel(
             nc.sync.dma_start(tab_w[a][:], tab_words[a].rearrange("p t i -> p (t i)").bitcast(I32))
 
         nc.sync.dma_start(idx1[:], offs)
-        nc.sync.dma_start(idx2[:], offs2)
         load_packed_planes(tab_s, tab_scales)
+        load_packed(0, 1)
         load_table_words(0)
         load_w1(0, 0, 1)
         load_w1(1, 0, 1)
         load_packed_planes(w2_s, w2_scales)
         load_table_words(1)
-        load_packed(0, 1)
         for q in range(QUADS):
-            nc.gpsimd.dma_start(
+            nc.sync.dma_start(
                 w3_s[32 * q : 32 * q + PLANE_ROWS, :, :].bitcast(I32),
                 w3_scales.bitcast(I32)[:, PLANE_ROWS * q : PLANE_ROWS * (q + 1), :].rearrange("a r c -> r a c"),
             )
@@ -140,7 +139,8 @@ def tile_list_latency_envelopes_kernel(
         nc.sync.dma_start(
             v_s1[0:plane_span, :].bitcast(I32), v_s[PLANE_ROWS : PLANE_ROWS + plane_span, :].bitcast(I32)
         )
-        wgs_sb = [keep.tile([P, BANK], F32, name="wgs_sb%d" % half) for half in range(2)]
+        nc.sync.dma_start(idx2[:], offs2)
+        wgs_sb = [keep.tile([P, BANK], F32, name="wgs_sb", tag="wgs%d" % half) for half in range(2)]
         nc.sync.dma_start(wgs_sb[0][:], wgs[:, :BANK])
         for a in range(PASSES):
             load_w1(a, 1, 2)
@@ -251,7 +251,7 @@ def tile_list_latency_envelopes_kernel(
             nc.scalar.activation(tile[:], bank[:], func, scale=scale)
             return tile
 
-        pos2, neg1, neg3 = {}, {}, {}
+        pos2, neg1, neg3, late = {}, {}, {}, {}
 
         def estimates(u):
             place = "pos2"
@@ -278,12 +278,15 @@ def tile_list_latency_envelopes_kernel(
                 spare = low
             else:
                 bank = turned_sum(pos2[u], neg3[u], long_bank([P, BANK]))
+                if KINDS[u] == "B":
+                    below = scaled_copy("below", bank, ACT.Relu, 1.0)
                 above = scaled_copy("above", turned_sum(pos2[u], neg1[u], upper_bank([P, BANK])), ACT.Relu, -1.0)
+                late[u] = neg1[u]
                 if KINDS[u] == "A":
                     nc.vector.scalar_tensor_tensor(h[:], bank[:], 0.0, above[:], ALU.max, ALU.add)
                 else:
-                    below = scaled_copy("below", bank, ACT.Relu, 1.0)
                     nc.scalar.copy(h[:], turned_sum(above, below, long_bank([P, BANK]))[:])
+                    spare, late[u] = below, above
             return h, spare
 
         damping = keep.tile([P, CHUNKS, PACK, CHUNK], F32, name="damping")
@@ -306,23 +309,28 @@ def tile_list_latency_envelopes_kernel(
             if 2 <= u < len(units) - 1:
                 estimates(u + 1)
             h, spare = envelope(u)
-            if b > 0:
+            if b > 0 and u < len(units) - 1:
                 fetched[u] = (b - 1, 2 * half, 2 * half + 2, spare[:])
                 fetch(*fetched[u])
             put(u, h[:])
             if u - 1 in fetched:
-                spread(*fetched[u - 1], neg1[u])
+                spread(*fetched[u - 1], late[u])
             if u < PAGES - 1:
                 quantize_w1(u + 1)
             elif u < PAGES - 1 + N // WO_PIECE:
                 round_wo(u - PAGES + 1)
 
         last_x = keep.tile([P, M], F32, name="last_x")
-        spread(*fetched[len(units) - 1], unit_tile("neg1"))
-        for c in range(CHUNKS):
-            fetch(PAGES - 1, c, c + 1, last_x[:, c * CHUNK : (c + 1) * CHUNK])
-            last_e = ring.tile([P, CHUNK], F32, name="last_e", bufs=CHUNKS)
-            spread(PAGES - 1, c, c + 1, last_x[:, c * CHUNK : (c + 1) * CHUNK], last_e)
+        late_x = keep.tile([P, BANK], F32, name="late_x", tag="wgs1")
+        for b, c0, c1, x in [
+            (PAGES - 1, 0, 1, last_x[:, :CHUNK]),
+            (PAGES - 1, 1, 2, last_x[:, CHUNK:BANK]),
+            (PAGES - 1, 2, 4, last_x[:, BANK:]),
+            (PAGES - 2, 2, 4, late_x[:]),
+        ]:
+            fetch(b, c0, c1, x)
+            last_e = ring.tile([P, (c1 - c0) * CHUNK], F32, name="last_e", bufs=CHUNKS)
+            spread(b, c0, c1, x, last_e)
         wo_c = keep.tile([P, N], U32, name="wo_c", tag="wo_c", align_bytes=64)
         wo_s = keep.tile([P, N], U8, name="wo_s", align_bytes=64)
         for k in range(N // WO_PIECE):
@@ -353,7 +361,7 @@ def tile_list_latency_envelopes_kernel(
                         rhs=z_c[:].bitcast(FP8X4), rhs_scale=z_s[:], start=True, stop=True,
                     )
                 result = ring.tile([P, 2, CHUNK], F32, name="result", bufs=12)
-                copy_out = nc.vector.tensor_copy if c == CHUNKS - 1 and g == 1 else nc.scalar.copy
+                copy_out = nc.vector.tensor_copy if (c, g) in ((CHUNKS - 2, 2), (CHUNKS - 1, 1)) else nc.scalar.copy
                 copy_out(result[:], acc[:])
                 nc.sync.dma_start(out_rows[:, 2 * g : 2 * (g + 1), c * CHUNK : (c + 1) * CHUNK], result[:])
 

@@ -28,7 +28,7 @@ BANK = 512
 CHUNK = 256
 CHUNKS = M // CHUNK
 WO_PIECE = 256
-KINDS = "EAABBBBB"
+KINDS = "EAAADDDD"
 E_BANKS = 3
 LONG_BANKS = 4
 
@@ -204,7 +204,7 @@ def tile_list_latency_envelopes_kernel(
             b, half = units[u]
             j0 = half * BANK
             for a in range(PASSES):
-                if KINDS[u] != "A":
+                if KINDS[u] in ("E", "B"):
                     nc.tensor.matmul_mx(
                         out=bank[:], lhsT=codes[b, a], lhsT_scale=scales[a],
                         rhs=v_w[a, half][:].bitcast(FP8X4), rhs_scale=planes[a][:, j0 : j0 + BANK],
@@ -232,6 +232,8 @@ def tile_list_latency_envelopes_kernel(
             c0 = units[u][0] * P
             return estimate(u, bank, w3_c, [w3_s[:, a, c0 : c0 + P] for a in range(PASSES)])
 
+        weighted = {}
+
         def turned_sum(first, second, bank):
             for c0 in range(0, BANK, P):
                 nc.tensor.matmul(bank[:, c0 : c0 + P], first[:, c0 : c0 + P], ident[:],
@@ -240,8 +242,18 @@ def tile_list_latency_envelopes_kernel(
                                  start=False, stop=True, is_transpose=True)
             return bank
 
+        def weigh(u, h):
+            if KINDS[u] == "D":
+                weighted[u] = unit_tile("weighted")
+                nc.gpsimd.tensor_tensor(weighted[u][:], h, wgs_sb[units[u][1]][:], ALU.mult)
+
         def put(u, h):
             b, half = units[u]
+            if KINDS[u] == "D":
+                nc.vector.tensor_copy(
+                    pages[b][:].indirect(entries(idx2, half * BANK, (half + 1) * BANK)), weighted[u][:]
+                )
+                return
             nc.vector.tensor_tensor(
                 pages[b][:].indirect(entries(idx2, half * BANK, (half + 1) * BANK)), h, wgs_sb[half][:], ALU.mult
             )
@@ -267,7 +279,7 @@ def tile_list_latency_envelopes_kernel(
                 neg1[u] = scaled_copy("neg1", e1(u, short_bank([P, BANK])), ACT.Copy, -1.0)
 
         def envelope(u):
-            h = unit_tile("h") if u < len(units) - 1 else keep.tile([P, BANK], F32, name="h", tag="wo_c", align_bytes=64)
+            h = unit_tile("h")
             spare = neg3[u]
             if KINDS[u] == "E":
                 high = unit_tile("neg1")
@@ -278,12 +290,15 @@ def tile_list_latency_envelopes_kernel(
                 spare = low
             else:
                 bank = turned_sum(pos2[u], neg3[u], long_bank([P, BANK]))
-                if KINDS[u] == "B":
+                if KINDS[u] != "A":
                     below = scaled_copy("below", bank, ACT.Relu, 1.0)
                 above = scaled_copy("above", turned_sum(pos2[u], neg1[u], upper_bank([P, BANK])), ACT.Relu, -1.0)
                 late[u] = neg1[u]
                 if KINDS[u] == "A":
                     nc.vector.scalar_tensor_tensor(h[:], bank[:], 0.0, above[:], ALU.max, ALU.add)
+                elif KINDS[u] == "D":
+                    nc.gpsimd.tensor_tensor(h[:], above[:], below[:], ALU.add)
+                    spare, late[u] = below, above
                 else:
                     nc.scalar.copy(h[:], turned_sum(above, below, long_bank([P, BANK]))[:])
                     spare, late[u] = below, above
@@ -309,19 +324,21 @@ def tile_list_latency_envelopes_kernel(
             if 2 <= u < len(units) - 1:
                 estimates(u + 1)
             h, spare = envelope(u)
+            weigh(u, h[:])
             if b > 0 and u < len(units) - 1:
                 fetched[u] = (b - 1, 2 * half, 2 * half + 2, spare[:])
                 fetch(*fetched[u])
             put(u, h[:])
-            if u - 1 in fetched:
-                spread(*fetched[u - 1], late[u])
+            if u - 2 in fetched:
+                spread(*fetched[u - 2], late[u])
             if u < PAGES - 1:
                 quantize_w1(u + 1)
             elif u < PAGES - 1 + N // WO_PIECE:
                 round_wo(u - PAGES + 1)
 
+        spread(*fetched[len(units) - 2], unit_tile("neg1"))
         last_x = keep.tile([P, M], F32, name="last_x")
-        late_x = keep.tile([P, BANK], F32, name="late_x", tag="wgs1")
+        late_x = weighted[len(units) - 1]
         for b, c0, c1, x in [
             (PAGES - 1, 0, 1, last_x[:, :CHUNK]),
             (PAGES - 1, 1, 2, last_x[:, CHUNK:BANK]),
@@ -331,7 +348,7 @@ def tile_list_latency_envelopes_kernel(
             fetch(b, c0, c1, x)
             last_e = ring.tile([P, (c1 - c0) * CHUNK], F32, name="last_e", bufs=CHUNKS)
             spread(b, c0, c1, x, last_e)
-        wo_c = keep.tile([P, N], U32, name="wo_c", tag="wo_c", align_bytes=64)
+        wo_c = keep.tile([P, N], U32, name="wo_c", tag="page2", align_bytes=64)
         wo_s = keep.tile([P, N], U8, name="wo_s", align_bytes=64)
         for k in range(N // WO_PIECE):
             cols = slice(WO_PIECE * k, WO_PIECE * (k + 1))

@@ -28,8 +28,10 @@ BANK = 512
 CHUNK = 256
 CHUNKS = M // CHUNK
 WO_PIECE = 256
-KINDS = "EAAADDDD"
+KINDS = "EAFDDDDD"
+STOP = 8
 E_BANKS = 3
+WO_UNIT = 2 * PAGES - N // WO_PIECE
 LONG_BANKS = 4
 
 
@@ -61,7 +63,7 @@ def tile_list_latency_envelopes_kernel(
             return psum.tile(shape, F32, name="long_bank", bufs=LONG_BANKS)
 
         def unit_tile(name):
-            return ring.tile([P, BANK], F32, name=name, bufs=4)
+            return ring.tile([P, BANK], F32, name=name, bufs=3 if name == "pos2" else 4, align_bytes=64)
 
         idx1 = keep.tile([P, S // STRIPE], U16, name="idx1")
         idx2 = keep.tile([P, S // STRIPE], U16, name="idx2")
@@ -75,18 +77,25 @@ def tile_list_latency_envelopes_kernel(
         w2_s = keep.tile([P, H], U8, name="w2_s", align_bytes=64)
         w3_s = keep.tile([P, PASSES, H], U8, name="w3_s", align_bytes=64)
         nc.gpsimd.memset(tab_s[:].bitcast(I32), 0)
-        nc.vector.memset(w2_s[:].bitcast(I32), 0)
-        nc.vector.memset(w3_s[:].rearrange("p a c -> p (a c)").bitcast(I32), 0)
-        nc.vector.memset(v_s1[:].bitcast(I32), 0)
-        pages = [keep.tile([P, T2], F32, name="page0")]
-        nc.vector.memset(pages[0][:].bitcast(I32), 0)
+        nc.gpsimd.memset(w2_s[:].bitcast(I32), 0)
+        nc.gpsimd.memset(w3_s[:].rearrange("p a c -> p (a c)").bitcast(I32), 0)
+        nc.gpsimd.memset(v_s1[:].bitcast(I32), 0)
+        pages = []
 
         def open_page():
             page = keep.tile([P, T2], F32, name="page", tag="page%d" % len(pages), align_bytes=64)
             nc.gpsimd.memset(page[:].bitcast(I32), 0)
             pages.append(page)
 
-        tab_w = [keep.tile([P, T], I32, name="tab_w", tag="page%d" % (2 + a), align_bytes=64) for a in range(PASSES)]
+        for q in range(QUADS):
+            nc.gpsimd.dma_start(
+                w3_s[32 * q : 32 * q + PLANE_ROWS, :, :].bitcast(I32),
+                w3_scales.bitcast(I32)[:, PLANE_ROWS * q : PLANE_ROWS * (q + 1), :].rearrange("a r c -> r a c"),
+            )
+        open_page()
+        open_page()
+
+        tab_w = [keep.tile([P, T], I32, name="tab_w", tag="tab_w%d" % a, align_bytes=64) for a in range(PASSES)]
         w1_rows = w1.rearrange("(a p i) c -> a p i c", a=PASSES, i=PACK)
         w2_rows = w2_words.rearrange("a p c i -> p a (c i)")
         w3_rows = w3_words.rearrange("a p c -> p a c")
@@ -128,22 +137,17 @@ def tile_list_latency_envelopes_kernel(
         load_w1(1, 0, 1)
         load_packed_planes(w2_s, w2_scales)
         load_table_words(1)
-        for q in range(QUADS):
-            nc.sync.dma_start(
-                w3_s[32 * q : 32 * q + PLANE_ROWS, :, :].bitcast(I32),
-                w3_scales.bitcast(I32)[:, PLANE_ROWS * q : PLANE_ROWS * (q + 1), :].rearrange("a r c -> r a c"),
-            )
         v_s = keep.tile([P, S], U8, name="v_s", align_bytes=64)
         nc.vector.tensor_copy(v_s[:], tab_s[:].indirect(idx1[:]))
         plane_span = P - 32 + PLANE_ROWS
         nc.sync.dma_start(
             v_s1[0:plane_span, :].bitcast(I32), v_s[PLANE_ROWS : PLANE_ROWS + plane_span, :].bitcast(I32)
         )
-        nc.sync.dma_start(idx2[:], offs2)
-        wgs_sb = [keep.tile([P, BANK], F32, name="wgs_sb", tag="wgs%d" % half) for half in range(2)]
-        nc.sync.dma_start(wgs_sb[0][:], wgs[:, :BANK])
         for a in range(PASSES):
             load_w1(a, 1, 2)
+        wgs_sb = [keep.tile([P, BANK], F32, name="wgs_sb", tag="wgs%d" % half) for half in range(2)]
+        nc.sync.dma_start(wgs_sb[0][:], wgs[:, :BANK])
+        nc.sync.dma_start(idx2[:], offs2)
         load_packed(1, 2)
         nc.sync.dma_start(wgs_sb[1][:], wgs[:, BANK:])
         for a in range(PASSES):
@@ -171,32 +175,37 @@ def tile_list_latency_envelopes_kernel(
         w1_c, w1_s = {}, {}
 
         def quantize_w1(b):
-            rounded = keep.tile([P, PASSES, P, PACK], BF16, name="w1_bf", tag="page1" if b == 0 else "piece%d" % (b - 1), align_bytes=64)
+            rounded = keep.tile([P, PASSES, P, PACK], BF16, name="w1_bf", tag=("page%d" % (2 + b)) if b < 2 else ("piece%d" % (b - 1)), align_bytes=64)
+            codes = keep.tile([P, PASSES * P], U32, name="w1_c", tag="w1_c%d" % b, align_bytes=64)
+            scales = keep.tile([P, PASSES * P], U8, name="w1_s%d" % b, align_bytes=64)
             for a in range(PASSES):
                 nc.scalar.copy(out=woven_out(rounded[:, a, :, :]), in_=woven(w1_raw[b, a]))
-            codes = keep.tile([P, PASSES * P], U32, name="w1_c%d" % b, align_bytes=64)
-            scales = keep.tile([P, PASSES * P], U8, name="w1_s%d" % b, align_bytes=64)
-            nc.vector.quantize_mx(
-                out=codes[:].bitcast(FP8X4), scales=scales[:], in_=rounded[:].rearrange("p a c i -> p (a c i)")
-            )
-            for a in range(PASSES):
                 w1_c[b, a] = codes[:, a * P : (a + 1) * P].bitcast(FP8X4)
                 w1_s[b, a] = scales[:, a * P : (a + 1) * P]
+                if b == 0:
+                    nc.vector.quantize_mx(
+                        out=w1_c[b, a], scales=w1_s[b, a], in_=rounded[:, a, :, :].rearrange("p c i -> p (c i)")
+                    )
+            if b > 0:
+                nc.vector.quantize_mx(
+                    out=codes[:].bitcast(FP8X4), scales=scales[:], in_=rounded[:].rearrange("p a c i -> p (a c i)")
+                )
 
         gather_words(0, 0)
         quantize_w1(0)
         gather_words(1, 0)
         gather_words(0, 1)
         gather_words(1, 1)
-        for b in range(1, PAGES):
-            open_page()
+        open_page()
 
 
+        pos2, neg1, neg3, late = {}, {}, {}, {}
         wo_bf = {}
 
         def round_wo(k):
-            wo_bf[k] = keep.tile([P, WO_PIECE, PACK], BF16, name="wo_bf", tag="piece%d" % (PAGES - 1 + k), align_bytes=64)
-            nc.scalar.copy(out=woven_out(wo_bf[k][:]), in_=woven(wo_raw[:, :, WO_PIECE * k : WO_PIECE * (k + 1)]))
+            place = (neg3, neg1, pos2)[k][2 * PAGES - 1]
+            wo_bf[k] = place[:].bitcast(BF16).rearrange("p (n i) -> p n i", i=PACK)
+            nc.scalar.copy(out=woven_out(wo_bf[k]), in_=woven(wo_raw[:, :, WO_PIECE * k : WO_PIECE * (k + 1)]))
 
         units = [(b, half) for b in range(PAGES) for half in range(2)]
 
@@ -243,13 +252,13 @@ def tile_list_latency_envelopes_kernel(
             return bank
 
         def weigh(u, h):
-            if KINDS[u] == "D":
+            if KINDS[u] in ("D", "F"):
                 weighted[u] = unit_tile("weighted")
                 nc.gpsimd.tensor_tensor(weighted[u][:], h, wgs_sb[units[u][1]][:], ALU.mult)
 
         def put(u, h):
             b, half = units[u]
-            if KINDS[u] == "D":
+            if KINDS[u] in ("D", "F"):
                 nc.vector.tensor_copy(
                     pages[b][:].indirect(entries(idx2, half * BANK, (half + 1) * BANK)), weighted[u][:]
                 )
@@ -263,48 +272,42 @@ def tile_list_latency_envelopes_kernel(
             nc.scalar.activation(tile[:], bank[:], func, scale=scale)
             return tile
 
-        pos2, neg1, neg3, late = {}, {}, {}, {}
 
-        def estimates(u):
-            place = "pos2"
-            if u < PAGES - 1 + N // WO_PIECE:
-                place = keep.tile([P, BANK], F32, name="pos2", tag="piece%d" % u, align_bytes=64)
-            if KINDS[u] == "E":
-                pos2[u] = scaled_copy(place, e2(u, short_bank([P, BANK])), ACT.Copy, 1.0)
-                neg1[u] = e1(u, long_bank([P, BANK]))
-                neg3[u] = e3(u, long_bank([P, BANK]))
-            else:
-                neg3[u] = scaled_copy("neg3", e3(u, short_bank([P, BANK])), ACT.Copy, -1.0)
-                pos2[u] = scaled_copy(place, e2(u, short_bank([P, BANK])), ACT.Copy, 1.0)
-                neg1[u] = scaled_copy("neg1", e1(u, short_bank([P, BANK])), ACT.Copy, -1.0)
+        def pos2_place(u):
+            if 0 < u < PAGES - 1:
+                return keep.tile([P, BANK], F32, name="pos2", tag="piece%d" % u, align_bytes=64)
+            return "pos2"
 
-        def envelope(u):
+        def copy_e2(u):
+            pos2[u] = scaled_copy(pos2_place(u), e2(u, short_bank([P, BANK])), ACT.Copy, 1.0)
+
+        def negate_e1(u):
+            neg1[u] = scaled_copy("neg1", e1(u, short_bank([P, BANK])), ACT.Copy, -1.0)
+
+        def negate_e3(u):
+            neg3[u] = scaled_copy("neg3", e3(u, short_bank([P, BANK])), ACT.Copy, -1.0)
+
+        lower, spare = {}, {}
+
+        def lower_part(u):
+            lower[u] = turned_sum(pos2[u], neg3[u], long_bank([P, BANK]))
+            if KINDS[u] == "D":
+                lower[u] = scaled_copy("below", lower[u], ACT.Relu, 1.0)
+
+        def upper_part(u):
+            above = scaled_copy("above", turned_sum(neg1[u], pos2[u], upper_bank([P, BANK])), ACT.Relu, -1.0)
             h = unit_tile("h")
-            spare = neg3[u]
-            if KINDS[u] == "E":
-                high = unit_tile("neg1")
-                nc.vector.tensor_tensor(high[:], neg1[u][:], pos2[u][:], ALU.max)
-                low = unit_tile("neg3")
-                nc.vector.tensor_tensor(low[:], neg3[u][:], pos2[u][:], ALU.min)
-                nc.vector.tensor_tensor(h[:], high[:], low[:], ALU.subtract)
-                spare = low
+            if KINDS[u] == "D":
+                nc.gpsimd.tensor_tensor(h[:], above[:], lower[u][:], ALU.add)
+                late[u] = above
+                spare[u] = h
             else:
-                bank = turned_sum(pos2[u], neg3[u], long_bank([P, BANK]))
-                if KINDS[u] != "A":
-                    below = scaled_copy("below", bank, ACT.Relu, 1.0)
-                above = scaled_copy("above", turned_sum(pos2[u], neg1[u], upper_bank([P, BANK])), ACT.Relu, -1.0)
+                spare[u] = above
+                nc.vector.scalar_tensor_tensor(h[:], lower[u][:], 0.0, above[:], ALU.max, ALU.add)
                 late[u] = neg1[u]
-                if KINDS[u] == "A":
-                    nc.vector.scalar_tensor_tensor(h[:], bank[:], 0.0, above[:], ALU.max, ALU.add)
-                elif KINDS[u] == "D":
-                    nc.gpsimd.tensor_tensor(h[:], above[:], below[:], ALU.add)
-                    spare, late[u] = below, above
-                else:
-                    nc.scalar.copy(h[:], turned_sum(above, below, long_bank([P, BANK]))[:])
-                    spare, late[u] = below, above
-            return h, spare
+            return h
 
-        damping = keep.tile([P, CHUNKS, PACK, CHUNK], F32, name="damping")
+        damping = keep.tile([P, CHUNKS, PACK, CHUNK], F32, name="damping", tag="tab_w0", align_bytes=64)
 
         def fetch(b, c0, c1, x):
             nc.vector.tensor_copy(x, pages[b][:].indirect(entries(idx3, c0 * CHUNK, c1 * CHUNK)))
@@ -317,27 +320,49 @@ def tile_list_latency_envelopes_kernel(
                 )
 
         fetched = {}
-        for u in range(len(units)):
+        copy_e2(0)
+        low_bank = e3(0, long_bank([P, BANK]))
+        high_bank = e1(0, long_bank([P, BANK]))
+        low = unit_tile("neg3")
+        nc.vector.tensor_tensor(low[:], low_bank[:], pos2[0][:], ALU.min)
+        high = keep.tile([P, BANK], F32, name="high", tag="w1_c1", align_bytes=64)
+        nc.vector.tensor_tensor(high[:], high_bank[:], pos2[0][:], ALU.max)
+        h = unit_tile("h")
+        nc.vector.tensor_tensor(h[:], high[:], low[:], ALU.subtract)
+        quantize_w1(1)
+        open_page()
+        put(0, h[:])
+        negate_e3(1)
+        copy_e2(1)
+        negate_e1(1)
+        last = len(units) - 1
+        for u in range(1, STOP):
             b, half = units[u]
-            if u <= 2:
-                estimates(u)
-            if 2 <= u < len(units) - 1:
-                estimates(u + 1)
-            h, spare = envelope(u)
+            lower_part(u)
+            if 1 < u < last:
+                negate_e3(u + 1)
+            h = upper_part(u)
+            if u == 1:
+                negate_e3(u + 1)
             weigh(u, h[:])
-            if b > 0 and u < len(units) - 1:
-                fetched[u] = (b - 1, 2 * half, 2 * half + 2, spare[:])
+            if b > 0 and u < last:
+                fetched[u] = (b - 1, 2 * half, 2 * half + 2, spare[u][:])
+            if u in fetched and KINDS[u] == "F":
                 fetch(*fetched[u])
             put(u, h[:])
-            if u - 2 in fetched:
-                spread(*fetched[u - 2], late[u])
+            if u in fetched and KINDS[u] == "D":
+                fetch(*fetched[u])
+            if u < last:
+                copy_e2(u + 1)
+                negate_e1(u + 1)
             if u < PAGES - 1:
                 quantize_w1(u + 1)
-            elif u < PAGES - 1 + N // WO_PIECE:
-                round_wo(u - PAGES + 1)
-
-        spread(*fetched[len(units) - 2], unit_tile("neg1"))
-        last_x = keep.tile([P, M], F32, name="last_x")
+            if u - 2 in fetched:
+                spread(*fetched[u - 2], late[u])
+        spread(*fetched[last - 1], lower[last])
+        for k in range(N // WO_PIECE):
+            round_wo(k)
+        last_x = keep.tile([P, M], F32, name="last_x", tag="tab_w1", align_bytes=64)
         late_x = weighted[len(units) - 1]
         for b, c0, c1, x in [
             (PAGES - 1, 0, 1, last_x[:, :CHUNK]),
@@ -353,7 +378,7 @@ def tile_list_latency_envelopes_kernel(
         for k in range(N // WO_PIECE):
             cols = slice(WO_PIECE * k, WO_PIECE * (k + 1))
             nc.vector.quantize_mx(
-                out=wo_c[:, cols].bitcast(FP8X4), scales=wo_s[:, cols], in_=wo_bf[k][:].rearrange("p n i -> p (n i)")
+                out=wo_c[:, cols].bitcast(FP8X4), scales=wo_s[:, cols], in_=wo_bf[k].rearrange("p n i -> p (n i)")
             )
         out_rows = out.rearrange("(i p) m -> p i m", p=P)
         z = {}

@@ -87,11 +87,6 @@ def tile_list_latency_envelopes_kernel(
             nc.gpsimd.memset(page[:].bitcast(I32), 0)
             pages.append(page)
 
-        for q in range(QUADS):
-            nc.gpsimd.dma_start(
-                w3_s[32 * q : 32 * q + PLANE_ROWS, :, :].bitcast(I32),
-                w3_scales.bitcast(I32)[:, PLANE_ROWS * q : PLANE_ROWS * (q + 1), :].rearrange("a r c -> r a c"),
-            )
         open_page()
         open_page()
 
@@ -120,7 +115,7 @@ def tile_list_latency_envelopes_kernel(
                     w3_c[b, a] = words3[:, a, 2 * c0 : 2 * (c0 + P)].bitcast(FP4X4)
 
         def load_packed_planes(tile, scales):
-            for q in range(QUADS):
+            for q in (0, 2, 1, 3):
                 nc.sync.dma_start(
                     tile[32 * q : 32 * q + PASSES * PLANE_ROWS, :].bitcast(I32),
                     scales.bitcast(I32)[:, PLANE_ROWS * q : PLANE_ROWS * (q + 1), :],
@@ -137,6 +132,11 @@ def tile_list_latency_envelopes_kernel(
         load_w1(1, 0, 1)
         load_packed_planes(w2_s, w2_scales)
         load_table_words(1)
+        for row in range(PLANE_ROWS):
+            nc.sync.dma_start(
+                w3_s[row:P:32, :, :].bitcast(I32),
+                w3_scales.bitcast(I32)[:, row : 4 * PLANE_ROWS : PLANE_ROWS, :].rearrange("a q c -> q a c"),
+            )
         v_s = keep.tile([P, S], U8, name="v_s", align_bytes=64)
         nc.vector.tensor_copy(v_s[:], tab_s[:].indirect(idx1[:]))
         plane_span = P - 32 + PLANE_ROWS
@@ -156,8 +156,9 @@ def tile_list_latency_envelopes_kernel(
         nc.sync.dma_start(idx3[:], offs3)
         wo_raw = keep.tile([P, PACK, N], F32, name="wo_raw")
         nc.sync.dma_start(wo_raw[:], wo.rearrange("(p i) n -> p i n", i=PACK))
-        load_sb = keep.tile([P, PACK, M], F32, name="load_sb")
-        nc.sync.dma_start(load_sb[:], load.rearrange("(p i) m -> p i m", i=PACK))
+        load_all = keep.tile([P, PACK, M], F32, name="load_sb")
+        nc.sync.dma_start(load_all[:], load.rearrange("(p i) m -> p i m", i=PACK))
+        load_sb = [load_all[:, :, c * CHUNK : (c + 1) * CHUNK] for c in range(CHUNKS)]
 
         planes = [v_s[:], v_s1[:]]
         ident = keep.tile([P, P], F32, name="ident")
@@ -296,7 +297,10 @@ def tile_list_latency_envelopes_kernel(
 
         def upper_part(u):
             above = scaled_copy("above", turned_sum(neg1[u], pos2[u], upper_bank([P, BANK])), ACT.Relu, -1.0)
-            h = unit_tile("h")
+            if u == len(units) - 1:
+                h = keep.tile([P, BANK], F32, name="h", tag="wo_c0", align_bytes=64)
+            else:
+                h = unit_tile("h")
             if KINDS[u] == "D":
                 nc.gpsimd.tensor_tensor(h[:], above[:], lower[u][:], ALU.add)
                 late[u] = above
@@ -338,12 +342,12 @@ def tile_list_latency_envelopes_kernel(
         last = len(units) - 1
         for u in range(1, STOP):
             b, half = units[u]
+            if u == 1:
+                negate_e3(u + 1)
             lower_part(u)
             if 1 < u < last:
                 negate_e3(u + 1)
             h = upper_part(u)
-            if u == 1:
-                negate_e3(u + 1)
             weigh(u, h[:])
             if b > 0 and u < last:
                 fetched[u] = (b - 1, 2 * half, 2 * half + 2, spare[u][:])
@@ -362,31 +366,39 @@ def tile_list_latency_envelopes_kernel(
         spread(*fetched[last - 1], lower[last])
         for k in range(N // WO_PIECE):
             round_wo(k)
+        wo_c, wo_s = {}, {}
+
+        def quantize_wo(k, codes):
+            wo_c[k] = codes
+            wo_s[k] = keep.tile([P, WO_PIECE], U8, name="wo_s%d" % k, align_bytes=64)
+            nc.vector.quantize_mx(
+                out=wo_c[k].bitcast(FP8X4), scales=wo_s[k][:], in_=wo_bf[k].rearrange("p n i -> p (n i)")
+            )
+
+        wo_first = keep.tile([P, WO_PIECE], U32, name="wo_first", tag="wo_c0", align_bytes=64)
+        quantize_wo(0, wo_first[:])
         last_x = keep.tile([P, M], F32, name="last_x", tag="tab_w1", align_bytes=64)
         late_x = weighted[len(units) - 1]
         for b, c0, c1, x in [
             (PAGES - 1, 0, 1, last_x[:, :CHUNK]),
             (PAGES - 1, 1, 2, last_x[:, CHUNK:BANK]),
-            (PAGES - 1, 2, 4, last_x[:, BANK:]),
             (PAGES - 2, 2, 4, late_x[:]),
+            (PAGES - 1, 2, 4, last_x[:, BANK:]),
         ]:
             fetch(b, c0, c1, x)
             last_e = ring.tile([P, (c1 - c0) * CHUNK], F32, name="last_e", bufs=CHUNKS)
             spread(b, c0, c1, x, last_e)
-        wo_c = keep.tile([P, N], U32, name="wo_c", tag="page2", align_bytes=64)
-        wo_s = keep.tile([P, N], U8, name="wo_s", align_bytes=64)
-        for k in range(N // WO_PIECE):
-            cols = slice(WO_PIECE * k, WO_PIECE * (k + 1))
-            nc.vector.quantize_mx(
-                out=wo_c[:, cols].bitcast(FP8X4), scales=wo_s[:, cols], in_=wo_bf[k].rearrange("p n i -> p (n i)")
-            )
+        wo_rest = keep.tile([P, 2, WO_PIECE], U32, name="wo_rest", tag="page2", align_bytes=64)
+        for k in range(1, N // WO_PIECE):
+            quantize_wo(k, wo_rest[:, k - 1, :])
+
         out_rows = out.rearrange("(i p) m -> p i m", p=P)
         z = {}
 
         def damp(c):
             z[c] = ring.tile([P, CHUNK, PACK], BF16, name="z", align_bytes=64, bufs=3)
             nc.vector.tensor_tensor(
-                woven_out(z[c][:]), woven(damping[:, c, :, :]), woven(load_sb[:, :, c * CHUNK : (c + 1) * CHUNK]),
+                woven_out(z[c][:]), woven(damping[:, c, :, :]), woven(load_sb[c]),
                 ALU.mult,
             )
 
@@ -397,9 +409,9 @@ def tile_list_latency_envelopes_kernel(
             for g in range(N // (2 * P)):
                 acc = (long_bank if g % 2 == 0 else short_bank)([P, 2, CHUNK])
                 for k in range(2):
-                    n0 = (2 * g + k) * P
+                    n0 = k * P
                     nc.tensor.matmul_mx(
-                        out=acc[:, k, :], lhsT=wo_c[:, n0 : n0 + P].bitcast(FP8X4), lhsT_scale=wo_s[:, n0 : n0 + P],
+                        out=acc[:, k, :], lhsT=wo_c[g][:, n0 : n0 + P].bitcast(FP8X4), lhsT_scale=wo_s[g][:, n0 : n0 + P],
                         rhs=z_c[:].bitcast(FP8X4), rhs_scale=z_s[:], start=True, stop=True,
                     )
                 result = ring.tile([P, 2, CHUNK], F32, name="result", bufs=12)

@@ -28,8 +28,9 @@ BANK = 512
 CHUNK = 256
 CHUNKS = M // CHUNK
 WO_PIECE = 256
-KINDS = "EAFDDDDD"
+KINDS = "EEDDDDDD"
 STOP = 8
+LAG = 3
 E_BANKS = 3
 WO_UNIT = 2 * PAGES - N // WO_PIECE
 LONG_BANKS = 4
@@ -63,7 +64,7 @@ def tile_list_latency_envelopes_kernel(
             return psum.tile(shape, F32, name="long_bank", bufs=LONG_BANKS)
 
         def unit_tile(name):
-            return ring.tile([P, BANK], F32, name=name, bufs=3 if name == "pos2" else 4, align_bytes=64)
+            return ring.tile([P, BANK], F32, name=name, bufs={"pos2": 3, "h": 6, "neg1": 3, "neg3": 3, "below": 3}.get(name, 4), align_bytes=64)
 
         idx1 = keep.tile([P, S // STRIPE], U16, name="idx1")
         idx2 = keep.tile([P, S // STRIPE], U16, name="idx2")
@@ -90,7 +91,7 @@ def tile_list_latency_envelopes_kernel(
         open_page()
         open_page()
 
-        tab_w = [keep.tile([P, T], I32, name="tab_w", tag="tab_w%d" % a, align_bytes=64) for a in range(PASSES)]
+        tab_w = [keep.tile([P, T], I32, name="tab_w", tag=("tab_w0", "page3")[a], align_bytes=64) for a in range(PASSES)]
         w1_rows = w1.rearrange("(a p i) c -> a p i c", a=PASSES, i=PACK)
         w2_rows = w2_words.rearrange("a p c i -> p a (c i)")
         w3_rows = w3_words.rearrange("a p c -> p a c")
@@ -176,7 +177,7 @@ def tile_list_latency_envelopes_kernel(
         w1_c, w1_s = {}, {}
 
         def quantize_w1(b):
-            rounded = keep.tile([P, PASSES, P, PACK], BF16, name="w1_bf", tag=("page%d" % (2 + b)) if b < 2 else ("piece%d" % (b - 1)), align_bytes=64)
+            rounded = keep.tile([P, PASSES, P, PACK], BF16, name="w1_bf", tag=("page2", "w1_bf1", "piece1", "piece2")[b], align_bytes=64)
             codes = keep.tile([P, PASSES * P], U32, name="w1_c", tag="w1_c%d" % b, align_bytes=64)
             scales = keep.tile([P, PASSES * P], U8, name="w1_s%d" % b, align_bytes=64)
             for a in range(PASSES):
@@ -197,6 +198,7 @@ def tile_list_latency_envelopes_kernel(
         gather_words(1, 0)
         gather_words(0, 1)
         gather_words(1, 1)
+        open_page()
         open_page()
 
 
@@ -253,19 +255,13 @@ def tile_list_latency_envelopes_kernel(
             return bank
 
         def weigh(u, h):
-            if KINDS[u] in ("D", "F"):
-                weighted[u] = unit_tile("weighted")
-                nc.gpsimd.tensor_tensor(weighted[u][:], h, wgs_sb[units[u][1]][:], ALU.mult)
+            weighted[u] = unit_tile("weighted")
+            nc.gpsimd.tensor_tensor(weighted[u][:], h, wgs_sb[units[u][1]][:], ALU.mult)
 
-        def put(u, h):
+        def put(u):
             b, half = units[u]
-            if KINDS[u] in ("D", "F"):
-                nc.vector.tensor_copy(
-                    pages[b][:].indirect(entries(idx2, half * BANK, (half + 1) * BANK)), weighted[u][:]
-                )
-                return
-            nc.vector.tensor_tensor(
-                pages[b][:].indirect(entries(idx2, half * BANK, (half + 1) * BANK)), h, wgs_sb[half][:], ALU.mult
+            nc.vector.tensor_copy(
+                pages[b][:].indirect(entries(idx2, half * BANK, (half + 1) * BANK)), weighted[u][:]
             )
 
         def scaled_copy(name, bank, func, scale):
@@ -324,26 +320,35 @@ def tile_list_latency_envelopes_kernel(
                 )
 
         fetched = {}
-        copy_e2(0)
-        low_bank = e3(0, long_bank([P, BANK]))
-        high_bank = e1(0, long_bank([P, BANK]))
-        low = unit_tile("neg3")
-        nc.vector.tensor_tensor(low[:], low_bank[:], pos2[0][:], ALU.min)
-        high = keep.tile([P, BANK], F32, name="high", tag="w1_c1", align_bytes=64)
-        nc.vector.tensor_tensor(high[:], high_bank[:], pos2[0][:], ALU.max)
+        banks = {}
+        for u in range(2):
+            copy_e2(u)
+            banks[u] = (e3(u, long_bank([P, BANK])), e1(u, long_bank([P, BANK])))
+
+        def bounds(u, high):
+            low = unit_tile("neg3")
+            nc.vector.tensor_tensor(low[:], banks[u][0][:], pos2[u][:], ALU.min)
+            nc.vector.tensor_tensor(high[:], banks[u][1][:], pos2[u][:], ALU.max)
+            return high, low
+
+        high, low = bounds(0, keep.tile([P, BANK], F32, name="high", tag="w1_c1", align_bytes=64))
         h = unit_tile("h")
         nc.vector.tensor_tensor(h[:], high[:], low[:], ALU.subtract)
         quantize_w1(1)
-        open_page()
-        put(0, h[:])
-        negate_e3(1)
-        copy_e2(1)
-        negate_e1(1)
+        weighted[0] = unit_tile("weighted")
+        nc.vector.tensor_tensor(weighted[0][:], h[:], wgs_sb[0][:], ALU.mult)
+        high, low = bounds(1, unit_tile("neg1"))
+        put(0)
+        nc.gpsimd.tensor_tensor(h[:], high[:], low[:], ALU.subtract)
+        weigh(1, h[:])
+        put(1)
+        negate_e3(2)
+        copy_e2(2)
+        negate_e1(2)
+        quantize_w1(2)
         last = len(units) - 1
-        for u in range(1, STOP):
+        for u in range(2, STOP):
             b, half = units[u]
-            if u == 1:
-                negate_e3(u + 1)
             lower_part(u)
             if 1 < u < last:
                 negate_e3(u + 1)
@@ -353,17 +358,18 @@ def tile_list_latency_envelopes_kernel(
                 fetched[u] = (b - 1, 2 * half, 2 * half + 2, spare[u][:])
             if u in fetched and KINDS[u] == "F":
                 fetch(*fetched[u])
-            put(u, h[:])
+            put(u)
             if u in fetched and KINDS[u] == "D":
                 fetch(*fetched[u])
             if u < last:
                 copy_e2(u + 1)
                 negate_e1(u + 1)
-            if u < PAGES - 1:
-                quantize_w1(u + 1)
-            if u - 2 in fetched:
-                spread(*fetched[u - 2], late[u])
-        spread(*fetched[last - 1], lower[last])
+            if u == 2:
+                quantize_w1(3)
+            if u - LAG in fetched:
+                spread(*fetched[u - LAG], late[u])
+        spread(*fetched[last - 2], lower[last])
+        spread(*fetched[last - 1], spare[last - 2])
         for k in range(N // WO_PIECE):
             round_wo(k)
         wo_c, wo_s = {}, {}
@@ -377,7 +383,7 @@ def tile_list_latency_envelopes_kernel(
 
         wo_first = keep.tile([P, WO_PIECE], U32, name="wo_first", tag="wo_c0", align_bytes=64)
         quantize_wo(0, wo_first[:])
-        last_x = keep.tile([P, M], F32, name="last_x", tag="tab_w1", align_bytes=64)
+        last_x = keep.tile([P, M], F32, name="last_x")
         late_x = weighted[len(units) - 1]
         for b, c0, c1, x in [
             (PAGES - 1, 0, 1, last_x[:, :CHUNK]),

@@ -28,9 +28,9 @@ BANK = 512
 CHUNK = 256
 CHUNKS = M // CHUNK
 WO_PIECE = 256
-KINDS = "EEDDDDDD"
+KINDS = "EEBBBBBB"
 STOP = 8
-LAG = 3
+LAG = 2
 E_BANKS = 3
 WO_UNIT = 2 * PAGES - N // WO_PIECE
 LONG_BANKS = 4
@@ -64,7 +64,7 @@ def tile_list_latency_envelopes_kernel(
             return psum.tile(shape, F32, name="long_bank", bufs=LONG_BANKS)
 
         def unit_tile(name):
-            return ring.tile([P, BANK], F32, name=name, bufs={"pos2": 3, "h": 6, "neg1": 3, "neg3": 3, "below": 3}.get(name, 4), align_bytes=64)
+            return ring.tile([P, BANK], F32, name=name, bufs={"pos2": 3, "h": 4, "neg1": 3, "neg3": 3, "below": 5}.get(name, 4), align_bytes=64)
 
         idx1 = keep.tile([P, S // STRIPE], U16, name="idx1")
         idx2 = keep.tile([P, S // STRIPE], U16, name="idx2")
@@ -81,15 +81,13 @@ def tile_list_latency_envelopes_kernel(
         nc.gpsimd.memset(w2_s[:].bitcast(I32), 0)
         nc.gpsimd.memset(w3_s[:].rearrange("p a c -> p (a c)").bitcast(I32), 0)
         nc.gpsimd.memset(v_s1[:].bitcast(I32), 0)
-        pages = []
+        pages = {}
 
-        def open_page():
-            page = keep.tile([P, T2], F32, name="page", tag="page%d" % len(pages), align_bytes=64)
-            nc.gpsimd.memset(page[:].bitcast(I32), 0)
-            pages.append(page)
+        def open_page(b):
+            pages[b] = keep.tile([P, T2], F32, name="page", tag="page%d" % b, align_bytes=64)
+            nc.gpsimd.memset(pages[b][:].bitcast(I32), 0)
 
-        open_page()
-        open_page()
+        open_page(0)
 
         tab_w = [keep.tile([P, T], I32, name="tab_w", tag=("tab_w0", "page3")[a], align_bytes=64) for a in range(PASSES)]
         w1_rows = w1.rearrange("(a p i) c -> a p i c", a=PASSES, i=PACK)
@@ -177,7 +175,7 @@ def tile_list_latency_envelopes_kernel(
         w1_c, w1_s = {}, {}
 
         def quantize_w1(b):
-            rounded = keep.tile([P, PASSES, P, PACK], BF16, name="w1_bf", tag=("page2", "w1_bf1", "piece1", "piece2")[b], align_bytes=64)
+            rounded = keep.tile([P, PASSES, P, PACK], BF16, name="w1_bf", tag=("w1_bf0", "page1", "piece1", "piece2")[b], align_bytes=64)
             codes = keep.tile([P, PASSES * P], U32, name="w1_c", tag="w1_c%d" % b, align_bytes=64)
             scales = keep.tile([P, PASSES * P], U8, name="w1_s%d" % b, align_bytes=64)
             for a in range(PASSES):
@@ -198,16 +196,14 @@ def tile_list_latency_envelopes_kernel(
         gather_words(1, 0)
         gather_words(0, 1)
         gather_words(1, 1)
-        open_page()
-        open_page()
+        open_page(3)
 
 
         pos2, neg1, neg3, late = {}, {}, {}, {}
         wo_bf = {}
 
         def round_wo(k):
-            place = (neg3, neg1, pos2)[k][2 * PAGES - 1]
-            wo_bf[k] = place[:].bitcast(BF16).rearrange("p (n i) -> p n i", i=PACK)
+            wo_bf[k] = wo_all[:, WO_PIECE * k : WO_PIECE * (k + 1), :]
             nc.scalar.copy(out=woven_out(wo_bf[k]), in_=woven(wo_raw[:, :, WO_PIECE * k : WO_PIECE * (k + 1)]))
 
         units = [(b, half) for b in range(PAGES) for half in range(2)]
@@ -216,7 +212,7 @@ def tile_list_latency_envelopes_kernel(
             b, half = units[u]
             j0 = half * BANK
             for a in range(PASSES):
-                if KINDS[u] in ("E", "B"):
+                if True:
                     nc.tensor.matmul_mx(
                         out=bank[:], lhsT=codes[b, a], lhsT_scale=scales[a],
                         rhs=v_w[a, half][:].bitcast(FP8X4), rhs_scale=planes[a][:, j0 : j0 + BANK],
@@ -254,14 +250,10 @@ def tile_list_latency_envelopes_kernel(
                                  start=False, stop=True, is_transpose=True)
             return bank
 
-        def weigh(u, h):
-            weighted[u] = unit_tile("weighted")
-            nc.gpsimd.tensor_tensor(weighted[u][:], h, wgs_sb[units[u][1]][:], ALU.mult)
-
-        def put(u):
+        def put(u, h):
             b, half = units[u]
-            nc.vector.tensor_copy(
-                pages[b][:].indirect(entries(idx2, half * BANK, (half + 1) * BANK)), weighted[u][:]
+            nc.vector.tensor_tensor(
+                pages[b][:].indirect(entries(idx2, half * BANK, (half + 1) * BANK)), h[:], wgs_sb[half][:], ALU.mult
             )
 
         def scaled_copy(name, bank, func, scale):
@@ -284,27 +276,20 @@ def tile_list_latency_envelopes_kernel(
         def negate_e3(u):
             neg3[u] = scaled_copy("neg3", e3(u, short_bank([P, BANK])), ACT.Copy, -1.0)
 
-        lower, spare = {}, {}
+        below, above = {}, {}
 
         def lower_part(u):
-            lower[u] = turned_sum(pos2[u], neg3[u], long_bank([P, BANK]))
-            if KINDS[u] == "D":
-                lower[u] = scaled_copy("below", lower[u], ACT.Relu, 1.0)
+            place = "below"
+            if u == len(units) - 2:
+                place = keep.tile([P, BANK], F32, name="below", tag="wo_bf", align_bytes=64)
+            below[u] = scaled_copy(place, turned_sum(pos2[u], neg3[u], long_bank([P, BANK])), ACT.Relu, 1.0)
 
         def upper_part(u):
-            above = scaled_copy("above", turned_sum(neg1[u], pos2[u], upper_bank([P, BANK])), ACT.Relu, -1.0)
-            if u == len(units) - 1:
-                h = keep.tile([P, BANK], F32, name="h", tag="wo_c0", align_bytes=64)
-            else:
-                h = unit_tile("h")
-            if KINDS[u] == "D":
-                nc.gpsimd.tensor_tensor(h[:], above[:], lower[u][:], ALU.add)
-                late[u] = above
-                spare[u] = h
-            else:
-                spare[u] = above
-                nc.vector.scalar_tensor_tensor(h[:], lower[u][:], 0.0, above[:], ALU.max, ALU.add)
-                late[u] = neg1[u]
+            above[u] = scaled_copy("above", turned_sum(neg1[u], pos2[u], upper_bank([P, BANK])), ACT.Relu, -1.0)
+
+        def envelope(u):
+            h = unit_tile("h")
+            nc.scalar.copy(h[:], turned_sum(below[u], above[u], long_bank([P, BANK]))[:])
             return h
 
         damping = keep.tile([P, CHUNKS, PACK, CHUNK], F32, name="damping", tag="tab_w0", align_bytes=64)
@@ -334,44 +319,43 @@ def tile_list_latency_envelopes_kernel(
         high, low = bounds(0, keep.tile([P, BANK], F32, name="high", tag="w1_c1", align_bytes=64))
         h = unit_tile("h")
         nc.vector.tensor_tensor(h[:], high[:], low[:], ALU.subtract)
+        high, low = bounds(1, keep.tile([P, BANK], F32, name="high", tag="page2", align_bytes=64))
         quantize_w1(1)
-        weighted[0] = unit_tile("weighted")
-        nc.vector.tensor_tensor(weighted[0][:], h[:], wgs_sb[0][:], ALU.mult)
-        high, low = bounds(1, unit_tile("neg1"))
-        put(0)
-        nc.gpsimd.tensor_tensor(h[:], high[:], low[:], ALU.subtract)
-        weigh(1, h[:])
-        put(1)
+        open_page(1)
+        put(0, h)
+        h = unit_tile("h")
+        nc.vector.tensor_tensor(h[:], high[:], low[:], ALU.subtract)
+        open_page(2)
         negate_e3(2)
         copy_e2(2)
         negate_e1(2)
         quantize_w1(2)
+        put(1, h)
         last = len(units) - 1
-        for u in range(2, STOP):
-            b, half = units[u]
+        for u in range(2, last + 1):
             lower_part(u)
-            if 1 < u < last:
+            if u < last:
                 negate_e3(u + 1)
-            h = upper_part(u)
-            weigh(u, h[:])
-            if b > 0 and u < last:
-                fetched[u] = (b - 1, 2 * half, 2 * half + 2, spare[u][:])
-            if u in fetched and KINDS[u] == "F":
-                fetch(*fetched[u])
-            put(u)
-            if u in fetched and KINDS[u] == "D":
-                fetch(*fetched[u])
+            upper_part(u)
             if u < last:
                 copy_e2(u + 1)
+            h = envelope(u)
+            if u > 2:
+                b, half = units[u - 3]
+                fetched[u] = (b, 2 * half, 2 * half + 2, below[u][:])
+                fetch(*fetched[u])
+            put(u, h)
+            if u < last:
                 negate_e1(u + 1)
             if u == 2:
                 quantize_w1(3)
             if u - LAG in fetched:
-                spread(*fetched[u - LAG], late[u])
-        spread(*fetched[last - 2], lower[last])
-        spread(*fetched[last - 1], spare[last - 2])
+                spread(*fetched[u - LAG], above[u])
+        spread(*fetched[last - 1], below[last - 2])
+        wo_all = keep.tile([P, N, PACK], BF16, name="wo_all", tag="wo_bf", align_bytes=64)
         for k in range(N // WO_PIECE):
             round_wo(k)
+        spread(*fetched[last], unit_tile("neg1"))
         wo_c, wo_s = {}, {}
 
         def quantize_wo(k, codes):
@@ -381,10 +365,8 @@ def tile_list_latency_envelopes_kernel(
                 out=wo_c[k].bitcast(FP8X4), scales=wo_s[k][:], in_=wo_bf[k].rearrange("p n i -> p (n i)")
             )
 
-        wo_first = keep.tile([P, WO_PIECE], U32, name="wo_first", tag="wo_c0", align_bytes=64)
-        quantize_wo(0, wo_first[:])
         last_x = keep.tile([P, M], F32, name="last_x")
-        late_x = weighted[len(units) - 1]
+        late_x = h
         for b, c0, c1, x in [
             (PAGES - 1, 0, 1, last_x[:, :CHUNK]),
             (PAGES - 1, 1, 2, last_x[:, CHUNK:BANK]),
@@ -394,9 +376,9 @@ def tile_list_latency_envelopes_kernel(
             fetch(b, c0, c1, x)
             last_e = ring.tile([P, (c1 - c0) * CHUNK], F32, name="last_e", bufs=CHUNKS)
             spread(b, c0, c1, x, last_e)
-        wo_rest = keep.tile([P, 2, WO_PIECE], U32, name="wo_rest", tag="page2", align_bytes=64)
-        for k in range(1, N // WO_PIECE):
-            quantize_wo(k, wo_rest[:, k - 1, :])
+        wo_rest = keep.tile([P, N // WO_PIECE, WO_PIECE], U32, name="wo_rest", tag="page2", align_bytes=64)
+        for k in range(N // WO_PIECE):
+            quantize_wo(k, wo_rest[:, k, :])
 
         out_rows = out.rearrange("(i p) m -> p i m", p=P)
         z = {}

@@ -31,6 +31,7 @@ WO_PIECE = 256
 KINDS = "EEBBBBBB"
 STOP = 8
 LAG = 2
+WO_CAST = 64
 E_BANKS = 3
 WO_UNIT = 2 * PAGES - N // WO_PIECE
 LONG_BANKS = 4
@@ -179,7 +180,11 @@ def tile_list_latency_envelopes_kernel(
             codes = keep.tile([P, PASSES * P], U32, name="w1_c", tag="w1_c%d" % b, align_bytes=64)
             scales = keep.tile([P, PASSES * P], U8, name="w1_s%d" % b, align_bytes=64)
             for a in range(PASSES):
-                nc.scalar.copy(out=woven_out(rounded[:, a, :, :]), in_=woven(w1_raw[b, a]))
+                step = P if b < 2 else P // 2
+                for c0 in range(0, P, step):
+                    nc.scalar.copy(
+                        out=woven_out(rounded[:, a, c0 : c0 + step, :]), in_=woven(w1_raw[b, a][:, :, c0 : c0 + step])
+                    )
                 w1_c[b, a] = codes[:, a * P : (a + 1) * P].bitcast(FP8X4)
                 w1_s[b, a] = scales[:, a * P : (a + 1) * P]
                 if b == 0:
@@ -263,8 +268,10 @@ def tile_list_latency_envelopes_kernel(
 
 
         def pos2_place(u):
-            if 0 < u < PAGES - 1:
-                return keep.tile([P, BANK], F32, name="pos2", tag="piece%d" % u, align_bytes=64)
+            if u == 0:
+                return keep.tile([P, BANK], F32, name="pos2", tag="w1_c1", align_bytes=64)
+            if u == len(units) - 1:
+                return keep.tile([P, BANK], F32, name="pos2", tag="wo_all", align_bytes=64)
             return "pos2"
 
         def copy_e2(u):
@@ -279,17 +286,14 @@ def tile_list_latency_envelopes_kernel(
         below, above = {}, {}
 
         def lower_part(u):
-            place = "below"
-            if u == len(units) - 2:
-                place = keep.tile([P, BANK], F32, name="below", tag="wo_bf", align_bytes=64)
-            below[u] = scaled_copy(place, turned_sum(pos2[u], neg3[u], long_bank([P, BANK])), ACT.Relu, 1.0)
+            below[u] = scaled_copy("below", turned_sum(pos2[u], neg3[u], long_bank([P, BANK])), ACT.Relu, 1.0)
 
         def upper_part(u):
             above[u] = scaled_copy("above", turned_sum(neg1[u], pos2[u], upper_bank([P, BANK])), ACT.Relu, -1.0)
 
         def envelope(u):
             h = unit_tile("h")
-            nc.scalar.copy(h[:], turned_sum(below[u], above[u], long_bank([P, BANK]))[:])
+            nc.scalar.copy(h[:], turned_sum(above[u], below[u], long_bank([P, BANK]))[:])
             return h
 
         damping = keep.tile([P, CHUNKS, PACK, CHUNK], F32, name="damping", tag="tab_w0", align_bytes=64)
@@ -316,11 +320,11 @@ def tile_list_latency_envelopes_kernel(
             nc.vector.tensor_tensor(high[:], banks[u][1][:], pos2[u][:], ALU.max)
             return high, low
 
-        high, low = bounds(0, keep.tile([P, BANK], F32, name="high", tag="w1_c1", align_bytes=64))
+        high, low = bounds(0, unit_tile("neg1"))
+        quantize_w1(1)
         h = unit_tile("h")
         nc.vector.tensor_tensor(h[:], high[:], low[:], ALU.subtract)
         high, low = bounds(1, keep.tile([P, BANK], F32, name="high", tag="page2", align_bytes=64))
-        quantize_w1(1)
         open_page(1)
         put(0, h)
         h = unit_tile("h")
@@ -329,7 +333,6 @@ def tile_list_latency_envelopes_kernel(
         negate_e3(2)
         copy_e2(2)
         negate_e1(2)
-        quantize_w1(2)
         put(1, h)
         last = len(units) - 1
         for u in range(2, last + 1):
@@ -339,23 +342,24 @@ def tile_list_latency_envelopes_kernel(
             upper_part(u)
             if u < last:
                 copy_e2(u + 1)
+                if u % 2 == 1:
+                    quantize_w1(units[u + 1][0])
+                negate_e1(u + 1)
             h = envelope(u)
             if u > 2:
                 b, half = units[u - 3]
                 fetched[u] = (b, 2 * half, 2 * half + 2, below[u][:])
                 fetch(*fetched[u])
             put(u, h)
-            if u < last:
-                negate_e1(u + 1)
-            if u == 2:
-                quantize_w1(3)
             if u - LAG in fetched:
                 spread(*fetched[u - LAG], above[u])
         spread(*fetched[last - 1], below[last - 2])
-        wo_all = keep.tile([P, N, PACK], BF16, name="wo_all", tag="wo_bf", align_bytes=64)
-        for k in range(N // WO_PIECE):
-            round_wo(k)
+        wo_all = keep.tile([P, N, PACK], BF16, name="wo_all", tag="wo_all", align_bytes=64)
+        for n0 in range(0, N, WO_CAST):
+            nc.scalar.copy(out=woven_out(wo_all[:, n0 : n0 + WO_CAST, :]), in_=woven(wo_raw[:, :, n0 : n0 + WO_CAST]))
         spread(*fetched[last], unit_tile("neg1"))
+        for k in range(N // WO_PIECE):
+            wo_bf[k] = wo_all[:, WO_PIECE * k : WO_PIECE * (k + 1), :]
         wo_c, wo_s = {}, {}
 
         def quantize_wo(k, codes):
@@ -376,15 +380,18 @@ def tile_list_latency_envelopes_kernel(
             fetch(b, c0, c1, x)
             last_e = ring.tile([P, (c1 - c0) * CHUNK], F32, name="last_e", bufs=CHUNKS)
             spread(b, c0, c1, x, last_e)
-        wo_rest = keep.tile([P, N // WO_PIECE, WO_PIECE], U32, name="wo_rest", tag="page2", align_bytes=64)
-        for k in range(N // WO_PIECE):
+        wo_rest = keep.tile([P, 2, WO_PIECE], U32, name="wo_rest", tag="page2", align_bytes=64)
+        for k in range(2):
             quantize_wo(k, wo_rest[:, k, :])
 
         out_rows = out.rearrange("(i p) m -> p i m", p=P)
         z = {}
 
         def damp(c):
-            z[c] = ring.tile([P, CHUNK, PACK], BF16, name="z", align_bytes=64, bufs=3)
+            if c == 0:
+                z[c] = keep.tile([P, CHUNK, PACK], BF16, name="z", tag="wo_last", align_bytes=64)
+            else:
+                z[c] = ring.tile([P, CHUNK, PACK], BF16, name="z", align_bytes=64, bufs=1)
             nc.vector.tensor_tensor(
                 woven_out(z[c][:]), woven(damping[:, c, :, :]), woven(load_sb[c]),
                 ALU.mult,
@@ -394,6 +401,9 @@ def tile_list_latency_envelopes_kernel(
             z_c = ring.tile([P, CHUNK], U32, name="z_c", align_bytes=64)
             z_s = ring.tile([P, CHUNK], U8, name="z_s", align_bytes=64)
             nc.vector.quantize_mx(out=z_c[:].bitcast(FP8X4), scales=z_s[:], in_=z[c][:].rearrange("p m i -> p (m i)"))
+            if c == 0:
+                wo_last = keep.tile([P, WO_PIECE], U32, name="wo_last", tag="wo_last", align_bytes=64)
+                quantize_wo(2, wo_last[:])
             for g in range(N // (2 * P)):
                 acc = (long_bank if g % 2 == 0 else short_bank)([P, 2, CHUNK])
                 for k in range(2):
@@ -403,7 +413,7 @@ def tile_list_latency_envelopes_kernel(
                         rhs=z_c[:].bitcast(FP8X4), rhs_scale=z_s[:], start=True, stop=True,
                     )
                 result = ring.tile([P, 2, CHUNK], F32, name="result", bufs=12)
-                copy_out = nc.vector.tensor_copy if (c, g) in ((CHUNKS - 2, 2), (CHUNKS - 1, 1)) else nc.scalar.copy
+                copy_out = nc.vector.tensor_copy if c == CHUNKS - 1 and g == 1 else nc.scalar.copy
                 copy_out(result[:], acc[:])
                 nc.sync.dma_start(out_rows[:, 2 * g : 2 * (g + 1), c * CHUNK : (c + 1) * CHUNK], result[:])
 

@@ -102,17 +102,23 @@ def tile_list_latency_envelopes_kernel(
             for b in range(b0, b1):
                 w1_raw[b, a] = raw[:, :, (b - b0) * P : (b - b0 + 1) * P]
 
-        def load_packed(b0, b1):
-            width = (b1 - b0) * P
-            words2 = keep.tile([P, PASSES, width], U32, name="w2_c%d" % b0, align_bytes=64)
-            nc.sync.dma_start(words2[:].bitcast(I32), w2_rows[:, :, 4 * b0 * P : 4 * b1 * P].bitcast(I32))
-            words3 = keep.tile([P, PASSES, 2 * width], U8, name="w3_c%d" % b0, align_bytes=64)
-            nc.sync.dma_start(words3[:].bitcast(I32), w3_rows[:, :, 2 * b0 * P : 2 * b1 * P].bitcast(I32))
+        def load_w2(b0, b1):
+            words = keep.tile([P, PASSES, (b1 - b0) * P], U32, name="w2_c", tag="page1" if b0 == 0 else "w2_c%d" % b0, align_bytes=64)
+            nc.sync.dma_start(words[:].bitcast(I32), w2_rows[:, :, 4 * b0 * P : 4 * b1 * P].bitcast(I32))
             for b in range(b0, b1):
-                c0 = (b - b0) * P
                 for a in range(PASSES):
-                    w2_c[b, a] = words2[:, a, c0 : c0 + P].bitcast(FP8X4)
-                    w3_c[b, a] = words3[:, a, 2 * c0 : 2 * (c0 + P)].bitcast(FP4X4)
+                    w2_c[b, a] = words[:, a, (b - b0) * P : (b - b0 + 1) * P].bitcast(FP8X4)
+
+        def load_w3(b0, b1):
+            words = keep.tile([P, PASSES, 2 * (b1 - b0) * P], U8, name="w3_c%d" % b0, align_bytes=64)
+            nc.sync.dma_start(words[:].bitcast(I32), w3_rows[:, :, 2 * b0 * P : 2 * b1 * P].bitcast(I32))
+            for b in range(b0, b1):
+                for a in range(PASSES):
+                    w3_c[b, a] = words[:, a, 2 * (b - b0) * P : 2 * (b - b0 + 1) * P].bitcast(FP4X4)
+
+        def load_packed(b0, b1):
+            load_w2(b0, b1)
+            load_w3(b0, b1)
 
         def load_packed_planes(tile, scales):
             for q in (0, 2, 1, 3):
@@ -128,10 +134,10 @@ def tile_list_latency_envelopes_kernel(
         load_packed_planes(tab_s, tab_scales)
         load_packed(0, 1)
         load_table_words(0)
-        load_w1(0, 0, 1)
-        load_w1(1, 0, 1)
         load_packed_planes(w2_s, w2_scales)
+        load_w1(0, 0, 1)
         load_table_words(1)
+        load_w1(1, 0, 1)
         for row in range(PLANE_ROWS):
             nc.sync.dma_start(
                 w3_s[row:P:32, :, :].bitcast(I32),
@@ -207,10 +213,6 @@ def tile_list_latency_envelopes_kernel(
         pos2, neg1, neg3, late = {}, {}, {}, {}
         wo_bf = {}
 
-        def round_wo(k):
-            wo_bf[k] = wo_all[:, WO_PIECE * k : WO_PIECE * (k + 1), :]
-            nc.scalar.copy(out=woven_out(wo_bf[k]), in_=woven(wo_raw[:, :, WO_PIECE * k : WO_PIECE * (k + 1)]))
-
         units = [(b, half) for b in range(PAGES) for half in range(2)]
 
         def estimate(u, bank, codes, scales):
@@ -275,7 +277,7 @@ def tile_list_latency_envelopes_kernel(
             return "pos2"
 
         def copy_e2(u):
-            pos2[u] = scaled_copy(pos2_place(u), e2(u, short_bank([P, BANK])), ACT.Copy, 1.0)
+            pos2[u] = scaled_copy(pos2_place(u), e2(u, (upper_bank if u == 0 else short_bank)([P, BANK])), ACT.Copy, 1.0)
 
         def negate_e1(u):
             neg1[u] = scaled_copy("neg1", e1(u, short_bank([P, BANK])), ACT.Copy, -1.0)
@@ -312,12 +314,13 @@ def tile_list_latency_envelopes_kernel(
         banks = {}
         for u in range(2):
             copy_e2(u)
-            banks[u] = (e3(u, long_bank([P, BANK])), e1(u, long_bank([P, BANK])))
+            low_bank = e3(u, (long_bank if u == 0 else upper_bank)([P, BANK]))
+            banks[u] = (e1(u, (short_bank if u == 0 else long_bank)([P, BANK])), low_bank)
 
         def bounds(u, high):
             low = unit_tile("neg3")
-            nc.vector.tensor_tensor(low[:], banks[u][0][:], pos2[u][:], ALU.min)
-            nc.vector.tensor_tensor(high[:], banks[u][1][:], pos2[u][:], ALU.max)
+            nc.vector.tensor_tensor(low[:], banks[u][1][:], pos2[u][:], ALU.min)
+            nc.vector.tensor_tensor(high[:], banks[u][0][:], pos2[u][:], ALU.max)
             return high, low
 
         high, low = bounds(0, unit_tile("neg1"))
@@ -385,38 +388,45 @@ def tile_list_latency_envelopes_kernel(
             quantize_wo(k, wo_rest[:, k, :])
 
         out_rows = out.rearrange("(i p) m -> p i m", p=P)
-        z = {}
 
-        def damp(c):
-            if c == 0:
-                z[c] = keep.tile([P, CHUNK, PACK], BF16, name="z", tag="wo_last", align_bytes=64)
-            else:
-                z[c] = ring.tile([P, CHUNK, PACK], BF16, name="z", align_bytes=64, bufs=1)
+        def damp(c, m0, m1, z):
             nc.vector.tensor_tensor(
-                woven_out(z[c][:]), woven(damping[:, c, :, :]), woven(load_sb[c]),
-                ALU.mult,
+                woven_out(z[:]), woven(damping[:, c, :, m0:m1]), woven(load_sb[c][:, :, m0:m1]), ALU.mult
             )
 
-        def project(c):
-            z_c = ring.tile([P, CHUNK], U32, name="z_c", align_bytes=64)
-            z_s = ring.tile([P, CHUNK], U8, name="z_s", align_bytes=64)
-            nc.vector.quantize_mx(out=z_c[:].bitcast(FP8X4), scales=z_s[:], in_=z[c][:].rearrange("p m i -> p (m i)"))
-            if c == 0:
-                wo_last = keep.tile([P, WO_PIECE], U32, name="wo_last", tag="wo_last", align_bytes=64)
-                quantize_wo(2, wo_last[:])
-            for g in range(N // (2 * P)):
-                acc = (long_bank if g % 2 == 0 else short_bank)([P, 2, CHUNK])
-                for k in range(2):
-                    n0 = k * P
-                    nc.tensor.matmul_mx(
-                        out=acc[:, k, :], lhsT=wo_c[g][:, n0 : n0 + P].bitcast(FP8X4), lhsT_scale=wo_s[g][:, n0 : n0 + P],
-                        rhs=z_c[:].bitcast(FP8X4), rhs_scale=z_s[:], start=True, stop=True,
-                    )
-                result = ring.tile([P, 2, CHUNK], F32, name="result", bufs=12)
-                copy_out = nc.vector.tensor_copy if c == CHUNKS - 1 and g == 1 else nc.scalar.copy
-                copy_out(result[:], acc[:])
-                nc.sync.dma_start(out_rows[:, 2 * g : 2 * (g + 1), c * CHUNK : (c + 1) * CHUNK], result[:])
+        def quantize_z(z, width):
+            z_c = ring.tile([P, width], U32, name="z_c", align_bytes=64, bufs=3)
+            z_s = ring.tile([P, width], U8, name="z_s", align_bytes=64, bufs=3)
+            nc.vector.quantize_mx(out=z_c[:].bitcast(FP8X4), scales=z_s[:], in_=z[:].rearrange("p m i -> p (m i)"))
+            return z_c, z_s
 
-        for c in range(CHUNKS):
-            damp(c)
-            project(c)
+        def project(z_q, m0, width, t0, t1, bank, copy_out):
+            acc = bank([P, t1 - t0, width])
+            for t in range(t0, t1):
+                k, n0 = divmod(t * P, WO_PIECE)
+                nc.tensor.matmul_mx(
+                    out=acc[:, t - t0, :], lhsT=wo_c[k][:, n0 : n0 + P].bitcast(FP8X4), lhsT_scale=wo_s[k][:, n0 : n0 + P],
+                    rhs=z_q[0][:].bitcast(FP8X4), rhs_scale=z_q[1][:], start=True, stop=True,
+                )
+            result = ring.tile([P, t1 - t0, width], F32, name="result", bufs=12)
+            copy_out(result[:], acc[:])
+            nc.sync.dma_start(out_rows[:, t0:t1, m0 : m0 + width], result[:])
+
+        halves = [
+            keep.tile([P, P, PACK], BF16, name="z_half", tag=("z_half", "wo_last")[k], align_bytes=64) for k in range(2)
+        ]
+        for k in range(2):
+            damp(0, k * P, (k + 1) * P, halves[k])
+        first = [quantize_z(halves[k], P) for k in range(2)]
+        wo_last = keep.tile([P, WO_PIECE], U32, name="wo_last", tag="wo_last", align_bytes=64)
+        quantize_wo(2, wo_last[:])
+        for t0 in (0, 3):
+            for k in range(2):
+                project(first[k], k * P, P, t0, t0 + 3, (long_bank, short_bank)[k], nc.scalar.copy)
+        for c in range(1, CHUNKS):
+            z = ring.tile([P, CHUNK, PACK], BF16, name="z", align_bytes=64, bufs=1)
+            damp(c, 0, CHUNK, z)
+            z_q = quantize_z(z, CHUNK)
+            for g in range(N // (2 * P)):
+                copy_out = nc.vector.tensor_copy if c == CHUNKS - 1 and g == 1 else nc.scalar.copy
+                project(z_q, c * CHUNK, CHUNK, 2 * g, 2 * g + 2, long_bank if g % 2 == 0 else short_bank, copy_out)

@@ -35,6 +35,8 @@ WO_CAST = 64
 E_BANKS = 3
 WO_UNIT = 2 * PAGES - N // WO_PIECE
 LONG_BANKS = 4
+Z_TAGS = ("z0", "wo_all", "page3", "z3", "z4")
+PIECES = [(0, 128), (128, 256), (256, 512), (512, 768), (768, 1024)]
 
 
 def woven(planes):
@@ -76,10 +78,10 @@ def tile_list_latency_envelopes_kernel(
 
         tab_s = keep.tile([P, T], U8, name="tab_s", align_bytes=64)
         v_s1 = keep.tile([P, S], U8, name="v_s1", align_bytes=64)
-        w2_s = keep.tile([P, H], U8, name="w2_s", align_bytes=64)
+        w2_s = keep.tile([P, PASSES, H], U8, name="w2_s", align_bytes=64)
         w3_s = keep.tile([P, PASSES, H], U8, name="w3_s", align_bytes=64)
         nc.gpsimd.memset(tab_s[:].bitcast(I32), 0)
-        nc.gpsimd.memset(w2_s[:].bitcast(I32), 0)
+        nc.gpsimd.memset(w2_s[:].rearrange("p a c -> p (a c)").bitcast(I32), 0)
         nc.gpsimd.memset(w3_s[:].rearrange("p a c -> p (a c)").bitcast(I32), 0)
         nc.gpsimd.memset(v_s1[:].bitcast(I32), 0)
         pages = {}
@@ -90,7 +92,7 @@ def tile_list_latency_envelopes_kernel(
 
         open_page(0)
 
-        tab_w = [keep.tile([P, T], I32, name="tab_w", tag=("tab_w0", "page3")[a], align_bytes=64) for a in range(PASSES)]
+        tab_w = [keep.tile([P, T], I32, name="tab_w", tag="tab_w%d" % a, align_bytes=64) for a in range(PASSES)]
         w1_rows = w1.rearrange("(a p i) c -> a p i c", a=PASSES, i=PACK)
         w2_rows = w2_words.rearrange("a p c i -> p a (c i)")
         w3_rows = w3_words.rearrange("a p c -> p a c")
@@ -130,19 +132,23 @@ def tile_list_latency_envelopes_kernel(
         def load_table_words(a):
             nc.sync.dma_start(tab_w[a][:], tab_words[a].rearrange("p t i -> p (t i)").bitcast(I32))
 
+        def load_planes_by_row(tile, scales):
+            for row in range(PLANE_ROWS):
+                nc.sync.dma_start(
+                    tile[row:P:32, :, :].bitcast(I32),
+                    scales.bitcast(I32)[:, row : 4 * PLANE_ROWS : PLANE_ROWS, :].rearrange("a q c -> q a c"),
+                )
+
         nc.sync.dma_start(idx1[:], offs)
         load_packed_planes(tab_s, tab_scales)
-        load_packed(0, 1)
+        load_w2(0, 1)
+        load_w3(0, 1)
         load_table_words(0)
-        load_packed_planes(w2_s, w2_scales)
+        load_planes_by_row(w2_s, w2_scales)
         load_w1(0, 0, 1)
         load_table_words(1)
         load_w1(1, 0, 1)
-        for row in range(PLANE_ROWS):
-            nc.sync.dma_start(
-                w3_s[row:P:32, :, :].bitcast(I32),
-                w3_scales.bitcast(I32)[:, row : 4 * PLANE_ROWS : PLANE_ROWS, :].rearrange("a q c -> q a c"),
-            )
+        load_planes_by_row(w3_s, w3_scales)
         v_s = keep.tile([P, S], U8, name="v_s", align_bytes=64)
         nc.vector.tensor_copy(v_s[:], tab_s[:].indirect(idx1[:]))
         plane_span = P - 32 + PLANE_ROWS
@@ -164,7 +170,6 @@ def tile_list_latency_envelopes_kernel(
         nc.sync.dma_start(wo_raw[:], wo.rearrange("(p i) n -> p i n", i=PACK))
         load_all = keep.tile([P, PACK, M], F32, name="load_sb")
         nc.sync.dma_start(load_all[:], load.rearrange("(p i) m -> p i m", i=PACK))
-        load_sb = [load_all[:, :, c * CHUNK : (c + 1) * CHUNK] for c in range(CHUNKS)]
 
         planes = [v_s[:], v_s1[:]]
         ident = keep.tile([P, P], F32, name="ident")
@@ -182,7 +187,7 @@ def tile_list_latency_envelopes_kernel(
         w1_c, w1_s = {}, {}
 
         def quantize_w1(b):
-            rounded = keep.tile([P, PASSES, P, PACK], BF16, name="w1_bf", tag=("w1_bf0", "page1", "piece1", "piece2")[b], align_bytes=64)
+            rounded = keep.tile([P, PASSES, P, PACK], BF16, name="w1_bf", tag=("w1_bf0", "page1", "page3", "w1_bf3")[b], align_bytes=64)
             codes = keep.tile([P, PASSES * P], U32, name="w1_c", tag="w1_c%d" % b, align_bytes=64)
             scales = keep.tile([P, PASSES * P], U8, name="w1_s%d" % b, align_bytes=64)
             for a in range(PASSES):
@@ -207,7 +212,6 @@ def tile_list_latency_envelopes_kernel(
         gather_words(1, 0)
         gather_words(0, 1)
         gather_words(1, 1)
-        open_page(3)
 
 
         pos2, neg1, neg3, late = {}, {}, {}, {}
@@ -241,7 +245,7 @@ def tile_list_latency_envelopes_kernel(
 
         def e2(u, bank):
             c0 = units[u][0] * P
-            return estimate(u, bank, w2_c, [w2_s[PLANE_ROWS * a : P, c0 : c0 + P] for a in range(PASSES)])
+            return estimate(u, bank, w2_c, [w2_s[:, a, c0 : c0 + P] for a in range(PASSES)])
 
         def e3(u, bank):
             c0 = units[u][0] * P
@@ -298,17 +302,23 @@ def tile_list_latency_envelopes_kernel(
             nc.scalar.copy(h[:], turned_sum(above[u], below[u], long_bank([P, BANK]))[:])
             return h
 
-        damping = keep.tile([P, CHUNKS, PACK, CHUNK], F32, name="damping", tag="tab_w0", align_bytes=64)
+        middle = keep.tile([P, 2, PACK, CHUNK], F32, name="middle", tag="tab_w0", align_bytes=64)
+        damping = [
+            keep.tile([P, PACK, P], F32, name="damping0")[:],
+            keep.tile([P, PACK, P], F32, name="damping1")[:],
+            middle[:, 0, :, :],
+            middle[:, 1, :, :],
+            keep.tile([P, PACK, CHUNK], F32, name="damping4")[:],
+        ]
 
-        def fetch(b, c0, c1, x):
-            nc.vector.tensor_copy(x, pages[b][:].indirect(entries(idx3, c0 * CHUNK, c1 * CHUNK)))
+        def fetch(b, m0, m1, x):
+            nc.vector.tensor_copy(x, pages[b][:].indirect(entries(idx3, m0, m1)))
 
-        def spread(b, c0, c1, x, e):
-            nc.scalar.activation(e[:], x, ACT.Exp, scale=-1.0)
-            for i in range(PACK):
-                nc.sync.dma_start(
-                    damping[32 * b : 32 * (b + 1), c0:c1, i, :], e[i:P:PACK, :].rearrange("p (c m) -> p c m", m=CHUNK)
-                )
+        def spread(b, m0, m1, x, e):
+            nc.scalar.activation(e, x, ACT.Exp, scale=-1.0)
+            for k, (p0, p1) in enumerate(PIECES):
+                if m0 <= p0 and p1 <= m1:
+                    nc.sync.dma_start(damping[k][32 * b : 32 * (b + 1), :, :], e[:, p0 - m0 : p1 - m0])
 
         fetched = {}
         banks = {}
@@ -345,22 +355,24 @@ def tile_list_latency_envelopes_kernel(
             upper_part(u)
             if u < last:
                 copy_e2(u + 1)
-                if u % 2 == 1:
-                    quantize_w1(units[u + 1][0])
+                if u % 2 == 0 and u < last - 1:
+                    quantize_w1(units[u + 2][0])
+                if u == 2:
+                    open_page(3)
                 negate_e1(u + 1)
             h = envelope(u)
             if u > 2:
                 b, half = units[u - 3]
-                fetched[u] = (b, 2 * half, 2 * half + 2, below[u][:])
+                fetched[u] = (b, half * BANK, (half + 1) * BANK, below[u][:])
                 fetch(*fetched[u])
             put(u, h)
             if u - LAG in fetched:
-                spread(*fetched[u - LAG], above[u])
-        spread(*fetched[last - 1], below[last - 2])
+                spread(*fetched[u - LAG], above[u][:])
+        spread(*fetched[last - 1], below[last - 2][:])
         wo_all = keep.tile([P, N, PACK], BF16, name="wo_all", tag="wo_all", align_bytes=64)
         for n0 in range(0, N, WO_CAST):
             nc.scalar.copy(out=woven_out(wo_all[:, n0 : n0 + WO_CAST, :]), in_=woven(wo_raw[:, :, n0 : n0 + WO_CAST]))
-        spread(*fetched[last], unit_tile("neg1"))
+        spread(*fetched[last], unit_tile("neg1")[:])
         for k in range(N // WO_PIECE):
             wo_bf[k] = wo_all[:, WO_PIECE * k : WO_PIECE * (k + 1), :]
         wo_c, wo_s = {}, {}
@@ -372,26 +384,23 @@ def tile_list_latency_envelopes_kernel(
                 out=wo_c[k].bitcast(FP8X4), scales=wo_s[k][:], in_=wo_bf[k].rearrange("p n i -> p (n i)")
             )
 
-        last_x = keep.tile([P, M], F32, name="last_x")
-        late_x = h
-        for b, c0, c1, x in [
-            (PAGES - 1, 0, 1, last_x[:, :CHUNK]),
-            (PAGES - 1, 1, 2, last_x[:, CHUNK:BANK]),
-            (PAGES - 2, 2, 4, late_x[:]),
-            (PAGES - 1, 2, 4, last_x[:, BANK:]),
-        ]:
-            fetch(b, c0, c1, x)
-            last_e = ring.tile([P, (c1 - c0) * CHUNK], F32, name="last_e", bufs=CHUNKS)
-            spread(b, c0, c1, x, last_e)
-        wo_rest = keep.tile([P, 2, WO_PIECE], U32, name="wo_rest", tag="page2", align_bytes=64)
-        for k in range(2):
-            quantize_wo(k, wo_rest[:, k, :])
+        def late(b, k0, k1, x):
+            m0, m1 = PIECES[k0][0], PIECES[k1 - 1][1]
+            fetch(b, m0, m1, x)
+            e = keep.tile([P, m1 - m0], F32, name="last_e", tag="last_e%d_%d" % (b, k0), align_bytes=64)
+            spread(b, m0, m1, x, e[:])
 
         out_rows = out.rearrange("(i p) m -> p i m", p=P)
 
-        def damp(c, m0, m1, z):
+        def z_tile(k):
+            m0, m1 = PIECES[k]
+            return keep.tile([P, m1 - m0, PACK], BF16, name="z", tag=Z_TAGS[k], align_bytes=64)
+
+        def damp(k, z, c0, c1):
+            m0 = PIECES[k][0]
             nc.vector.tensor_tensor(
-                woven_out(z[:]), woven(damping[:, c, :, m0:m1]), woven(load_sb[c][:, :, m0:m1]), ALU.mult
+                woven_out(z[:, c0:c1, :]), woven(damping[k][:, :, c0:c1]),
+                woven(load_all[:, :, m0 + c0 : m0 + c1]), ALU.mult,
             )
 
         def quantize_z(z, width):
@@ -400,33 +409,49 @@ def tile_list_latency_envelopes_kernel(
             nc.vector.quantize_mx(out=z_c[:].bitcast(FP8X4), scales=z_s[:], in_=z[:].rearrange("p m i -> p (m i)"))
             return z_c, z_s
 
-        def project(z_q, m0, width, t0, t1, bank, copy_out):
-            acc = bank([P, t1 - t0, width])
-            for t in range(t0, t1):
-                k, n0 = divmod(t * P, WO_PIECE)
-                nc.tensor.matmul_mx(
-                    out=acc[:, t - t0, :], lhsT=wo_c[k][:, n0 : n0 + P].bitcast(FP8X4), lhsT_scale=wo_s[k][:, n0 : n0 + P],
-                    rhs=z_q[0][:].bitcast(FP8X4), rhs_scale=z_q[1][:], start=True, stop=True,
-                )
-            result = ring.tile([P, t1 - t0, width], F32, name="result", bufs=12)
-            copy_out(result[:], acc[:])
-            nc.sync.dma_start(out_rows[:, t0:t1, m0 : m0 + width], result[:])
+        def project(z, k, banks, copy_outs):
+            m0, m1 = PIECES[k]
+            z_c, z_s = quantize_z(z, m1 - m0)
+            step = N // P // len(copy_outs)
+            for g, copy_out in enumerate(copy_outs):
+                t0, t1 = g * step, (g + 1) * step
+                acc = banks[g]([P, step, m1 - m0])
+                for t in range(t0, t1):
+                    w, n0 = divmod(t * P, WO_PIECE)
+                    nc.tensor.matmul_mx(
+                        out=acc[:, t - t0, :], lhsT=wo_c[w][:, n0 : n0 + P].bitcast(FP8X4),
+                        lhsT_scale=wo_s[w][:, n0 : n0 + P],
+                        rhs=z_c[:].bitcast(FP8X4), rhs_scale=z_s[:], start=True, stop=True,
+                    )
+                result = ring.tile([P, step, m1 - m0], F32, name="result", bufs=12)
+                copy_out(result[:], acc[:])
+                nc.sync.dma_start(out_rows[:, t0:t1, m0:m1], result[:])
 
-        halves = [
-            keep.tile([P, P, PACK], BF16, name="z_half", tag=("z_half", "wo_last")[k], align_bytes=64) for k in range(2)
-        ]
-        for k in range(2):
-            damp(0, k * P, (k + 1) * P, halves[k])
-        first = [quantize_z(halves[k], P) for k in range(2)]
-        wo_last = keep.tile([P, WO_PIECE], U32, name="wo_last", tag="wo_last", align_bytes=64)
-        quantize_wo(2, wo_last[:])
-        for t0 in (0, 3):
-            for k in range(2):
-                project(first[k], k * P, P, t0, t0 + 3, (long_bank, short_bank)[k], nc.scalar.copy)
-        for c in range(1, CHUNKS):
-            z = ring.tile([P, CHUNK, PACK], BF16, name="z", align_bytes=64, bufs=1)
-            damp(c, 0, CHUNK, z)
-            z_q = quantize_z(z, CHUNK)
-            for g in range(N // (2 * P)):
-                copy_out = nc.vector.tensor_copy if c == CHUNKS - 1 and g == 1 else nc.scalar.copy
-                project(z_q, c * CHUNK, CHUNK, 2 * g, 2 * g + 2, long_bank if g % 2 == 0 else short_bank, copy_out)
+        def x_on(tag):
+            return keep.tile([P, CHUNK], F32, name="held_x", tag=tag, align_bytes=64)[:]
+
+        last_x = keep.tile([P, 3 * CHUNK], F32, name="last_x")
+        for k in range(3):
+            late(PAGES - 1, k, k + 1, last_x[:, PIECES[k][0] : PIECES[k][1]])
+        wo_codes = keep.tile([P, 2 * WO_PIECE], U32, name="wo_codes", tag="page1", align_bytes=64)
+        for w in range(2):
+            quantize_wo(w, wo_codes[:, w * WO_PIECE : (w + 1) * WO_PIECE])
+        late(PAGES - 1, 3, 4, last_x[:, 2 * CHUNK :])
+        late(PAGES - 2, 3, 5, h[:])
+        copy = nc.scalar.copy
+        z = z_tile(0)
+        damp(0, z, 0, P)
+        quantize_wo(2, keep.tile([P, WO_PIECE], U32, name="wo_last", tag="last_e3_0", align_bytes=64)[:])
+        project(z, 0, (long_bank, short_bank), (copy, copy))
+        z = z_tile(1)
+        damp(1, z, 0, P)
+        late(PAGES - 1, 4, 5, x_on("z0"))
+        project(z, 1, (long_bank, short_bank), (copy, copy))
+        z, z_next = z_tile(2), z_tile(3)
+        damp(2, z, 0, CHUNK)
+        for k in (2, 3):
+            damp(k + 1, z_next, 0, P)
+            project(z, k, (long_bank, short_bank, long_bank), (copy, copy, copy))
+            damp(k + 1, z_next, P, CHUNK)
+            z, z_next = z_next, z_tile(4) if k == 2 else None
+        project(z, 4, (long_bank, short_bank, long_bank), (copy, nc.vector.tensor_copy, copy))

@@ -31,6 +31,7 @@ WO_PIECE = 256
 KINDS = "EEBBBBBB"
 STOP = 8
 LAG = 2
+SECOND_PLANE = 16
 WO_CAST = 64
 E_BANKS = 3
 WO_UNIT = 2 * PAGES - N // WO_PIECE
@@ -90,7 +91,8 @@ def tile_list_latency_envelopes_kernel(
             pages[b] = keep.tile([P, T2], F32, name="page", tag="page%d" % b, align_bytes=64)
             nc.gpsimd.memset(pages[b][:].bitcast(I32), 0)
 
-        open_page(0)
+        ident = keep.tile([P, P], F32, name="ident")
+        make_identity(nc, ident[:])
 
         tab_w = [keep.tile([P, T], I32, name="tab_w", tag="tab_w%d" % a, align_bytes=64) for a in range(PASSES)]
         w1_rows = w1.rearrange("(a p i) c -> a p i c", a=PASSES, i=PACK)
@@ -122,11 +124,11 @@ def tile_list_latency_envelopes_kernel(
             load_w2(b0, b1)
             load_w3(b0, b1)
 
-        def load_packed_planes(tile, scales):
-            for q in (0, 2, 1, 3):
+        def load_table_planes():
+            for row in range(PLANE_ROWS):
                 nc.sync.dma_start(
-                    tile[32 * q : 32 * q + PASSES * PLANE_ROWS, :].bitcast(I32),
-                    scales.bitcast(I32)[:, PLANE_ROWS * q : PLANE_ROWS * (q + 1), :],
+                    tab_s[row:P:SECOND_PLANE, :].bitcast(I32),
+                    tab_scales.bitcast(I32)[:, row : 4 * PLANE_ROWS : PLANE_ROWS, :].rearrange("a q t -> q a t"),
                 )
 
         def load_table_words(a):
@@ -140,7 +142,7 @@ def tile_list_latency_envelopes_kernel(
                 )
 
         nc.sync.dma_start(idx1[:], offs)
-        load_packed_planes(tab_s, tab_scales)
+        load_table_planes()
         load_w2(0, 1)
         load_w3(0, 1)
         load_table_words(0)
@@ -153,7 +155,7 @@ def tile_list_latency_envelopes_kernel(
         nc.vector.tensor_copy(v_s[:], tab_s[:].indirect(idx1[:]))
         plane_span = P - 32 + PLANE_ROWS
         nc.sync.dma_start(
-            v_s1[0:plane_span, :].bitcast(I32), v_s[PLANE_ROWS : PLANE_ROWS + plane_span, :].bitcast(I32)
+            v_s1[0:plane_span, :].bitcast(I32), v_s[SECOND_PLANE : SECOND_PLANE + plane_span, :].bitcast(I32)
         )
         for a in range(PASSES):
             load_w1(a, 1, 2)
@@ -172,9 +174,6 @@ def tile_list_latency_envelopes_kernel(
         nc.sync.dma_start(load_all[:], load.rearrange("(p i) m -> p i m", i=PACK))
 
         planes = [v_s[:], v_s1[:]]
-        ident = keep.tile([P, P], F32, name="ident")
-        if KINDS.count("E") < len(KINDS):
-            make_identity(nc, ident[:])
 
         v_w = {}
 
@@ -187,7 +186,7 @@ def tile_list_latency_envelopes_kernel(
         w1_c, w1_s = {}, {}
 
         def quantize_w1(b):
-            rounded = keep.tile([P, PASSES, P, PACK], BF16, name="w1_bf", tag=("w1_bf0", "page1", "page3", "w1_bf3")[b], align_bytes=64)
+            rounded = keep.tile([P, PASSES, P, PACK], BF16, name="w1_bf", tag=("page0", "page1", "page3", "w1_bf3")[b], align_bytes=64)
             codes = keep.tile([P, PASSES * P], U32, name="w1_c", tag="w1_c%d" % b, align_bytes=64)
             scales = keep.tile([P, PASSES * P], U8, name="w1_s%d" % b, align_bytes=64)
             for a in range(PASSES):
@@ -212,6 +211,7 @@ def tile_list_latency_envelopes_kernel(
         gather_words(1, 0)
         gather_words(0, 1)
         gather_words(1, 1)
+        open_page(0)
 
 
         pos2, neg1, neg3, late = {}, {}, {}, {}
@@ -399,7 +399,7 @@ def tile_list_latency_envelopes_kernel(
         def damp(k, z, c0, c1):
             m0 = PIECES[k][0]
             nc.vector.tensor_tensor(
-                woven_out(z[:, c0:c1, :]), woven(damping[k][:, :, c0:c1]),
+                woven_out(z), woven(damping[k][:, :, c0:c1]),
                 woven(load_all[:, :, m0 + c0 : m0 + c1]), ALU.mult,
             )
 
@@ -409,8 +409,7 @@ def tile_list_latency_envelopes_kernel(
             nc.vector.quantize_mx(out=z_c[:].bitcast(FP8X4), scales=z_s[:], in_=z[:].rearrange("p m i -> p (m i)"))
             return z_c, z_s
 
-        def project(z, k, banks, copy_outs):
-            m0, m1 = PIECES[k]
+        def project(z, m0, m1, banks, copy_outs):
             z_c, z_s = quantize_z(z, m1 - m0)
             step = N // P // len(copy_outs)
             for g, copy_out in enumerate(copy_outs):
@@ -440,18 +439,22 @@ def tile_list_latency_envelopes_kernel(
         late(PAGES - 2, 3, 5, h[:])
         copy = nc.scalar.copy
         z = z_tile(0)
-        damp(0, z, 0, P)
+        damp(0, z[:], 0, P)
         quantize_wo(2, keep.tile([P, WO_PIECE], U32, name="wo_last", tag="last_e3_0", align_bytes=64)[:])
-        project(z, 0, (long_bank, short_bank), (copy, copy))
+        project(z, *PIECES[0], (long_bank, short_bank), (copy, copy))
         z = z_tile(1)
-        damp(1, z, 0, P)
+        damp(1, z[:], 0, P)
         late(PAGES - 1, 4, 5, x_on("z0"))
-        project(z, 1, (long_bank, short_bank), (copy, copy))
-        z, z_next = z_tile(2), z_tile(3)
-        damp(2, z, 0, CHUNK)
-        for k in (2, 3):
-            damp(k + 1, z_next, 0, P)
-            project(z, k, (long_bank, short_bank, long_bank), (copy, copy, copy))
-            damp(k + 1, z_next, P, CHUNK)
-            z, z_next = z_next, z_tile(4) if k == 2 else None
-        project(z, 4, (long_bank, short_bank, long_bank), (copy, nc.vector.tensor_copy, copy))
+        project(z, *PIECES[1], (long_bank, short_bank), (copy, copy))
+        three = (long_bank, short_bank, long_bank)
+        z2, z3 = z_tile(2), z_tile(3)
+        damp(2, z2[:], 0, CHUNK)
+        damp(3, z3[:, :P, :], 0, P)
+        project(z2, *PIECES[2], three, (copy, copy, copy))
+        damp(3, z3[:, P:, :], P, CHUNK)
+        ends = [keep.tile([P, P, PACK], BF16, name="z_end%d" % k, align_bytes=64) for k in range(2)]
+        damp(4, ends[0][:], 0, P)
+        project(z3, *PIECES[3], three, (copy, copy, copy))
+        damp(4, ends[1][:], P, CHUNK)
+        project(ends[0], M - CHUNK, M - P, (long_bank, short_bank), (copy, nc.vector.tensor_copy))
+        project(ends[1], M - P, M, (long_bank, short_bank), (copy, nc.vector.tensor_copy))

@@ -20,24 +20,19 @@ ACT = mybir.ActivationFunctionType
 P = 128
 PACK = 4
 STRIPE = 16
+QUADRANT = 32
 PLANE_ROWS = 4
-QUADS = P // 32
+SECOND_PLANE = 16
 PASSES = K // (P * PACK)
 PAGES = H // P
 BANK = 512
+BANKS = 8
 CHUNK = 256
-CHUNKS = M // CHUNK
 WO_PIECE = 256
-KINDS = "EEBBBBBB"
-STOP = 8
-LAG = 2
-SECOND_PLANE = 16
-WO_CAST = 64
-E_BANKS = 3
-WO_UNIT = 2 * PAGES - N // WO_PIECE
-LONG_BANKS = 4
-Z_TAGS = ("z0", "wo_all", "page3", "z3", "z4")
-PIECES = [(0, 128), (128, 256), (256, 512), (512, 768), (768, 1024)]
+WO_CAST = 128
+W1_CAST = 128
+EXP_LAG = 2
+MOVED = [(0, 128), (128, 256), (256, 512), (512, 768), (768, 1024)]
 
 
 def woven(planes):
@@ -58,17 +53,19 @@ def tile_list_latency_envelopes_kernel(
         ring = ctx.enter_context(tc.tile_pool(name="ring", bufs=2))
         psum = ctx.enter_context(tc.psum_pool(name="psum", bufs=1))
 
-        def short_bank(shape):
-            return psum.tile(shape, F32, name="short_bank", bufs=E_BANKS)
+        def on(tag, shape, dtype):
+            return keep.tile(shape, dtype, name=tag, tag=tag, align_bytes=64)
 
-        def upper_bank(shape):
-            return psum.tile(shape, F32, name="upper_bank", bufs=1)
+        def bank(k, shape=(P, BANK)):
+            return psum.tile(list(shape), F32, name="bank", tag="bank%d" % k)
 
-        def long_bank(shape):
-            return psum.tile(shape, F32, name="long_bank", bufs=LONG_BANKS)
+        outer_bank, lower_bank, upper_bank = 0, 1, 2
+        sum_banks = (3, 4)
 
-        def unit_tile(name):
-            return ring.tile([P, BANK], F32, name=name, bufs={"pos2": 3, "h": 4, "neg1": 3, "neg3": 3, "below": 5}.get(name, 4), align_bytes=64)
+        depths = {"pos2": 3, "neg1": 3, "neg3": 3, "below": 5, "above": 4, "h": 4}
+
+        def unit_tile(kind):
+            return ring.tile([P, BANK], F32, name=kind, bufs=depths[kind], align_bytes=64)
 
         idx1 = keep.tile([P, S // STRIPE], U16, name="idx1")
         idx2 = keep.tile([P, S // STRIPE], U16, name="idx2")
@@ -77,24 +74,24 @@ def tile_list_latency_envelopes_kernel(
         def entries(idx, j0, j1):
             return idx[:, j0 // STRIPE : j1 // STRIPE]
 
-        tab_s = keep.tile([P, T], U8, name="tab_s", align_bytes=64)
-        v_s1 = keep.tile([P, S], U8, name="v_s1", align_bytes=64)
-        w2_s = keep.tile([P, PASSES, H], U8, name="w2_s", align_bytes=64)
-        w3_s = keep.tile([P, PASSES, H], U8, name="w3_s", align_bytes=64)
+        tab_s = on("tab_s", [P, T], U8)
+        w2_s = on("w2_s", [P, PASSES, H], U8)
+        w3_s = on("w3_s", [P, PASSES, H], U8)
+        v_s1 = on("v_s1", [P, S], U8)
         nc.gpsimd.memset(tab_s[:].bitcast(I32), 0)
         nc.gpsimd.memset(w2_s[:].rearrange("p a c -> p (a c)").bitcast(I32), 0)
         nc.gpsimd.memset(w3_s[:].rearrange("p a c -> p (a c)").bitcast(I32), 0)
         nc.gpsimd.memset(v_s1[:].bitcast(I32), 0)
-        pages = {}
-
-        def open_page(b):
-            pages[b] = keep.tile([P, T2], F32, name="page", tag="page%d" % b, align_bytes=64)
-            nc.gpsimd.memset(pages[b][:].bitcast(I32), 0)
-
         ident = keep.tile([P, P], F32, name="ident")
         make_identity(nc, ident[:])
 
-        tab_w = [keep.tile([P, T], I32, name="tab_w", tag="tab_w%d" % a, align_bytes=64) for a in range(PASSES)]
+        pages = {}
+
+        def open_page(b):
+            pages[b] = on("page%d" % b, [P, T2], F32)
+            nc.gpsimd.memset(pages[b][:].bitcast(I32), 0)
+
+        tab_w = [on("tab_w%d" % a, [P, T], I32) for a in range(PASSES)]
         w1_rows = w1.rearrange("(a p i) c -> a p i c", a=PASSES, i=PACK)
         w2_rows = w2_words.rearrange("a p c i -> p a (c i)")
         w3_rows = w3_words.rearrange("a p c -> p a c")
@@ -106,63 +103,48 @@ def tile_list_latency_envelopes_kernel(
             for b in range(b0, b1):
                 w1_raw[b, a] = raw[:, :, (b - b0) * P : (b - b0 + 1) * P]
 
-        def load_w2(b0, b1):
-            words = keep.tile([P, PASSES, (b1 - b0) * P], U32, name="w2_c", tag="page1" if b0 == 0 else "w2_c%d" % b0, align_bytes=64)
+        def load_packed(b0, b1):
+            words = on("page1" if b0 == 0 else "w2_c%d" % b0, [P, PASSES, (b1 - b0) * P], U32)
             nc.sync.dma_start(words[:].bitcast(I32), w2_rows[:, :, 4 * b0 * P : 4 * b1 * P].bitcast(I32))
+            nibbles = on("w3_c%d" % b0, [P, PASSES, 2 * (b1 - b0) * P], U8)
+            nc.sync.dma_start(nibbles[:].bitcast(I32), w3_rows[:, :, 2 * b0 * P : 2 * b1 * P].bitcast(I32))
             for b in range(b0, b1):
                 for a in range(PASSES):
                     w2_c[b, a] = words[:, a, (b - b0) * P : (b - b0 + 1) * P].bitcast(FP8X4)
+                    w3_c[b, a] = nibbles[:, a, 2 * (b - b0) * P : 2 * (b - b0 + 1) * P].bitcast(FP4X4)
 
-        def load_w3(b0, b1):
-            words = keep.tile([P, PASSES, 2 * (b1 - b0) * P], U8, name="w3_c%d" % b0, align_bytes=64)
-            nc.sync.dma_start(words[:].bitcast(I32), w3_rows[:, :, 2 * b0 * P : 2 * b1 * P].bitcast(I32))
-            for b in range(b0, b1):
-                for a in range(PASSES):
-                    w3_c[b, a] = words[:, a, 2 * (b - b0) * P : 2 * (b - b0 + 1) * P].bitcast(FP4X4)
-
-        def load_packed(b0, b1):
-            load_w2(b0, b1)
-            load_w3(b0, b1)
-
-        def load_table_planes():
+        def load_scale_rows(rows_of, scales):
             for row in range(PLANE_ROWS):
                 nc.sync.dma_start(
-                    tab_s[row:P:SECOND_PLANE, :].bitcast(I32),
-                    tab_scales.bitcast(I32)[:, row : 4 * PLANE_ROWS : PLANE_ROWS, :].rearrange("a q t -> q a t"),
+                    rows_of(row).bitcast(I32),
+                    scales.bitcast(I32)[:, row : 4 * PLANE_ROWS : PLANE_ROWS, :].rearrange("a q c -> q a c"),
                 )
 
         def load_table_words(a):
             nc.sync.dma_start(tab_w[a][:], tab_words[a].rearrange("p t i -> p (t i)").bitcast(I32))
 
-        def load_planes_by_row(tile, scales):
-            for row in range(PLANE_ROWS):
-                nc.sync.dma_start(
-                    tile[row:P:32, :, :].bitcast(I32),
-                    scales.bitcast(I32)[:, row : 4 * PLANE_ROWS : PLANE_ROWS, :].rearrange("a q c -> q a c"),
-                )
-
         nc.sync.dma_start(idx1[:], offs)
-        load_table_planes()
-        load_w2(0, 1)
-        load_w3(0, 1)
+        load_scale_rows(lambda row: tab_s[row:P:SECOND_PLANE, :], tab_scales)
+        load_packed(0, 1)
         load_table_words(0)
-        load_planes_by_row(w2_s, w2_scales)
+        load_scale_rows(lambda row: w2_s[row:P:QUADRANT, :, :], w2_scales)
         load_w1(0, 0, 1)
         load_table_words(1)
         load_w1(1, 0, 1)
-        load_planes_by_row(w3_s, w3_scales)
-        v_s = keep.tile([P, S], U8, name="v_s", align_bytes=64)
+        load_scale_rows(lambda row: w3_s[row:P:QUADRANT, :, :], w3_scales)
+        v_s = on("v_s", [P, S], U8)
         nc.vector.tensor_copy(v_s[:], tab_s[:].indirect(idx1[:]))
-        plane_span = P - 32 + PLANE_ROWS
+        plane_span = P - QUADRANT + PLANE_ROWS
         nc.sync.dma_start(
             v_s1[0:plane_span, :].bitcast(I32), v_s[SECOND_PLANE : SECOND_PLANE + plane_span, :].bitcast(I32)
         )
+        planes = [v_s[:], v_s1[:]]
         for a in range(PASSES):
             load_w1(a, 1, 2)
-        wgs_sb = [keep.tile([P, BANK], F32, name="wgs_sb", tag="wgs%d" % half) for half in range(2)]
+        wgs_sb = [keep.tile([P, BANK], F32, name="wgs%d" % half) for half in range(2)]
+        load_packed(1, 2)
         nc.sync.dma_start(wgs_sb[0][:], wgs[:, :BANK])
         nc.sync.dma_start(idx2[:], offs2)
-        load_packed(1, 2)
         nc.sync.dma_start(wgs_sb[1][:], wgs[:, BANK:])
         for a in range(PASSES):
             load_w1(a, 2, PAGES)
@@ -170,15 +152,13 @@ def tile_list_latency_envelopes_kernel(
         nc.sync.dma_start(idx3[:], offs3)
         wo_raw = keep.tile([P, PACK, N], F32, name="wo_raw")
         nc.sync.dma_start(wo_raw[:], wo.rearrange("(p i) n -> p i n", i=PACK))
-        load_all = keep.tile([P, PACK, M], F32, name="load_sb")
-        nc.sync.dma_start(load_all[:], load.rearrange("(p i) m -> p i m", i=PACK))
-
-        planes = [v_s[:], v_s1[:]]
+        load_sb = keep.tile([P, PACK, M], F32, name="load_sb")
+        nc.sync.dma_start(load_sb[:], load.rearrange("(p i) m -> p i m", i=PACK))
 
         v_w = {}
 
         def gather_words(a, half):
-            v_w[a, half] = keep.tile([P, BANK], U32, name="v_w%d%d" % (a, half), align_bytes=64)
+            v_w[a, half] = on("v_w%d%d" % (a, half), [P, BANK], U32)
             nc.vector.tensor_copy(
                 v_w[a, half][:], tab_w[a][:].bitcast(U32).indirect(entries(idx1, half * BANK, (half + 1) * BANK))
             )
@@ -186,11 +166,11 @@ def tile_list_latency_envelopes_kernel(
         w1_c, w1_s = {}, {}
 
         def quantize_w1(b):
-            rounded = keep.tile([P, PASSES, P, PACK], BF16, name="w1_bf", tag=("page0", "page1", "page3", "w1_bf3")[b], align_bytes=64)
-            codes = keep.tile([P, PASSES * P], U32, name="w1_c", tag="w1_c%d" % b, align_bytes=64)
-            scales = keep.tile([P, PASSES * P], U8, name="w1_s%d" % b, align_bytes=64)
+            rounded = on(("page0", "page1", "page3", "w1_bf3")[b], [P, PASSES, P, PACK], BF16)
+            codes = on("w1_c%d" % b, [P, PASSES * P], U32)
+            scales = on("w1_s%d" % b, [P, PASSES * P], U8)
+            step = P if b < 2 else W1_CAST
             for a in range(PASSES):
-                step = P if b < 2 else P // 2
                 for c0 in range(0, P, step):
                     nc.scalar.copy(
                         out=woven_out(rounded[:, a, c0 : c0 + step, :]), in_=woven(w1_raw[b, a][:, :, c0 : c0 + step])
@@ -213,53 +193,42 @@ def tile_list_latency_envelopes_kernel(
         gather_words(1, 1)
         open_page(0)
 
-
-        pos2, neg1, neg3, late = {}, {}, {}, {}
-        wo_bf = {}
-
         units = [(b, half) for b in range(PAGES) for half in range(2)]
+        last = len(units) - 1
 
-        def estimate(u, bank, codes, scales):
+        def estimate(u, k, codes, scales):
             b, half = units[u]
-            j0 = half * BANK
+            acc = bank(k)
             for a in range(PASSES):
-                if True:
-                    nc.tensor.matmul_mx(
-                        out=bank[:], lhsT=codes[b, a], lhsT_scale=scales[a],
-                        rhs=v_w[a, half][:].bitcast(FP8X4), rhs_scale=planes[a][:, j0 : j0 + BANK],
-                        start=(a == 0), stop=(a == PASSES - 1),
-                    )
-                else:
-                    for c0 in range(0, BANK, P):
-                        nc.tensor.matmul_mx(
-                            out=bank[:, c0 : c0 + P],
-                            lhsT=v_w[a, half][:, c0 : c0 + P].bitcast(FP8X4),
-                            lhsT_scale=planes[a][:, j0 + c0 : j0 + c0 + P],
-                            rhs=codes[b, a], rhs_scale=scales[a],
-                            start=(a == 0 and c0 == 0), stop=(a == PASSES - 1 and c0 == BANK - P),
-                        )
-            return bank
+                nc.tensor.matmul_mx(
+                    out=acc[:], lhsT=codes[b, a], lhsT_scale=scales(b, a),
+                    rhs=v_w[a, half][:].bitcast(FP8X4), rhs_scale=planes[a][:, half * BANK : (half + 1) * BANK],
+                    start=(a == 0), stop=(a == PASSES - 1),
+                )
+            return acc
 
-        def e1(u, bank):
-            return estimate(u, bank, w1_c, [w1_s[units[u][0], a] for a in range(PASSES)])
+        def e1(u, k):
+            return estimate(u, k, w1_c, lambda b, a: w1_s[b, a])
 
-        def e2(u, bank):
-            c0 = units[u][0] * P
-            return estimate(u, bank, w2_c, [w2_s[:, a, c0 : c0 + P] for a in range(PASSES)])
+        def e2(u, k):
+            return estimate(u, k, w2_c, lambda b, a: w2_s[:, a, b * P : (b + 1) * P])
 
-        def e3(u, bank):
-            c0 = units[u][0] * P
-            return estimate(u, bank, w3_c, [w3_s[:, a, c0 : c0 + P] for a in range(PASSES)])
+        def e3(u, k):
+            return estimate(u, k, w3_c, lambda b, a: w3_s[:, a, b * P : (b + 1) * P])
 
-        weighted = {}
+        def turn(acc, tile, start=True, stop=True):
+            nc.tensor.matmul(acc, tile, ident[:], start=start, stop=stop, is_transpose=True)
 
-        def turned_sum(first, second, bank):
+        def turned_sum(first, second, k):
+            acc = bank(k)
             for c0 in range(0, BANK, P):
-                nc.tensor.matmul(bank[:, c0 : c0 + P], first[:, c0 : c0 + P], ident[:],
-                                 start=True, stop=False, is_transpose=True)
-                nc.tensor.matmul(bank[:, c0 : c0 + P], second[:, c0 : c0 + P], ident[:],
-                                 start=False, stop=True, is_transpose=True)
-            return bank
+                turn(acc[:, c0 : c0 + P], first[:, c0 : c0 + P], stop=False)
+                turn(acc[:, c0 : c0 + P], second[:, c0 : c0 + P], start=False)
+            return acc
+
+        def copy_out(tile, acc, func, scale):
+            nc.scalar.activation(tile[:], acc[:], func, scale=scale)
+            return tile
 
         def put(u, h):
             b, half = units[u]
@@ -267,42 +236,34 @@ def tile_list_latency_envelopes_kernel(
                 pages[b][:].indirect(entries(idx2, half * BANK, (half + 1) * BANK)), h[:], wgs_sb[half][:], ALU.mult
             )
 
-        def scaled_copy(name, bank, func, scale):
-            tile = unit_tile(name) if isinstance(name, str) else name
-            nc.scalar.activation(tile[:], bank[:], func, scale=scale)
-            return tile
+        pos2, neg1, neg3, below, above = {}, {}, {}, {}, {}
 
-
-        def pos2_place(u):
-            if u == 0:
-                return keep.tile([P, BANK], F32, name="pos2", tag="w1_c1", align_bytes=64)
-            if u == len(units) - 1:
-                return keep.tile([P, BANK], F32, name="pos2", tag="wo_all", align_bytes=64)
-            return "pos2"
-
-        def copy_e2(u):
-            pos2[u] = scaled_copy(pos2_place(u), e2(u, (upper_bank if u == 0 else short_bank)([P, BANK])), ACT.Copy, 1.0)
+        def copy_e2(u, k):
+            place = {0: "w1_c1", last: "wo_bf"}
+            tile = on(place[u], [P, BANK], F32) if u in place else unit_tile("pos2")
+            pos2[u] = copy_out(tile, e2(u, k), ACT.Copy, 1.0)
 
         def negate_e1(u):
-            neg1[u] = scaled_copy("neg1", e1(u, short_bank([P, BANK])), ACT.Copy, -1.0)
+            tile = on("w1_bf3", [P, BANK], F32) if u == 3 else unit_tile("neg1")
+            neg1[u] = copy_out(tile, e1(u, outer_bank), ACT.Copy, -1.0)
 
         def negate_e3(u):
-            neg3[u] = scaled_copy("neg3", e3(u, short_bank([P, BANK])), ACT.Copy, -1.0)
-
-        below, above = {}, {}
+            tile = on("page3", [P, BANK], F32) if u == 2 else unit_tile("neg3")
+            neg3[u] = copy_out(tile, e3(u, 5 if u == 3 else outer_bank), ACT.Copy, -1.0)
 
         def lower_part(u):
-            below[u] = scaled_copy("below", turned_sum(pos2[u], neg3[u], long_bank([P, BANK])), ACT.Relu, 1.0)
+            first, second = (neg3, pos2) if u == 2 else (pos2, neg3)
+            below[u] = copy_out(unit_tile("below"), turned_sum(first[u], second[u], lower_bank), ACT.Relu, 1.0)
 
         def upper_part(u):
-            above[u] = scaled_copy("above", turned_sum(neg1[u], pos2[u], upper_bank([P, BANK])), ACT.Relu, -1.0)
+            above[u] = copy_out(unit_tile("above"), turned_sum(neg1[u], pos2[u], upper_bank), ACT.Relu, -1.0)
 
         def envelope(u):
             h = unit_tile("h")
-            nc.scalar.copy(h[:], turned_sum(above[u], below[u], long_bank([P, BANK]))[:])
+            nc.scalar.copy(h[:], turned_sum(below[u], above[u], sum_banks[u % 2])[:])
             return h
 
-        middle = keep.tile([P, 2, PACK, CHUNK], F32, name="middle", tag="tab_w0", align_bytes=64)
+        middle = on("tab_w0", [P, 2, PACK, CHUNK], F32)
         damping = [
             keep.tile([P, PACK, P], F32, name="damping0")[:],
             keep.tile([P, PACK, P], F32, name="damping1")[:],
@@ -316,46 +277,48 @@ def tile_list_latency_envelopes_kernel(
 
         def spread(b, m0, m1, x, e):
             nc.scalar.activation(e, x, ACT.Exp, scale=-1.0)
-            for k, (p0, p1) in enumerate(PIECES):
+            for k, (p0, p1) in enumerate(MOVED):
                 if m0 <= p0 and p1 <= m1:
-                    nc.sync.dma_start(damping[k][32 * b : 32 * (b + 1), :, :], e[:, p0 - m0 : p1 - m0])
+                    nc.sync.dma_start(damping[k][QUADRANT * b : QUADRANT * (b + 1), :, :], e[:, p0 - m0 : p1 - m0])
 
-        fetched = {}
-        banks = {}
-        for u in range(2):
-            copy_e2(u)
-            low_bank = e3(u, (long_bank if u == 0 else upper_bank)([P, BANK]))
-            banks[u] = (e1(u, (short_bank if u == 0 else long_bank)([P, BANK])), low_bank)
+        copy_e2(0, upper_bank)
+        e3_0, e1_0 = e3(0, 5), e1(0, 6)
+        copy_e2(1, 7)
+        e3_1, e1_1 = e3(1, upper_bank), e1(1, sum_banks[0])
 
-        def bounds(u, high):
+        def bounds(u, e1_u, e3_u, high):
             low = unit_tile("neg3")
-            nc.vector.tensor_tensor(low[:], banks[u][1][:], pos2[u][:], ALU.min)
-            nc.vector.tensor_tensor(high[:], banks[u][0][:], pos2[u][:], ALU.max)
+            nc.vector.tensor_tensor(low[:], e3_u[:], pos2[u][:], ALU.min)
+            nc.vector.tensor_tensor(high[:], e1_u[:], pos2[u][:], ALU.max)
             return high, low
 
-        high, low = bounds(0, unit_tile("neg1"))
+        def difference(high, low):
+            h = unit_tile("h")
+            nc.vector.tensor_tensor(h[:], high[:], low[:], ALU.subtract)
+            return h
+
+        first = bounds(0, e1_0, e3_0, unit_tile("neg1"))
         quantize_w1(1)
-        h = unit_tile("h")
-        nc.vector.tensor_tensor(h[:], high[:], low[:], ALU.subtract)
-        high, low = bounds(1, keep.tile([P, BANK], F32, name="high", tag="page2", align_bytes=64))
+        h = difference(*first)
+        second = bounds(1, e1_1, e3_1, on("page2", [P, BANK], F32))
         open_page(1)
         put(0, h)
-        h = unit_tile("h")
-        nc.vector.tensor_tensor(h[:], high[:], low[:], ALU.subtract)
+        h = difference(*second)
         open_page(2)
         negate_e3(2)
-        copy_e2(2)
+        copy_e2(2, lower_bank)
         negate_e1(2)
         put(1, h)
-        last = len(units) - 1
+
+        fetched = {}
         for u in range(2, last + 1):
             lower_part(u)
             if u < last:
                 negate_e3(u + 1)
             upper_part(u)
             if u < last:
-                copy_e2(u + 1)
-                if u % 2 == 0 and u < last - 1:
+                copy_e2(u + 1, 6 if u == 2 else lower_bank)
+                if u in (2, 4):
                     quantize_w1(units[u + 2][0])
                 if u == 2:
                     open_page(3)
@@ -363,98 +326,84 @@ def tile_list_latency_envelopes_kernel(
             h = envelope(u)
             if u > 2:
                 b, half = units[u - 3]
-                fetched[u] = (b, half * BANK, (half + 1) * BANK, below[u][:])
+                m0, m1 = half * BANK, (half + 1) * BANK
+                fetched[u] = (b, m0, m1, below[u][:, : m1 - m0])
                 fetch(*fetched[u])
             put(u, h)
-            if u - LAG in fetched:
-                spread(*fetched[u - LAG], above[u][:])
+            if u - EXP_LAG in fetched:
+                x = fetched[u - EXP_LAG]
+                spread(*x, above[u][:, : x[2] - x[1]])
         spread(*fetched[last - 1], below[last - 2][:])
-        wo_all = keep.tile([P, N, PACK], BF16, name="wo_all", tag="wo_all", align_bytes=64)
+        wo_bf = on("wo_bf", [P, N, PACK], BF16)
         for n0 in range(0, N, WO_CAST):
-            nc.scalar.copy(out=woven_out(wo_all[:, n0 : n0 + WO_CAST, :]), in_=woven(wo_raw[:, :, n0 : n0 + WO_CAST]))
+            nc.scalar.copy(out=woven_out(wo_bf[:, n0 : n0 + WO_CAST, :]), in_=woven(wo_raw[:, :, n0 : n0 + WO_CAST]))
         spread(*fetched[last], unit_tile("neg1")[:])
-        for k in range(N // WO_PIECE):
-            wo_bf[k] = wo_all[:, WO_PIECE * k : WO_PIECE * (k + 1), :]
         wo_c, wo_s = {}, {}
 
-        def quantize_wo(k, codes):
-            wo_c[k] = codes
-            wo_s[k] = keep.tile([P, WO_PIECE], U8, name="wo_s%d" % k, align_bytes=64)
+        def quantize_wo(k, tag):
+            wo_c[k] = on(tag, [P, WO_PIECE], U32)
+            wo_s[k] = on("wo_s%d" % k, [P, WO_PIECE], U8)
             nc.vector.quantize_mx(
-                out=wo_c[k].bitcast(FP8X4), scales=wo_s[k][:], in_=wo_bf[k].rearrange("p n i -> p (n i)")
+                out=wo_c[k][:].bitcast(FP8X4), scales=wo_s[k][:],
+                in_=wo_bf[:, WO_PIECE * k : WO_PIECE * (k + 1), :].rearrange("p n i -> p (n i)"),
             )
 
-        def late(b, k0, k1, x):
-            m0, m1 = PIECES[k0][0], PIECES[k1 - 1][1]
+        def late(b, k, k1, x):
+            m0, m1 = MOVED[k][0], MOVED[k1 - 1][1]
             fetch(b, m0, m1, x)
-            e = keep.tile([P, m1 - m0], F32, name="last_e", tag="last_e%d_%d" % (b, k0), align_bytes=64)
-            spread(b, m0, m1, x, e[:])
+            spread(b, m0, m1, x, on("late_e%d%d" % (b, k), [P, m1 - m0], F32)[:])
 
-        out_rows = out.rearrange("(i p) m -> p i m", p=P)
+        def damp(z, factor, m0):
+            width = factor.shape[2]
+            nc.vector.tensor_tensor(woven_out(z), woven(factor), woven(load_sb[:, :, m0 : m0 + width]), ALU.mult)
 
-        def z_tile(k):
-            m0, m1 = PIECES[k]
-            return keep.tile([P, m1 - m0, PACK], BF16, name="z", tag=Z_TAGS[k], align_bytes=64)
+        out_rows = out.rearrange("(t p) m -> p t m", p=P)
+        free_banks = list(range(BANKS))
+        used = []
 
-        def damp(k, z, c0, c1):
-            m0 = PIECES[k][0]
-            nc.vector.tensor_tensor(
-                woven_out(z), woven(damping[k][:, :, c0:c1]),
-                woven(load_all[:, :, m0 + c0 : m0 + c1]), ALU.mult,
-            )
-
-        def quantize_z(z, width):
+        def quantize_z(z):
+            width = z.shape[1]
             z_c = ring.tile([P, width], U32, name="z_c", align_bytes=64, bufs=3)
             z_s = ring.tile([P, width], U8, name="z_s", align_bytes=64, bufs=3)
-            nc.vector.quantize_mx(out=z_c[:].bitcast(FP8X4), scales=z_s[:], in_=z[:].rearrange("p m i -> p (m i)"))
+            nc.vector.quantize_mx(out=z_c[:].bitcast(FP8X4), scales=z_s[:], in_=z.rearrange("p m i -> p (m i)"))
             return z_c, z_s
 
-        def project(z, m0, m1, banks, copy_outs):
-            z_c, z_s = quantize_z(z, m1 - m0)
-            step = N // P // len(copy_outs)
-            for g, copy_out in enumerate(copy_outs):
-                t0, t1 = g * step, (g + 1) * step
-                acc = banks[g]([P, step, m1 - m0])
+        def project(z_q, m0, groups):
+            z_c, z_s = z_q
+            width = z_c.shape[1]
+            for t0, t1, copy in groups:
+                acc = bank(free_banks[len(used) % len(free_banks)], (P, t1 - t0, width))
+                used.append(acc)
                 for t in range(t0, t1):
-                    w, n0 = divmod(t * P, WO_PIECE)
+                    k, n0 = divmod(t * P, WO_PIECE)
                     nc.tensor.matmul_mx(
-                        out=acc[:, t - t0, :], lhsT=wo_c[w][:, n0 : n0 + P].bitcast(FP8X4),
-                        lhsT_scale=wo_s[w][:, n0 : n0 + P],
+                        out=acc[:, t - t0, :], lhsT=wo_c[k][:, n0 : n0 + P].bitcast(FP8X4),
+                        lhsT_scale=wo_s[k][:, n0 : n0 + P],
                         rhs=z_c[:].bitcast(FP8X4), rhs_scale=z_s[:], start=True, stop=True,
                     )
-                result = ring.tile([P, step, m1 - m0], F32, name="result", bufs=12)
-                copy_out(result[:], acc[:])
-                nc.sync.dma_start(out_rows[:, t0:t1, m0:m1], result[:])
+                result = ring.tile([P, t1 - t0, width], F32, name="result", bufs=14)
+                copy(result[:], acc[:])
+                nc.sync.dma_start(out_rows[:, t0:t1, m0 : m0 + width], result[:])
 
-        def x_on(tag):
-            return keep.tile([P, CHUNK], F32, name="held_x", tag=tag, align_bytes=64)[:]
-
-        last_x = keep.tile([P, 3 * CHUNK], F32, name="last_x")
+        late_x = keep.tile([P, 3 * CHUNK], F32, name="late_x")
         for k in range(3):
-            late(PAGES - 1, k, k + 1, last_x[:, PIECES[k][0] : PIECES[k][1]])
-        wo_codes = keep.tile([P, 2 * WO_PIECE], U32, name="wo_codes", tag="page1", align_bytes=64)
-        for w in range(2):
-            quantize_wo(w, wo_codes[:, w * WO_PIECE : (w + 1) * WO_PIECE])
-        late(PAGES - 1, 3, 4, last_x[:, 2 * CHUNK :])
+            late(PAGES - 1, k, k + 1, late_x[:, MOVED[k][0] : MOVED[k][1]])
+        for k in range(2):
+            quantize_wo(k, "wo_c%d" % k)
+        late(PAGES - 1, 3, 4, late_x[:, 2 * CHUNK :])
         late(PAGES - 2, 3, 5, h[:])
-        copy = nc.scalar.copy
-        z = z_tile(0)
-        damp(0, z[:], 0, P)
-        quantize_wo(2, keep.tile([P, WO_PIECE], U32, name="wo_last", tag="last_e3_0", align_bytes=64)[:])
-        project(z, *PIECES[0], (long_bank, short_bank), (copy, copy))
-        z = z_tile(1)
-        damp(1, z[:], 0, P)
-        late(PAGES - 1, 4, 5, x_on("z0"))
-        project(z, *PIECES[1], (long_bank, short_bank), (copy, copy))
-        three = (long_bank, short_bank, long_bank)
-        z2, z3 = z_tile(2), z_tile(3)
-        damp(2, z2[:], 0, CHUNK)
-        damp(3, z3[:, :P, :], 0, P)
-        project(z2, *PIECES[2], three, (copy, copy, copy))
-        damp(3, z3[:, P:, :], P, CHUNK)
-        ends = [keep.tile([P, P, PACK], BF16, name="z_end%d" % k, align_bytes=64) for k in range(2)]
-        damp(4, ends[0][:], 0, P)
-        project(z3, *PIECES[3], three, (copy, copy, copy))
-        damp(4, ends[1][:], P, CHUNK)
-        project(ends[0], M - CHUNK, M - P, (long_bank, short_bank), (copy, nc.vector.tensor_copy))
-        project(ends[1], M - P, M, (long_bank, short_bank), (copy, nc.vector.tensor_copy))
+        by_scalar, by_vector = nc.scalar.copy, nc.vector.tensor_copy
+        pairs = [(t, t + 2, by_scalar) for t in range(0, N // P, 2)]
+
+        z = on("z0", [P, P, PACK], BF16)
+        damp(z[:], damping[0], MOVED[0][0])
+        quantize_wo(2, "late_e30")
+        project(quantize_z(z[:]), MOVED[0][0], [(0, 1, by_scalar), (1, 3, by_scalar), (3, 6, by_scalar)])
+        z = on("wo_bf", [P, P, PACK], BF16)
+        damp(z[:], damping[1], MOVED[1][0])
+        late(PAGES - 1, 4, 5, on("z0", [P, CHUNK], F32)[:])
+        project(quantize_z(z[:]), MOVED[1][0], [(0, 3, by_scalar), (3, 6, by_scalar)])
+        for k in (2, 3, 4):
+            z = on("page3", [P, CHUNK, PACK], BF16)
+            damp(z[:], damping[k], MOVED[k][0])
+            project(quantize_z(z[:]), MOVED[k][0], pairs if k < 4 else [pairs[0], (2, 4, by_vector), pairs[2]])

@@ -62,7 +62,7 @@ def tile_list_latency_envelopes_kernel(
         outer_bank, lower_bank, upper_bank = 0, 1, 2
         sum_banks = (3, 4)
 
-        depths = {"pos2": 3, "neg1": 3, "neg3": 3, "below": 5, "above": 4, "h": 4}
+        depths = {"pos2": 3, "neg1": 3, "neg3": 3, "below": 4, "above": 5, "h": 4}
 
         def unit_tile(kind):
             return ring.tile([P, BANK], F32, name=kind, bufs=depths[kind], align_bytes=64)
@@ -98,7 +98,7 @@ def tile_list_latency_envelopes_kernel(
         w1_raw, w2_c, w3_c = {}, {}, {}
 
         def load_w1(a, b0, b1):
-            raw = keep.tile([P, PACK, (b1 - b0) * P], F32, name="w1_raw%d_%d" % (b0, a))
+            raw = on("w1_raw%d_%d" % (b0, a), [P, PACK, (b1 - b0) * P], F32)
             nc.sync.dma_start(raw[:], w1_rows[a][:, :, b0 * P : b1 * P])
             for b in range(b0, b1):
                 w1_raw[b, a] = raw[:, :, (b - b0) * P : (b - b0 + 1) * P]
@@ -128,16 +128,23 @@ def tile_list_latency_envelopes_kernel(
         load_packed(0, 1)
         load_table_words(0)
         load_scale_rows(lambda row: w2_s[row:P:QUADRANT, :, :], w2_scales)
-        load_w1(0, 0, 1)
         load_table_words(1)
-        load_w1(1, 0, 1)
         load_scale_rows(lambda row: w3_s[row:P:QUADRANT, :, :], w3_scales)
+        load_w1(0, 0, 1)
         v_s = on("v_s", [P, S], U8)
         nc.vector.tensor_copy(v_s[:], tab_s[:].indirect(idx1[:]))
         plane_span = P - QUADRANT + PLANE_ROWS
-        nc.sync.dma_start(
-            v_s1[0:plane_span, :].bitcast(I32), v_s[SECOND_PLANE : SECOND_PLANE + plane_span, :].bitcast(I32)
-        )
+
+        def move_plane(half):
+            columns = slice(half * BANK, (half + 1) * BANK)
+            nc.sync.dma_start(
+                v_s1[0:plane_span, columns].bitcast(I32),
+                v_s[SECOND_PLANE : SECOND_PLANE + plane_span, columns].bitcast(I32),
+            )
+
+        move_plane(0)
+        load_w1(1, 0, 1)
+        move_plane(1)
         planes = [v_s[:], v_s1[:]]
         for a in range(PASSES):
             load_w1(a, 1, 2)
@@ -171,10 +178,9 @@ def tile_list_latency_envelopes_kernel(
             scales = on("w1_s%d" % b, [P, PASSES * P], U8)
             step = P if b < 2 else W1_CAST
             for a in range(PASSES):
+                cast = nc.vector.tensor_copy if (b, a) == (0, 1) else nc.scalar.copy
                 for c0 in range(0, P, step):
-                    nc.scalar.copy(
-                        out=woven_out(rounded[:, a, c0 : c0 + step, :]), in_=woven(w1_raw[b, a][:, :, c0 : c0 + step])
-                    )
+                    cast(woven_out(rounded[:, a, c0 : c0 + step, :]), woven(w1_raw[b, a][:, :, c0 : c0 + step]))
                 w1_c[b, a] = codes[:, a * P : (a + 1) * P].bitcast(FP8X4)
                 w1_s[b, a] = scales[:, a * P : (a + 1) * P]
                 if b == 0:
@@ -260,16 +266,11 @@ def tile_list_latency_envelopes_kernel(
 
         def envelope(u):
             h = unit_tile("h")
-            nc.scalar.copy(h[:], turned_sum(below[u], above[u], sum_banks[u % 2])[:])
+            nc.scalar.copy(h[:], turned_sum(above[u], below[u], sum_banks[u % 2])[:])
             return h
 
-        middle = on("tab_w0", [P, 2, PACK, CHUNK], F32)
         damping = [
-            keep.tile([P, PACK, P], F32, name="damping0")[:],
-            keep.tile([P, PACK, P], F32, name="damping1")[:],
-            middle[:, 0, :, :],
-            middle[:, 1, :, :],
-            keep.tile([P, PACK, CHUNK], F32, name="damping4")[:],
+            on("tab_w0" if k == 2 else "damping%d" % k, [P, PACK, m1 - m0], F32)[:] for k, (m0, m1) in enumerate(MOVED)
         ]
 
         def fetch(b, m0, m1, x):
@@ -287,7 +288,7 @@ def tile_list_latency_envelopes_kernel(
         e3_1, e1_1 = e3(1, upper_bank), e1(1, sum_banks[0])
 
         def bounds(u, e1_u, e3_u, high):
-            low = unit_tile("neg3")
+            low = on("w1_raw0_%d" % (1 - u), [P, BANK], F32)
             nc.vector.tensor_tensor(low[:], e3_u[:], pos2[u][:], ALU.min)
             nc.vector.tensor_tensor(high[:], e1_u[:], pos2[u][:], ALU.max)
             return high, low
@@ -327,26 +328,28 @@ def tile_list_latency_envelopes_kernel(
             if u > 2:
                 b, half = units[u - 3]
                 m0, m1 = half * BANK, (half + 1) * BANK
-                fetched[u] = (b, m0, m1, below[u][:, : m1 - m0])
+                fetched[u] = (b, m0, m1, above[u][:, : m1 - m0])
                 fetch(*fetched[u])
             put(u, h)
             if u - EXP_LAG in fetched:
                 x = fetched[u - EXP_LAG]
-                spread(*x, above[u][:, : x[2] - x[1]])
-        spread(*fetched[last - 1], below[last - 2][:])
+                spread(*x, below[u][:, : x[2] - x[1]])
+        spread(*fetched[last - 1], above[last - 2][:])
         wo_bf = on("wo_bf", [P, N, PACK], BF16)
         for n0 in range(0, N, WO_CAST):
             nc.scalar.copy(out=woven_out(wo_bf[:, n0 : n0 + WO_CAST, :]), in_=woven(wo_raw[:, :, n0 : n0 + WO_CAST]))
         spread(*fetched[last], unit_tile("neg1")[:])
         wo_c, wo_s = {}, {}
 
-        def quantize_wo(k, tag):
-            wo_c[k] = on(tag, [P, WO_PIECE], U32)
-            wo_s[k] = on("wo_s%d" % k, [P, WO_PIECE], U8)
+        def quantize_wo(n0, n1, tag):
+            codes = on(tag, [P, n1 - n0], U32)
+            scales = on("wo_s%d" % n0, [P, n1 - n0], U8)
             nc.vector.quantize_mx(
-                out=wo_c[k][:].bitcast(FP8X4), scales=wo_s[k][:],
-                in_=wo_bf[:, WO_PIECE * k : WO_PIECE * (k + 1), :].rearrange("p n i -> p (n i)"),
+                out=codes[:].bitcast(FP8X4), scales=scales[:], in_=wo_bf[:, n0:n1, :].rearrange("p n i -> p (n i)")
             )
+            for n in range(n0, n1, P):
+                wo_c[n // P] = codes[:, n - n0 : n - n0 + P].bitcast(FP8X4)
+                wo_s[n // P] = scales[:, n - n0 : n - n0 + P]
 
         def late(b, k, k1, x):
             m0, m1 = MOVED[k][0], MOVED[k1 - 1][1]
@@ -375,10 +378,8 @@ def tile_list_latency_envelopes_kernel(
                 acc = bank(free_banks[len(used) % len(free_banks)], (P, t1 - t0, width))
                 used.append(acc)
                 for t in range(t0, t1):
-                    k, n0 = divmod(t * P, WO_PIECE)
                     nc.tensor.matmul_mx(
-                        out=acc[:, t - t0, :], lhsT=wo_c[k][:, n0 : n0 + P].bitcast(FP8X4),
-                        lhsT_scale=wo_s[k][:, n0 : n0 + P],
+                        out=acc[:, t - t0, :], lhsT=wo_c[t], lhsT_scale=wo_s[t],
                         rhs=z_c[:].bitcast(FP8X4), rhs_scale=z_s[:], start=True, stop=True,
                     )
                 result = ring.tile([P, t1 - t0, width], F32, name="result", bufs=14)
@@ -386,24 +387,23 @@ def tile_list_latency_envelopes_kernel(
                 nc.sync.dma_start(out_rows[:, t0:t1, m0 : m0 + width], result[:])
 
         late_x = keep.tile([P, 3 * CHUNK], F32, name="late_x")
-        for k in range(3):
+        for k in range(4):
             late(PAGES - 1, k, k + 1, late_x[:, MOVED[k][0] : MOVED[k][1]])
-        for k in range(2):
-            quantize_wo(k, "wo_c%d" % k)
-        late(PAGES - 1, 3, 4, late_x[:, 2 * CHUNK :])
         late(PAGES - 2, 3, 5, h[:])
         by_scalar, by_vector = nc.scalar.copy, nc.vector.tensor_copy
         pairs = [(t, t + 2, by_scalar) for t in range(0, N // P, 2)]
 
         z = on("z0", [P, P, PACK], BF16)
         damp(z[:], damping[0], MOVED[0][0])
-        quantize_wo(2, "late_e30")
-        project(quantize_z(z[:]), MOVED[0][0], [(0, 1, by_scalar), (1, 3, by_scalar), (3, 6, by_scalar)])
-        z = on("wo_bf", [P, P, PACK], BF16)
+        quantize_wo(0, WO_PIECE, "late_e30")
+        z_q = quantize_z(z[:])
+        quantize_wo(WO_PIECE, N, "late_e31")
+        project(z_q, MOVED[0][0], pairs)
+        z = on("z1", [P, P, PACK], BF16)
         damp(z[:], damping[1], MOVED[1][0])
         late(PAGES - 1, 4, 5, on("z0", [P, CHUNK], F32)[:])
         project(quantize_z(z[:]), MOVED[1][0], [(0, 3, by_scalar), (3, 6, by_scalar)])
-        for k in (2, 3, 4):
-            z = on("page3", [P, CHUNK, PACK], BF16)
+        for k, place in ((2, "page3"), (3, "tab_w0"), (4, "damping3")):
+            z = on(place, [P, CHUNK, PACK], BF16)
             damp(z[:], damping[k], MOVED[k][0])
             project(quantize_z(z[:]), MOVED[k][0], pairs if k < 4 else [pairs[0], (2, 4, by_vector), pairs[2]])

@@ -28,11 +28,10 @@ PAGES = H // P
 BANK = 512
 BANKS = 8
 CHUNK = 256
-WO_PIECE = 256
+WO_FIRST = 256
 WO_CAST = 128
-W1_CAST = 128
 EXP_LAG = 2
-MOVED = [(0, 128), (128, 256), (256, 512), (512, 768), (768, 1024)]
+PIECES = [(0, P), (P, CHUNK), (CHUNK, 2 * CHUNK), (2 * CHUNK, 3 * CHUNK), (3 * CHUNK, M)]
 
 
 def woven(planes):
@@ -61,6 +60,7 @@ def tile_list_latency_envelopes_kernel(
 
         outer_bank, lower_bank, upper_bank = 0, 1, 2
         sum_banks = (3, 4)
+        spare_banks = (5, 6, 7)
 
         depths = {"pos2": 3, "neg1": 3, "neg3": 3, "below": 4, "above": 5, "h": 4}
 
@@ -176,11 +176,9 @@ def tile_list_latency_envelopes_kernel(
             rounded = on(("page0", "page1", "page3", "w1_bf3")[b], [P, PASSES, P, PACK], BF16)
             codes = on("w1_c%d" % b, [P, PASSES * P], U32)
             scales = on("w1_s%d" % b, [P, PASSES * P], U8)
-            step = P if b < 2 else W1_CAST
             for a in range(PASSES):
                 cast = nc.vector.tensor_copy if (b, a) == (0, 1) else nc.scalar.copy
-                for c0 in range(0, P, step):
-                    cast(woven_out(rounded[:, a, c0 : c0 + step, :]), woven(w1_raw[b, a][:, :, c0 : c0 + step]))
+                cast(woven_out(rounded[:, a, :, :]), woven(w1_raw[b, a]))
                 w1_c[b, a] = codes[:, a * P : (a + 1) * P].bitcast(FP8X4)
                 w1_s[b, a] = scales[:, a * P : (a + 1) * P]
                 if b == 0:
@@ -222,14 +220,14 @@ def tile_list_latency_envelopes_kernel(
         def e3(u, k):
             return estimate(u, k, w3_c, lambda b, a: w3_s[:, a, b * P : (b + 1) * P])
 
-        def turn(acc, tile, start=True, stop=True):
-            nc.tensor.matmul(acc, tile, ident[:], start=start, stop=stop, is_transpose=True)
-
         def turned_sum(first, second, k):
             acc = bank(k)
             for c0 in range(0, BANK, P):
-                turn(acc[:, c0 : c0 + P], first[:, c0 : c0 + P], stop=False)
-                turn(acc[:, c0 : c0 + P], second[:, c0 : c0 + P], start=False)
+                for tile in (first, second):
+                    nc.tensor.matmul(
+                        acc[:, c0 : c0 + P], tile[:, c0 : c0 + P], ident[:],
+                        start=tile is first, stop=tile is second, is_transpose=True,
+                    )
             return acc
 
         def copy_out(tile, acc, func, scale):
@@ -255,7 +253,7 @@ def tile_list_latency_envelopes_kernel(
 
         def negate_e3(u):
             tile = on("page3", [P, BANK], F32) if u == 2 else unit_tile("neg3")
-            neg3[u] = copy_out(tile, e3(u, 5 if u == 3 else outer_bank), ACT.Copy, -1.0)
+            neg3[u] = copy_out(tile, e3(u, spare_banks[0] if u == 3 else outer_bank), ACT.Copy, -1.0)
 
         def lower_part(u):
             first, second = (neg3, pos2) if u == 2 else (pos2, neg3)
@@ -270,21 +268,40 @@ def tile_list_latency_envelopes_kernel(
             return h
 
         damping = [
-            on("tab_w0" if k == 2 else "damping%d" % k, [P, PACK, m1 - m0], F32)[:] for k, (m0, m1) in enumerate(MOVED)
+            on("tab_w0" if k == 2 else "damping%d" % k, [P, PACK, m1 - m0], F32)[:] for k, (m0, m1) in enumerate(PIECES[:-1])
         ]
+        steps = CHUNK // P
+        turned = on("tab_w1", [P, steps, PACK, P], F32)
+
+        def turn_in(b0, xs, k):
+            acc = bank(k, (P, steps, len(xs), P))
+            for n, x in enumerate(xs):
+                for s in range(steps):
+                    nc.tensor.transpose(acc[:, s, n, :], x[:, s * P : (s + 1) * P], ident[:])
+            nc.scalar.activation(
+                turned[:, :, :, QUADRANT * b0 : QUADRANT * (b0 + len(xs))],
+                acc[:].rearrange("m s b (q i) -> m s i (b q)", i=PACK), ACT.Exp, scale=-1.0,
+            )
 
         def fetch(b, m0, m1, x):
             nc.vector.tensor_copy(x, pages[b][:].indirect(entries(idx3, m0, m1)))
 
         def spread(b, m0, m1, x, e):
+            if m1 == M:
+                m1 -= CHUNK
+                x, rest, e = x[:, :CHUNK], x[:, CHUNK:], e[:, :CHUNK]
+            else:
+                rest = None
             nc.scalar.activation(e, x, ACT.Exp, scale=-1.0)
-            for k, (p0, p1) in enumerate(MOVED):
+            if rest is not None:
+                turn_in(b, [rest], spare_banks[2])
+            for k, (p0, p1) in enumerate(PIECES[:-1]):
                 if m0 <= p0 and p1 <= m1:
                     nc.sync.dma_start(damping[k][QUADRANT * b : QUADRANT * (b + 1), :, :], e[:, p0 - m0 : p1 - m0])
 
         copy_e2(0, upper_bank)
-        e3_0, e1_0 = e3(0, 5), e1(0, 6)
-        copy_e2(1, 7)
+        e3_0, e1_0 = e3(0, spare_banks[0]), e1(0, spare_banks[1])
+        copy_e2(1, spare_banks[2])
         e3_1, e1_1 = e3(1, upper_bank), e1(1, sum_banks[0])
 
         def bounds(u, e1_u, e3_u, high):
@@ -318,7 +335,7 @@ def tile_list_latency_envelopes_kernel(
                 negate_e3(u + 1)
             upper_part(u)
             if u < last:
-                copy_e2(u + 1, 6 if u == 2 else lower_bank)
+                copy_e2(u + 1, spare_banks[1] if u == 2 else lower_bank)
                 if u in (2, 4):
                     quantize_w1(units[u + 2][0])
                 if u == 2:
@@ -327,18 +344,17 @@ def tile_list_latency_envelopes_kernel(
             h = envelope(u)
             if u > 2:
                 b, half = units[u - 3]
-                m0, m1 = half * BANK, (half + 1) * BANK
-                fetched[u] = (b, m0, m1, above[u][:, : m1 - m0])
+                fetched[u] = (b, half * BANK, (half + 1) * BANK, above[u][:])
                 fetch(*fetched[u])
             put(u, h)
             if u - EXP_LAG in fetched:
-                x = fetched[u - EXP_LAG]
-                spread(*x, below[u][:, : x[2] - x[1]])
+                spread(*fetched[u - EXP_LAG], below[u][:])
         spread(*fetched[last - 1], above[last - 2][:])
         wo_bf = on("wo_bf", [P, N, PACK], BF16)
         for n0 in range(0, N, WO_CAST):
+            if n0 == BANK:
+                spread(*fetched[last], unit_tile("neg1")[:])
             nc.scalar.copy(out=woven_out(wo_bf[:, n0 : n0 + WO_CAST, :]), in_=woven(wo_raw[:, :, n0 : n0 + WO_CAST]))
-        spread(*fetched[last], unit_tile("neg1")[:])
         wo_c, wo_s = {}, {}
 
         def quantize_wo(n0, n1, tag):
@@ -351,59 +367,77 @@ def tile_list_latency_envelopes_kernel(
                 wo_c[n // P] = codes[:, n - n0 : n - n0 + P].bitcast(FP8X4)
                 wo_s[n // P] = scales[:, n - n0 : n - n0 + P]
 
-        def late(b, k, k1, x):
-            m0, m1 = MOVED[k][0], MOVED[k1 - 1][1]
+        def late(b, k0, k1, x):
+            m0, m1 = PIECES[k0][0], PIECES[k1 - 1][1]
             fetch(b, m0, m1, x)
-            spread(b, m0, m1, x, on("late_e%d%d" % (b, k), [P, m1 - m0], F32)[:])
+            spread(b, m0, m1, x, on("late_e%d%d" % (b, k0), [P, m1 - m0], F32)[:])
 
-        def damp(z, factor, m0):
-            width = factor.shape[2]
-            nc.vector.tensor_tensor(woven_out(z), woven(factor), woven(load_sb[:, :, m0 : m0 + width]), ALU.mult)
+        def damp(k, tag):
+            m0, m1 = PIECES[k]
+            z = on(tag, [P, m1 - m0, PACK], BF16)
+            nc.vector.tensor_tensor(woven_out(z[:]), woven(damping[k]), woven(load_sb[:, :, m0:m1]), ALU.mult)
+            return z
 
         out_rows = out.rearrange("(t p) m -> p t m", p=P)
-        free_banks = list(range(BANKS))
-        used = []
+        result_banks = list(range(3, BANKS))
+        filled = []
 
         def quantize_z(z):
             width = z.shape[1]
             z_c = ring.tile([P, width], U32, name="z_c", align_bytes=64, bufs=3)
             z_s = ring.tile([P, width], U8, name="z_s", align_bytes=64, bufs=3)
-            nc.vector.quantize_mx(out=z_c[:].bitcast(FP8X4), scales=z_s[:], in_=z.rearrange("p m i -> p (m i)"))
+            nc.vector.quantize_mx(out=z_c[:].bitcast(FP8X4), scales=z_s[:], in_=z[:].rearrange("p m i -> p (m i)"))
             return z_c, z_s
 
-        def project(z_q, m0, groups):
+        def project(z_q, k, groups):
             z_c, z_s = z_q
-            width = z_c.shape[1]
+            m0, m1 = PIECES[k]
             for t0, t1, copy in groups:
-                acc = bank(free_banks[len(used) % len(free_banks)], (P, t1 - t0, width))
-                used.append(acc)
+                acc = bank(result_banks[len(filled) % len(result_banks)], (P, t1 - t0, m1 - m0))
+                filled.append(acc)
                 for t in range(t0, t1):
                     nc.tensor.matmul_mx(
                         out=acc[:, t - t0, :], lhsT=wo_c[t], lhsT_scale=wo_s[t],
                         rhs=z_c[:].bitcast(FP8X4), rhs_scale=z_s[:], start=True, stop=True,
                     )
-                result = ring.tile([P, t1 - t0, width], F32, name="result", bufs=14)
+                result = ring.tile([P, t1 - t0, m1 - m0], F32, name="result", bufs=14)
                 copy(result[:], acc[:])
-                nc.sync.dma_start(out_rows[:, t0:t1, m0 : m0 + width], result[:])
+                nc.sync.dma_start(out_rows[:, t0:t1, m0:m1], result[:])
 
         late_x = keep.tile([P, 3 * CHUNK], F32, name="late_x")
         for k in range(4):
-            late(PAGES - 1, k, k + 1, late_x[:, MOVED[k][0] : MOVED[k][1]])
+            late(PAGES - 1, k, k + 1, late_x[:, PIECES[k][0] : PIECES[k][1]])
         late(PAGES - 2, 3, 5, h[:])
         by_scalar, by_vector = nc.scalar.copy, nc.vector.tensor_copy
         pairs = [(t, t + 2, by_scalar) for t in range(0, N // P, 2)]
 
-        z = on("z0", [P, P, PACK], BF16)
-        damp(z[:], damping[0], MOVED[0][0])
-        quantize_wo(0, WO_PIECE, "late_e30")
-        z_q = quantize_z(z[:])
-        quantize_wo(WO_PIECE, N, "late_e31")
-        project(z_q, MOVED[0][0], pairs)
-        z = on("z1", [P, P, PACK], BF16)
-        damp(z[:], damping[1], MOVED[1][0])
-        late(PAGES - 1, 4, 5, on("z0", [P, CHUNK], F32)[:])
-        project(quantize_z(z[:]), MOVED[1][0], [(0, 3, by_scalar), (3, 6, by_scalar)])
-        for k, place in ((2, "page3"), (3, "tab_w0"), (4, "damping3")):
-            z = on(place, [P, CHUNK, PACK], BF16)
-            damp(z[:], damping[k], MOVED[k][0])
-            project(quantize_z(z[:]), MOVED[k][0], pairs if k < 4 else [pairs[0], (2, 4, by_vector), pairs[2]])
+        z = damp(0, "z0")
+        quantize_wo(0, WO_FIRST, "late_e30")
+        z_q = quantize_z(z)
+        quantize_wo(WO_FIRST, 2 * WO_FIRST, "late_e31")
+        project(z_q, 0, pairs[:2])
+        z = damp(1, "z1")
+        quantize_wo(2 * WO_FIRST, N, "z0")
+        project(z_q, 0, pairs[2:])
+        project(quantize_z(z), 1, [(0, 3, by_scalar), (3, 6, by_scalar)])
+        z = damp(2, "wo_bf")
+        x = on("z1", [P, CHUNK], F32)
+        fetch(PAGES - 1, *PIECES[4], x[:])
+        z_q = quantize_z(z)
+        project(z_q, 2, pairs[:1])
+        turn_in(PAGES - 1, [x[:]], 0)
+        project(z_q, 2, pairs[1:])
+        z_q = quantize_z(damp(3, "page3"))
+        back = []
+        for s in range(steps):
+            back.append(bank(1 + s, (P, PACK, P)))
+            for i in range(PACK):
+                nc.tensor.transpose(back[s][:, i, :], turned[:, s, i, :], ident[:])
+        project(z_q, 3, pairs)
+        z = on("z4", [P, CHUNK, PACK], BF16)
+        for s in range(steps):
+            m0 = PIECES[4][0] + s * P
+            nc.vector.tensor_tensor(
+                woven_out(z[:, s * P : (s + 1) * P, :]), woven(back[s][:]), woven(load_sb[:, :, m0 : m0 + P]), ALU.mult
+            )
+        project(quantize_z(z), 4, [pairs[0], (2, 4, by_vector), pairs[2]])

@@ -389,7 +389,7 @@ def tile_list_latency_envelopes_kernel(
             nc.vector.quantize_mx(out=z_c[:].bitcast(FP8X4), scales=z_s[:], in_=z[:].rearrange("p m i -> p (m i)"))
             return z_c, z_s
 
-        def project(z_q, k, groups):
+        def project(z_q, k, groups, tag=None):
             z_c, z_s = z_q
             m0, m1 = PIECES[k]
             for t0, t1, copy in groups:
@@ -400,21 +400,21 @@ def tile_list_latency_envelopes_kernel(
                         out=acc[:, t - t0, :], lhsT=wo_c[t], lhsT_scale=wo_s[t],
                         rhs=z_c[:].bitcast(FP8X4), rhs_scale=z_s[:], start=True, stop=True,
                     )
-                result = ring.tile([P, t1 - t0, m1 - m0], F32, name="result", bufs=14)
+                shape = [P, t1 - t0, m1 - m0]
+                result = on(tag, shape, F32) if tag else ring.tile(shape, F32, name="result", bufs=13)
                 copy(result[:], acc[:])
                 nc.sync.dma_start(out_rows[:, t0:t1, m0:m1], result[:])
 
-        late_x = keep.tile([P, 3 * CHUNK], F32, name="late_x")
         for k in range(4):
-            late(PAGES - 1, k, k + 1, late_x[:, PIECES[k][0] : PIECES[k][1]])
-        late(PAGES - 2, 3, 5, h[:])
+            late(PAGES - 1, k, k + 1, on("late_x%d" % k, [P, PIECES[k][1] - PIECES[k][0]], F32)[:])
+        late(PAGES - 2, 3, 4, h[:, :CHUNK])
+        quantize_wo(0, WO_FIRST, "late_x0")
         by_scalar, by_vector = nc.scalar.copy, nc.vector.tensor_copy
         pairs = [(t, t + 2, by_scalar) for t in range(0, N // P, 2)]
 
         z = damp(0, "z0")
-        quantize_wo(0, WO_FIRST, "late_e30")
+        quantize_wo(WO_FIRST, 2 * WO_FIRST, "late_e30")
         z_q = quantize_z(z)
-        quantize_wo(WO_FIRST, 2 * WO_FIRST, "late_e31")
         project(z_q, 0, pairs[:2])
         z = damp(1, "z1")
         quantize_wo(2 * WO_FIRST, N, "z0")
@@ -423,17 +423,23 @@ def tile_list_latency_envelopes_kernel(
         z = damp(2, "wo_bf")
         x = on("z1", [P, CHUNK], F32)
         fetch(PAGES - 1, *PIECES[4], x[:])
-        z_q = quantize_z(z)
-        project(z_q, 2, pairs[:1])
         turn_in(PAGES - 1, [x[:]], 0)
-        project(z_q, 2, pairs[1:])
-        z_q = quantize_z(damp(3, "page3"))
+        z_q = quantize_z(z)
+        x = on("page3", [P, CHUNK], F32)
+        fetch(PAGES - 2, *PIECES[4], x[:])
+        project(z_q, 2, pairs[:1])
+        turn_in(PAGES - 2, [x[:]], 2)
+        project(z_q, 2, pairs[1:2])
+        z_next = quantize_z(damp(3, "tab_w0"))
+        project(z_q, 2, [(4, 6, by_vector)], "tab_w0")
         back = []
         for s in range(steps):
-            back.append(bank(1 + s, (P, PACK, P)))
+            back.append(bank(s, (P, PACK, P)))
             for i in range(PACK):
                 nc.tensor.transpose(back[s][:, i, :], turned[:, s, i, :], ident[:])
-        project(z_q, 3, pairs)
+            if s == 0:
+                project(z_next, 3, pairs[:1])
+        project(z_next, 3, pairs[1:])
         z = on("z4", [P, CHUNK, PACK], BF16)
         for s in range(steps):
             m0 = PIECES[4][0] + s * P

@@ -26,12 +26,11 @@ SECOND_PLANE = 16
 PASSES = K // (P * PACK)
 PAGES = H // P
 BANK = 512
-BANKS = 8
 CHUNK = 256
-WO_FIRST = 256
-WO_CAST = 128
-EXP_LAG = 2
-PIECES = [(0, P), (P, CHUNK), (CHUNK, 2 * CHUNK), (2 * CHUNK, 3 * CHUNK), (3 * CHUNK, M)]
+WO_RAW_BYTES = 4 * PACK * N
+TURNED_BYTES = 4 * 2 * PACK * P
+PLACES = {"rounded": 0, "h": 960, "above": 3072, "codes": 3072, "x": 3584, "x2": 4608}
+REGION = 5632
 
 
 def woven(planes):
@@ -49,7 +48,7 @@ def tile_list_latency_envelopes_kernel(
     nc = tc.nc
     with ExitStack() as ctx:
         keep = ctx.enter_context(tc.tile_pool(name="keep", bufs=1))
-        ring = ctx.enter_context(tc.tile_pool(name="ring", bufs=2))
+        shared = ctx.enter_context(tc.tile_pool(name="shared", bufs=1))
         psum = ctx.enter_context(tc.psum_pool(name="psum", bufs=1))
 
         def on(tag, shape, dtype):
@@ -58,14 +57,9 @@ def tile_list_latency_envelopes_kernel(
         def bank(k, shape=(P, BANK)):
             return psum.tile(list(shape), F32, name="bank", tag="bank%d" % k)
 
-        outer_bank, lower_bank, upper_bank = 0, 1, 2
-        sum_banks = (3, 4)
-        spare_banks = (5, 6, 7)
-
-        depths = {"pos2": 3, "neg1": 3, "neg3": 3, "below": 4, "above": 5, "h": 4}
-
-        def unit_tile(kind):
-            return ring.tile([P, BANK], F32, name=kind, bufs=depths[kind], align_bytes=64)
+        def placed(u, place, shape, dtype):
+            offset = WO_RAW_BYTES + TURNED_BYTES + u * REGION + PLACES[place]
+            return shared.tile(shape, dtype, name="%s%d_%d" % (place, u, shape[1]), align_bytes=64, offset=offset)
 
         idx1 = keep.tile([P, S // STRIPE], U16, name="idx1")
         idx2 = keep.tile([P, S // STRIPE], U16, name="idx2")
@@ -88,8 +82,11 @@ def tile_list_latency_envelopes_kernel(
         pages = {}
 
         def open_page(b):
-            pages[b] = on("page%d" % b, [P, T2], F32)
+            pages[b] = on("w1_bf1" if b == 3 else "page%d" % b, [P, T2], F32)
             nc.gpsimd.memset(pages[b][:].bitcast(I32), 0)
+
+        for b in range(PAGES - 1):
+            open_page(b)
 
         tab_w = [on("tab_w%d" % a, [P, T], I32) for a in range(PASSES)]
         w1_rows = w1.rearrange("(a p i) c -> a p i c", a=PASSES, i=PACK)
@@ -104,7 +101,7 @@ def tile_list_latency_envelopes_kernel(
                 w1_raw[b, a] = raw[:, :, (b - b0) * P : (b - b0 + 1) * P]
 
         def load_packed(b0, b1):
-            words = on("page1" if b0 == 0 else "w2_c%d" % b0, [P, PASSES, (b1 - b0) * P], U32)
+            words = on("w1_bf1" if b0 == 0 else "w2_c%d" % b0, [P, PASSES, (b1 - b0) * P], U32)
             nc.sync.dma_start(words[:].bitcast(I32), w2_rows[:, :, 4 * b0 * P : 4 * b1 * P].bitcast(I32))
             nibbles = on("w3_c%d" % b0, [P, PASSES, 2 * (b1 - b0) * P], U8)
             nc.sync.dma_start(nibbles[:].bitcast(I32), w3_rows[:, :, 2 * b0 * P : 2 * b1 * P].bitcast(I32))
@@ -152,15 +149,18 @@ def tile_list_latency_envelopes_kernel(
         load_packed(1, 2)
         nc.sync.dma_start(wgs_sb[0][:], wgs[:, :BANK])
         nc.sync.dma_start(idx2[:], offs2)
+        for a in range(PASSES):
+            load_w1(a, 2, 3)
         nc.sync.dma_start(wgs_sb[1][:], wgs[:, BANK:])
         for a in range(PASSES):
-            load_w1(a, 2, PAGES)
+            load_w1(a, 3, PAGES)
         load_packed(2, PAGES)
         nc.sync.dma_start(idx3[:], offs3)
-        wo_raw = keep.tile([P, PACK, N], F32, name="wo_raw")
+        wo_raw = shared.tile([P, PACK, N], F32, name="wo_raw", align_bytes=64, offset=0)
         nc.sync.dma_start(wo_raw[:], wo.rearrange("(p i) n -> p i n", i=PACK))
+        load_rows = load.rearrange("(p i) m -> p i m", i=PACK)
         load_sb = keep.tile([P, PACK, M], F32, name="load_sb")
-        nc.sync.dma_start(load_sb[:], load.rearrange("(p i) m -> p i m", i=PACK))
+        nc.sync.dma_start(load_sb[:], load_rows)
 
         v_w = {}
 
@@ -172,30 +172,37 @@ def tile_list_latency_envelopes_kernel(
 
         w1_c, w1_s = {}, {}
 
-        def quantize_w1(b):
-            rounded = on(("page0", "page1", "page3", "w1_bf3")[b], [P, PASSES, P, PACK], BF16)
-            codes = on("w1_c%d" % b, [P, PASSES * P], U32)
-            scales = on("w1_s%d" % b, [P, PASSES * P], U8)
-            for a in range(PASSES):
-                cast = nc.vector.tensor_copy if (b, a) == (0, 1) else nc.scalar.copy
-                cast(woven_out(rounded[:, a, :, :]), woven(w1_raw[b, a]))
-                w1_c[b, a] = codes[:, a * P : (a + 1) * P].bitcast(FP8X4)
-                w1_s[b, a] = scales[:, a * P : (a + 1) * P]
-                if b == 0:
-                    nc.vector.quantize_mx(
-                        out=w1_c[b, a], scales=w1_s[b, a], in_=rounded[:, a, :, :].rearrange("p c i -> p (c i)")
-                    )
-            if b > 0:
-                nc.vector.quantize_mx(
-                    out=codes[:].bitcast(FP8X4), scales=scales[:], in_=rounded[:].rearrange("p a c i -> p (a c i)")
-                )
+        def quantize_w1(b, passes, tag, cast=nc.scalar.copy):
+            a0, count = passes[0], len(passes)
+            rounded = on(tag, [P, count, P, PACK], BF16)
+            codes = on("w1_c%d%d" % (b, a0), [P, count * P], U32)
+            scales = on("w1_s%d%d" % (b, a0), [P, count * P], U8)
+            for n, a in enumerate(passes):
+                cast(woven_out(rounded[:, n, :, :]), woven(w1_raw[b, a]))
+                w1_c[b, a] = codes[:, n * P : (n + 1) * P].bitcast(FP8X4)
+                w1_s[b, a] = scales[:, n * P : (n + 1) * P]
+            nc.vector.quantize_mx(
+                out=codes[:].bitcast(FP8X4), scales=scales[:], in_=rounded[:].rearrange("p a c i -> p (a c i)")
+            )
+
+        def round_beside(u, raw):
+            rounded = placed(u, "rounded", [P, P, PACK], BF16)
+            nc.gpsimd.tensor_scalar(rounded[:], raw.rearrange("p i c -> p c i"), 1.0, 0.0, ALU.mult, ALU.add)
+            return rounded
+
+        def quantize_block(rounded, codes, tag):
+            scales = on(tag, [P, P], U8)
+            nc.vector.quantize_mx(
+                out=codes[:].bitcast(FP8X4), scales=scales[:], in_=rounded[:].rearrange("p c i -> p (c i)")
+            )
+            return codes[:].bitcast(FP8X4), scales[:]
 
         gather_words(0, 0)
-        quantize_w1(0)
+        quantize_w1(0, [0], "w1_bf0")
+        quantize_w1(0, [1], "w1_bf01", nc.vector.tensor_copy)
         gather_words(1, 0)
         gather_words(0, 1)
         gather_words(1, 1)
-        open_page(0)
 
         units = [(b, half) for b in range(PAGES) for half in range(2)]
         last = len(units) - 1
@@ -220,17 +227,18 @@ def tile_list_latency_envelopes_kernel(
         def e3(u, k):
             return estimate(u, k, w3_c, lambda b, a: w3_s[:, a, b * P : (b + 1) * P])
 
-        def turned_sum(first, second, k):
+        def turned_sum(early, late, k):
             acc = bank(k)
-            for c0 in range(0, BANK, P):
-                for tile in (first, second):
+            for tile in (early, late):
+                for c0 in range(0, BANK, P):
                     nc.tensor.matmul(
                         acc[:, c0 : c0 + P], tile[:, c0 : c0 + P], ident[:],
-                        start=tile is first, stop=tile is second, is_transpose=True,
+                        start=tile is early and c0 == 0, stop=tile is late and c0 == BANK - P, is_transpose=True,
                     )
             return acc
 
-        def copy_out(tile, acc, func, scale):
+        def copy_out(tag, acc, func, scale):
+            tile = on(tag, [P, BANK], F32) if isinstance(tag, str) else placed(tag, "above", [P, BANK], F32)
             nc.scalar.activation(tile[:], acc[:], func, scale=scale)
             return tile
 
@@ -240,210 +248,200 @@ def tile_list_latency_envelopes_kernel(
                 pages[b][:].indirect(entries(idx2, half * BANK, (half + 1) * BANK)), h[:], wgs_sb[half][:], ALU.mult
             )
 
+        def fetch(b, m0, m1, x):
+            nc.vector.tensor_copy(x[:], pages[b][:].indirect(entries(idx3, m0, m1)))
+            return x
+
         pos2, neg1, neg3, below, above = {}, {}, {}, {}, {}
+        sum_bank = 2
 
         def copy_e2(u, k):
-            place = {0: "w1_c1", last: "wo_bf"}
-            tile = on(place[u], [P, BANK], F32) if u in place else unit_tile("pos2")
-            pos2[u] = copy_out(tile, e2(u, k), ACT.Copy, 1.0)
-
-        def negate_e1(u):
-            tile = on("w1_bf3", [P, BANK], F32) if u == 3 else unit_tile("neg1")
-            neg1[u] = copy_out(tile, e1(u, outer_bank), ACT.Copy, -1.0)
+            pos2[u] = copy_out({0: "w1_c10", 1: "pos2_first"}.get(u, "pos2_%d" % (u % 2)), e2(u, k), ACT.Copy, 1.0)
 
         def negate_e3(u):
-            tile = on("page3", [P, BANK], F32) if u == 2 else unit_tile("neg3")
-            neg3[u] = copy_out(tile, e3(u, spare_banks[0] if u == 3 else outer_bank), ACT.Copy, -1.0)
+            neg3[u] = copy_out("w1_bf2" if u == 2 else "neg3_%d" % (u % 2), e3(u, 4 if u == 2 else 5), ACT.Copy, -1.0)
+
+        def negate_e1(u):
+            neg1[u] = copy_out("neg1_%d" % (u % 2), e1(u, 6), ACT.Copy, -1.0)
 
         def lower_part(u):
-            first, second = (neg3, pos2) if u == 2 else (pos2, neg3)
-            below[u] = copy_out(unit_tile("below"), turned_sum(first[u], second[u], lower_bank), ACT.Relu, 1.0)
+            below[u] = copy_out("below%d" % u, turned_sum(neg3[u], pos2[u], 0), ACT.Relu, 1.0)
 
         def upper_part(u):
-            above[u] = copy_out(unit_tile("above"), turned_sum(neg1[u], pos2[u], upper_bank), ACT.Relu, -1.0)
+            above[u] = copy_out(u, turned_sum(pos2[u], neg1[u], 1), ACT.Relu, -1.0)
 
-        def envelope(u):
-            h = unit_tile("h")
-            nc.scalar.copy(h[:], turned_sum(above[u], below[u], sum_banks[u % 2])[:])
-            return h
+        moved = {m0: on("moved%d" % m0, [P, PACK, CHUNK], F32) for m0 in range(CHUNK, M, CHUNK)}
 
-        damping = [
-            on("tab_w0" if k == 2 else "damping%d" % k, [P, PACK, m1 - m0], F32)[:] for k, (m0, m1) in enumerate(PIECES[:-1])
-        ]
-        steps = CHUNK // P
-        turned = on("tab_w1", [P, steps, PACK, P], F32)
+        def move(b, m0, x, e):
+            nc.scalar.activation(e[:], x, ACT.Exp, scale=-1.0)
+            for c in range(0, x.shape[1], CHUNK):
+                nc.sync.dma_start(moved[m0 + c][QUADRANT * b : QUADRANT * (b + 1), :, :], e[:, c : c + CHUNK])
 
-        def turn_in(b0, xs, k):
-            acc = bank(k, (P, steps, len(xs), P))
+        turned = shared.tile([P, 2, PACK, P], F32, name="turned", align_bytes=64, offset=WO_RAW_BYTES)
+
+        def turn_in(s, b0, xs, k):
+            acc = bank(k, (P, len(xs), P))
             for n, x in enumerate(xs):
-                for s in range(steps):
-                    nc.tensor.transpose(acc[:, s, n, :], x[:, s * P : (s + 1) * P], ident[:])
+                nc.tensor.transpose(acc[:, n, :], x, ident[:])
             nc.scalar.activation(
-                turned[:, :, :, QUADRANT * b0 : QUADRANT * (b0 + len(xs))],
-                acc[:].rearrange("m s b (q i) -> m s i (b q)", i=PACK), ACT.Exp, scale=-1.0,
+                turned[:, s, :, QUADRANT * b0 : QUADRANT * (b0 + len(xs))],
+                acc[:].rearrange("m b (q i) -> m i (b q)", i=PACK), ACT.Exp, scale=-1.0,
             )
 
-        def fetch(b, m0, m1, x):
-            nc.vector.tensor_copy(x, pages[b][:].indirect(entries(idx3, m0, m1)))
+        def turn_back(s, k):
+            acc = bank(k, (P, PACK, P))
+            for i in range(PACK):
+                nc.tensor.transpose(acc[:, i, :], turned[:, s, i, :], ident[:])
+            return acc
 
-        def spread(b, m0, m1, x, e):
-            if m1 == M:
-                m1 -= CHUNK
-                x, rest, e = x[:, :CHUNK], x[:, CHUNK:], e[:, :CHUNK]
-            else:
-                rest = None
-            nc.scalar.activation(e, x, ACT.Exp, scale=-1.0)
-            if rest is not None:
-                turn_in(b, [rest], spare_banks[2])
-            for k, (p0, p1) in enumerate(PIECES[:-1]):
-                if m0 <= p0 and p1 <= m1:
-                    nc.sync.dma_start(damping[k][QUADRANT * b : QUADRANT * (b + 1), :, :], e[:, p0 - m0 : p1 - m0])
+        copy_e2(0, 3)
+        e3_0, e1_0 = e3(0, 5), e1(0, 6)
+        copy_e2(1, 7)
+        e1_1, e3_1 = e1(1, 3), e3(1, 5)
 
-        copy_e2(0, upper_bank)
-        e3_0, e1_0 = e3(0, spare_banks[0]), e1(0, spare_banks[1])
-        copy_e2(1, spare_banks[2])
-        e3_1, e1_1 = e3(1, upper_bank), e1(1, sum_banks[0])
-
-        def bounds(u, e1_u, e3_u, high):
-            low = on("w1_raw0_%d" % (1 - u), [P, BANK], F32)
-            nc.vector.tensor_tensor(low[:], e3_u[:], pos2[u][:], ALU.min)
-            nc.vector.tensor_tensor(high[:], e1_u[:], pos2[u][:], ALU.max)
+        def bounds(u, e1_u, e3_u, tag):
+            low = on(("w1_bf01", "w1_raw0_0")[u], [P, BANK], F32)
+            high = on(tag, [P, BANK], F32)
+            steps = [(low, e3_u, ALU.min), (high, e1_u, ALU.max)]
+            for bound, estimate_u, op in steps[:: 1 - 2 * u]:
+                nc.vector.tensor_tensor(bound[:], estimate_u[:], pos2[u][:], op)
             return high, low
 
-        def difference(high, low):
-            h = unit_tile("h")
+        def difference(u, high, low):
+            h = placed(u, "h", [P, BANK], F32)
             nc.vector.tensor_tensor(h[:], high[:], low[:], ALU.subtract)
             return h
 
-        first = bounds(0, e1_0, e3_0, unit_tile("neg1"))
-        quantize_w1(1)
-        h = difference(*first)
-        second = bounds(1, e1_1, e3_1, on("page2", [P, BANK], F32))
-        open_page(1)
+        first = bounds(0, e1_0, e3_0, "high0")
+        quantize_w1(1, [0, 1], "w1_bf1")
+        h = difference(0, *first)
+        second = bounds(1, e1_1, e3_1, "high1")
         put(0, h)
-        h = difference(*second)
-        open_page(2)
+        h = difference(1, *second)
         negate_e3(2)
-        copy_e2(2, lower_bank)
+        copy_e2(2, 7)
         negate_e1(2)
         put(1, h)
 
-        fetched = {}
+        x, wo_c, wo_s = {}, {}, {}
+        blocks = [w1_raw[3, 0], w1_raw[3, 1]] + [wo_raw[:, :, t * P : (t + 1) * P] for t in range(4)]
+        rounded = {}
+
+        def quantize_rounded(u):
+            made = quantize_block(rounded[u - 1], placed(u + 1, "codes", [P, P], U32), "block_s%d" % u)
+            if u < 4:
+                w1_c[3, u - 2], w1_s[3, u - 2] = made
+            else:
+                wo_c[u - 4], wo_s[u - 4] = made
+
+        def behind_scatter(u):
+            if 1 < u < last:
+                quantize_rounded(u)
+            if u < last:
+                rounded[u] = round_beside(u, blocks[u - 1])
+            b = (u - 1) // 2
+            if u % 2 == 0:
+                x[b, CHUNK] = fetch(b, CHUNK, 3 * CHUNK, placed(u + 1, "x", [P, 2 * CHUNK], F32))
+                return
+            if b > 0:
+                tile = placed(u + 1, "x", [P, CHUNK], F32) if u < last else placed(4, "x2", [P, CHUNK], F32)
+                x[b - 1, 3 * CHUNK] = fetch(b - 1, 3 * CHUNK, M, tile)
+            if u < last:
+                x[b, 0] = fetch(b, 0, CHUNK, placed(u + 1, "x2", [P, CHUNK], F32))
+
         for u in range(2, last + 1):
             lower_part(u)
             if u < last:
                 negate_e3(u + 1)
             upper_part(u)
+            if u == 2:
+                quantize_w1(2, [0, 1], "w1_bf2")
             if u < last:
-                copy_e2(u + 1, spare_banks[1] if u == 2 else lower_bank)
-                if u in (2, 4):
-                    quantize_w1(units[u + 2][0])
-                if u == 2:
-                    open_page(3)
+                copy_e2(u + 1, 7)
+            if u == 2:
+                open_page(3)
+            if u < last:
                 negate_e1(u + 1)
-            h = envelope(u)
-            if u > 2:
-                b, half = units[u - 3]
-                fetched[u] = (b, half * BANK, (half + 1) * BANK, above[u][:])
-                fetch(*fetched[u])
+            acc = turned_sum(below[u], above[u], sum_bank)
+            if u > 3:
+                b, m0 = (u - 4) // 2, CHUNK * (1 + 2 * (u % 2))
+                move(b, m0, x[b, m0][:], on("below%d" % u, list(x[b, m0].shape), F32))
+            h = placed(u, "h", [P, BANK], F32)
+            nc.scalar.copy(h[:], acc[:])
+            behind_scatter(u - 1)
             put(u, h)
-            if u - EXP_LAG in fetched:
-                spread(*fetched[u - EXP_LAG], below[u][:])
-        spread(*fetched[last - 1], above[last - 2][:])
-        wo_bf = on("wo_bf", [P, N, PACK], BF16)
-        for n0 in range(0, N, WO_CAST):
-            if n0 == BANK:
-                spread(*fetched[last], unit_tile("neg1")[:])
-            nc.scalar.copy(out=woven_out(wo_bf[:, n0 : n0 + WO_CAST, :]), in_=woven(wo_raw[:, :, n0 : n0 + WO_CAST]))
-        wo_c, wo_s = {}, {}
 
-        def quantize_wo(n0, n1, tag):
-            codes = on(tag, [P, n1 - n0], U32)
-            scales = on("wo_s%d" % n0, [P, n1 - n0], U8)
-            nc.vector.quantize_mx(
-                out=codes[:].bitcast(FP8X4), scales=scales[:], in_=wo_bf[:, n0:n1, :].rearrange("p n i -> p (n i)")
-            )
-            for n in range(n0, n1, P):
-                wo_c[n // P] = codes[:, n - n0 : n - n0 + P].bitcast(FP8X4)
-                wo_s[n // P] = scales[:, n - n0 : n - n0 + P]
+        other_bank = 1
+        for s in range(2):
+            turn_in(s, 0, [x[b, 0][:, s * P : (s + 1) * P] for b in range(3)], (other_bank, sum_bank)[s])
+        behind_scatter(last)
+        wo_bf = {3: rounded[last - 1]}
+        for t in range(4, N // P):
+            wo_bf[t] = on("neg1_%d" % (t % 2), [P, P, PACK], BF16)
+            nc.scalar.copy(out=woven_out(wo_bf[t][:]), in_=woven(wo_raw[:, :, t * P : (t + 1) * P]))
+        move(2, CHUNK, x[2, CHUNK][:], placed(2, "x", [P, 2 * CHUNK], F32))
 
-        def late(b, k0, k1, x):
-            m0, m1 = PIECES[k0][0], PIECES[k1 - 1][1]
-            fetch(b, m0, m1, x)
-            spread(b, m0, m1, x, on("late_e%d%d" % (b, k0), [P, m1 - m0], F32)[:])
+        def quantize_wo(t):
+            codes = shared.tile([P, P], U32, name="wo_c%d" % t, align_bytes=64, offset=WO_RAW_BYTES + 4 * P * t)
+            wo_c[t], wo_s[t] = quantize_block(wo_bf[t], codes, "wo_s%d" % t)
 
-        def damp(k, tag):
-            m0, m1 = PIECES[k]
-            z = on(tag, [P, m1 - m0, PACK], BF16)
-            nc.vector.tensor_tensor(woven_out(z[:]), woven(damping[k]), woven(load_sb[:, :, m0:m1]), ALU.mult)
-            return z
+        def damp(z, factor, m0):
+            width = z.shape[1]
+            nc.vector.tensor_tensor(woven_out(z), woven(factor), woven(load_sb[:, :, m0 : m0 + width]), ALU.mult)
+
+        def quantize_z(z, m0):
+            width = z.shape[1]
+            z_c = on("z_c%d" % m0, [P, width], U32)
+            z_s = on("z_s%d" % m0, [P, width], U8)
+            nc.vector.quantize_mx(out=z_c[:].bitcast(FP8X4), scales=z_s[:], in_=z[:].rearrange("p m i -> p (m i)"))
+            return z_c, z_s, m0
 
         out_rows = out.rearrange("(t p) m -> p t m", p=P)
-        result_banks = list(range(3, BANKS))
+        result_banks = (5, 6, 7, 0, 1)
+        free_tags = ["v_w%d%d" % (a, half) for a in range(PASSES) for half in range(2)]
+        free_tags += ["w1_raw%d_%d" % (b, a) for b in range(3) for a in range(PASSES)]
+        free_tags += ["%s_%d" % (kind, n) for kind in ("pos2", "neg3", "neg1") for n in range(2)]
         filled = []
 
-        def quantize_z(z):
-            width = z.shape[1]
-            z_c = ring.tile([P, width], U32, name="z_c", align_bytes=64, bufs=3)
-            z_s = ring.tile([P, width], U8, name="z_s", align_bytes=64, bufs=3)
-            nc.vector.quantize_mx(out=z_c[:].bitcast(FP8X4), scales=z_s[:], in_=z[:].rearrange("p m i -> p (m i)"))
-            return z_c, z_s
-
-        def project(z_q, k, groups, tag=None):
-            z_c, z_s = z_q
-            m0, m1 = PIECES[k]
+        def project(z_q, groups):
+            z_c, z_s, m0 = z_q
+            width = z_c.shape[1]
             for t0, t1, copy in groups:
-                acc = bank(result_banks[len(filled) % len(result_banks)], (P, t1 - t0, m1 - m0))
-                filled.append(acc)
+                acc = bank(result_banks[len(filled) % len(result_banks)], (P, t1 - t0, width))
                 for t in range(t0, t1):
                     nc.tensor.matmul_mx(
                         out=acc[:, t - t0, :], lhsT=wo_c[t], lhsT_scale=wo_s[t],
                         rhs=z_c[:].bitcast(FP8X4), rhs_scale=z_s[:], start=True, stop=True,
                     )
-                shape = [P, t1 - t0, m1 - m0]
-                result = on(tag, shape, F32) if tag else ring.tile(shape, F32, name="result", bufs=13)
+                result = on(free_tags[len(filled)], [P, t1 - t0, width], F32)
+                filled.append(result)
                 copy(result[:], acc[:])
-                nc.sync.dma_start(out_rows[:, t0:t1, m0:m1], result[:])
+                nc.sync.dma_start(out_rows[:, t0:t1, m0 : m0 + width], result[:])
 
-        for k in range(4):
-            late(PAGES - 1, k, k + 1, on("late_x%d" % k, [P, PIECES[k][1] - PIECES[k][0]], F32)[:])
-        late(PAGES - 2, 3, 4, h[:, :CHUNK])
-        quantize_wo(0, WO_FIRST, "late_x0")
         by_scalar, by_vector = nc.scalar.copy, nc.vector.tensor_copy
         pairs = [(t, t + 2, by_scalar) for t in range(0, N // P, 2)]
-
-        z = damp(0, "z0")
-        quantize_wo(WO_FIRST, 2 * WO_FIRST, "late_e30")
-        z_q = quantize_z(z)
-        project(z_q, 0, pairs[:2])
-        z = damp(1, "z1")
-        quantize_wo(2 * WO_FIRST, N, "z0")
-        project(z_q, 0, pairs[2:])
-        project(quantize_z(z), 1, [(0, 3, by_scalar), (3, 6, by_scalar)])
-        z = damp(2, "wo_bf")
-        x = on("z1", [P, CHUNK], F32)
-        fetch(PAGES - 1, *PIECES[4], x[:])
-        turn_in(PAGES - 1, [x[:]], 0)
-        z_q = quantize_z(z)
-        x = on("page3", [P, CHUNK], F32)
-        fetch(PAGES - 2, *PIECES[4], x[:])
-        project(z_q, 2, pairs[:1])
-        turn_in(PAGES - 2, [x[:]], 2)
-        project(z_q, 2, pairs[1:2])
-        z_next = quantize_z(damp(3, "tab_w0"))
-        project(z_q, 2, [(4, 6, by_vector)], "tab_w0")
         back = []
-        for s in range(steps):
-            back.append(bank(s, (P, PACK, P)))
-            for i in range(PACK):
-                nc.tensor.transpose(back[s][:, i, :], turned[:, s, i, :], ident[:])
-            if s == 0:
-                project(z_next, 3, pairs[:1])
-        project(z_next, 3, pairs[1:])
-        z = on("z4", [P, CHUNK, PACK], BF16)
-        for s in range(steps):
-            m0 = PIECES[4][0] + s * P
-            nc.vector.tensor_tensor(
-                woven_out(z[:, s * P : (s + 1) * P, :]), woven(back[s][:]), woven(load_sb[:, :, m0 : m0 + P]), ALU.mult
-            )
-        project(quantize_z(z), 4, [pairs[0], (2, 4, by_vector), pairs[2]])
+        for s in range(2):
+            late = fetch(3, s * P, (s + 1) * P, on("high%d" % s, [P, P], F32))
+            turn_in(s, 3, [late[:]], (other_bank, sum_bank)[s])
+            back.append(turn_back(s, 3 + s))
+        for n, m0 in enumerate(range(CHUNK, M, CHUNK)):
+            late = fetch(3, m0, m0 + CHUNK, on("late%d" % n, [P, CHUNK], F32))
+            move(3, m0, late[:], on(("high0", "high1", "late0")[n], [P, CHUNK], F32))
+        move(2, M - CHUNK, x[2, M - CHUNK][:], on("late1", [P, CHUNK], F32))
+        z = {m0: on("z%d" % m0, [P, P if m0 < CHUNK else CHUNK, PACK], BF16) for m0 in (0, P, *range(CHUNK, M, CHUNK))}
+        damp(z[0][:], back[0][:], 0)
+        for t in range(3, N // P):
+            quantize_wo(t)
+        project(quantize_z(z[0], 0), pairs)
+        damp(z[P][:], back[1][:], P)
+        project(quantize_z(z[P], P), [(0, 3, by_scalar), (3, 6, by_scalar)])
+        groups = {
+            CHUNK: [(0, 1, by_scalar), (1, 3, by_scalar), (3, 5, by_scalar), (5, 6, by_scalar)],
+            2 * CHUNK: pairs,
+            3 * CHUNK: [pairs[0], (2, 4, by_vector), pairs[2]],
+        }
+        for m0 in range(CHUNK, M, CHUNK):
+            for c in range(0, CHUNK, P):
+                damp(z[m0][:, c : c + P, :], moved[m0][:, :, c : c + P], m0 + c)
+            project(quantize_z(z[m0], m0), groups[m0])

@@ -29,8 +29,9 @@ BANK = 512
 CHUNK = 256
 WO_RAW_BYTES = 4 * PACK * N
 TURNED_BYTES = 4 * 2 * PACK * P
-PLACES = {"rounded": 0, "h": 960, "above": 3072, "codes": 3072, "x": 3584, "x2": 4608}
-REGION = 5632
+PLACES = {"above": 960, "x": 1024, "x2": 2048, "before": 1088, "behind": 3008}
+REGION = 3072
+FILLER = 64
 
 
 def woven(planes):
@@ -58,7 +59,7 @@ def tile_list_latency_envelopes_kernel(
             return psum.tile(list(shape), F32, name="bank", tag="bank%d" % k)
 
         def placed(u, place, shape, dtype):
-            offset = WO_RAW_BYTES + TURNED_BYTES + u * REGION + PLACES[place]
+            offset = WO_RAW_BYTES + TURNED_BYTES + (u - 2) * REGION + PLACES[place]
             return shared.tile(shape, dtype, name="%s%d_%d" % (place, u, shape[1]), align_bytes=64, offset=offset)
 
         idx1 = keep.tile([P, S // STRIPE], U16, name="idx1")
@@ -82,11 +83,10 @@ def tile_list_latency_envelopes_kernel(
         pages = {}
 
         def open_page(b):
-            pages[b] = on("w1_bf1" if b == 3 else "page%d" % b, [P, T2], F32)
+            pages[b] = on(("page0", "w1_bf1", "low1", "below3")[b], [P, T2], F32)
             nc.gpsimd.memset(pages[b][:].bitcast(I32), 0)
 
-        for b in range(PAGES - 1):
-            open_page(b)
+        open_page(0)
 
         tab_w = [on("tab_w%d" % a, [P, T], I32) for a in range(PASSES)]
         w1_rows = w1.rearrange("(a p i) c -> a p i c", a=PASSES, i=PACK)
@@ -156,8 +156,12 @@ def tile_list_latency_envelopes_kernel(
             load_w1(a, 3, PAGES)
         load_packed(2, PAGES)
         nc.sync.dma_start(idx3[:], offs3)
-        wo_raw = shared.tile([P, PACK, N], F32, name="wo_raw", align_bytes=64, offset=0)
-        nc.sync.dma_start(wo_raw[:], wo.rearrange("(p i) n -> p i n", i=PACK))
+        wo_raw = {}
+        for n0, n1 in ((0, CHUNK), (CHUNK, N)):
+            raw = shared.tile([P, PACK, n1 - n0], F32, name="wo_raw%d" % n0, align_bytes=64, offset=4 * PACK * n0)
+            nc.sync.dma_start(raw[:], wo.rearrange("(p i) n -> p i n", i=PACK)[:, :, n0:n1])
+            for n in range(n0, n1, P):
+                wo_raw[n // P] = raw[:, :, n - n0 : n - n0 + P]
         load_rows = load.rearrange("(p i) m -> p i m", i=PACK)
         load_sb = keep.tile([P, PACK, M], F32, name="load_sb")
         nc.sync.dma_start(load_sb[:], load_rows)
@@ -184,11 +188,6 @@ def tile_list_latency_envelopes_kernel(
             nc.vector.quantize_mx(
                 out=codes[:].bitcast(FP8X4), scales=scales[:], in_=rounded[:].rearrange("p a c i -> p (a c i)")
             )
-
-        def round_beside(u, raw):
-            rounded = placed(u, "rounded", [P, P, PACK], BF16)
-            nc.gpsimd.tensor_scalar(rounded[:], raw.rearrange("p i c -> p c i"), 1.0, 0.0, ALU.mult, ALU.add)
-            return rounded
 
         def quantize_block(rounded, codes, tag):
             scales = on(tag, [P, P], U8)
@@ -277,21 +276,24 @@ def tile_list_latency_envelopes_kernel(
             for c in range(0, x.shape[1], CHUNK):
                 nc.sync.dma_start(moved[m0 + c][QUADRANT * b : QUADRANT * (b + 1), :, :], e[:, c : c + CHUNK])
 
-        turned = shared.tile([P, 2, PACK, P], F32, name="turned", align_bytes=64, offset=WO_RAW_BYTES)
+        turned = [
+            shared.tile([P, PACK, P], F32, name="turned%d" % s, align_bytes=64, offset=WO_RAW_BYTES + s * TURNED_BYTES // 2)
+            for s in range(2)
+        ]
 
         def turn_in(s, b0, xs, k):
             acc = bank(k, (P, len(xs), P))
             for n, x in enumerate(xs):
                 nc.tensor.transpose(acc[:, n, :], x, ident[:])
             nc.scalar.activation(
-                turned[:, s, :, QUADRANT * b0 : QUADRANT * (b0 + len(xs))],
+                turned[s][:, :, QUADRANT * b0 : QUADRANT * (b0 + len(xs))],
                 acc[:].rearrange("m b (q i) -> m i (b q)", i=PACK), ACT.Exp, scale=-1.0,
             )
 
         def turn_back(s, k):
             acc = bank(k, (P, PACK, P))
             for i in range(PACK):
-                nc.tensor.transpose(acc[:, i, :], turned[:, s, i, :], ident[:])
+                nc.tensor.transpose(acc[:, i, :], turned[s][:, i, :], ident[:])
             return acc
 
         copy_e2(0, 3)
@@ -300,7 +302,7 @@ def tile_list_latency_envelopes_kernel(
         e1_1, e3_1 = e1(1, 3), e3(1, 5)
 
         def bounds(u, e1_u, e3_u, tag):
-            low = on(("w1_bf01", "w1_raw0_0")[u], [P, BANK], F32)
+            low = on(("w1_bf01", "low1")[u], [P, BANK], F32)
             high = on(tag, [P, BANK], F32)
             steps = [(low, e3_u, ALU.min), (high, e1_u, ALU.max)]
             for bound, estimate_u, op in steps[:: 1 - 2 * u]:
@@ -308,7 +310,7 @@ def tile_list_latency_envelopes_kernel(
             return high, low
 
         def difference(u, high, low):
-            h = placed(u, "h", [P, BANK], F32)
+            h = on("h%d" % (u % 4), [P, BANK], F32)
             nc.vector.tensor_tensor(h[:], high[:], low[:], ALU.subtract)
             return h
 
@@ -316,38 +318,33 @@ def tile_list_latency_envelopes_kernel(
         quantize_w1(1, [0, 1], "w1_bf1")
         h = difference(0, *first)
         second = bounds(1, e1_1, e3_1, "high1")
+        open_page(1)
         put(0, h)
         h = difference(1, *second)
+        open_page(2)
         negate_e3(2)
         copy_e2(2, 7)
         negate_e1(2)
         put(1, h)
 
         x, wo_c, wo_s = {}, {}, {}
-        blocks = [w1_raw[3, 0], w1_raw[3, 1]] + [wo_raw[:, :, t * P : (t + 1) * P] for t in range(4)]
-        rounded = {}
+        wo_bf = {}
 
-        def quantize_rounded(u):
-            made = quantize_block(rounded[u - 1], placed(u + 1, "codes", [P, P], U32), "block_s%d" % u)
-            if u < 4:
-                w1_c[3, u - 2], w1_s[3, u - 2] = made
-            else:
-                wo_c[u - 4], wo_s[u - 4] = made
+        def round_wo(t, tile):
+            wo_bf[t] = tile
+            nc.scalar.copy(out=woven_out(tile[:]), in_=woven(wo_raw[t]))
+
+        def quantize_wo(t, codes):
+            wo_c[t], wo_s[t] = quantize_block(wo_bf[t], codes, "wo_s%d" % t)
 
         def behind_scatter(u):
-            if 1 < u < last:
-                quantize_rounded(u)
-            if u < last:
-                rounded[u] = round_beside(u, blocks[u - 1])
             b = (u - 1) // 2
             if u % 2 == 0:
                 x[b, CHUNK] = fetch(b, CHUNK, 3 * CHUNK, placed(u + 1, "x", [P, 2 * CHUNK], F32))
                 return
             if b > 0:
-                tile = placed(u + 1, "x", [P, CHUNK], F32) if u < last else placed(4, "x2", [P, CHUNK], F32)
-                x[b - 1, 3 * CHUNK] = fetch(b - 1, 3 * CHUNK, M, tile)
-            if u < last:
-                x[b, 0] = fetch(b, 0, CHUNK, placed(u + 1, "x2", [P, CHUNK], F32))
+                x[b - 1, 3 * CHUNK] = fetch(b - 1, 3 * CHUNK, M, placed(u + 1, "x", [P, CHUNK], F32))
+            x[b, 0] = fetch(b, 0, CHUNK, placed(u + 1, "x2", [P, CHUNK], F32))
 
         for u in range(2, last + 1):
             lower_part(u)
@@ -358,32 +355,35 @@ def tile_list_latency_envelopes_kernel(
                 quantize_w1(2, [0, 1], "w1_bf2")
             if u < last:
                 copy_e2(u + 1, 7)
-            if u == 2:
-                open_page(3)
             if u < last:
                 negate_e1(u + 1)
             acc = turned_sum(below[u], above[u], sum_bank)
-            if u > 3:
+            if u < 4:
+                quantize_w1(3, [u - 2], "below%d" % u)
+                if u == 3:
+                    open_page(u)
+            else:
                 b, m0 = (u - 4) // 2, CHUNK * (1 + 2 * (u % 2))
                 move(b, m0, x[b, m0][:], on("below%d" % u, list(x[b, m0].shape), F32))
-            h = placed(u, "h", [P, BANK], F32)
+            h = on("h%d" % (u % 4), [P, BANK], F32)
             nc.scalar.copy(h[:], acc[:])
+            if u > 5:
+                round_wo(u - 5, on("neg1_%d" % (u % 2), [P, P, PACK], BF16))
+                quantize_wo(u - 5, on("wo_c%d" % (u - 5), [P, P], U32))
             behind_scatter(u - 1)
             put(u, h)
 
         other_bank = 1
         for s in range(2):
             turn_in(s, 0, [x[b, 0][:, s * P : (s + 1) * P] for b in range(3)], (other_bank, sum_bank)[s])
-        behind_scatter(last)
-        wo_bf = {3: rounded[last - 1]}
-        for t in range(4, N // P):
-            wo_bf[t] = on("neg1_%d" % (t % 2), [P, P, PACK], BF16)
-            nc.scalar.copy(out=woven_out(wo_bf[t][:]), in_=woven(wo_raw[:, :, t * P : (t + 1) * P]))
-        move(2, CHUNK, x[2, CHUNK][:], placed(2, "x", [P, 2 * CHUNK], F32))
+        for t, u, place in ((0, 4, "before"), (3, 4, "behind"), (4, 6, "before"), (5, 6, "behind")):
+            round_wo(t, placed(u, place, [P, P, PACK], BF16))
+        quantize_wo(0, on("wo_c0", [P, P], U32))
+        move(2, CHUNK, x[2, CHUNK][:], shared.tile([P, 2 * CHUNK], F32, name="behind_wo", align_bytes=64, offset=0))
 
-        def quantize_wo(t):
-            codes = shared.tile([P, P], U32, name="wo_c%d" % t, align_bytes=64, offset=WO_RAW_BYTES + 4 * P * t)
-            wo_c[t], wo_s[t] = quantize_block(wo_bf[t], codes, "wo_s%d" % t)
+        def behind_turn(t):
+            offset = WO_RAW_BYTES + 4 * P * (t - 3)
+            quantize_wo(t, shared.tile([P, P], U32, name="wo_c%d" % t, align_bytes=64, offset=offset))
 
         def damp(z, factor, m0):
             width = z.shape[1]
@@ -428,13 +428,17 @@ def tile_list_latency_envelopes_kernel(
         for n, m0 in enumerate(range(CHUNK, M, CHUNK)):
             late = fetch(3, m0, m0 + CHUNK, on("late%d" % n, [P, CHUNK], F32))
             move(3, m0, late[:], on(("high0", "high1", "late0")[n], [P, CHUNK], F32))
-        move(2, M - CHUNK, x[2, M - CHUNK][:], on("late1", [P, CHUNK], F32))
         z = {m0: on("z%d" % m0, [P, P if m0 < CHUNK else CHUNK, PACK], BF16) for m0 in (0, P, *range(CHUNK, M, CHUNK))}
         damp(z[0][:], back[0][:], 0)
-        for t in range(3, N // P):
-            quantize_wo(t)
-        project(quantize_z(z[0], 0), pairs)
+        behind_turn(3)
+        behind_turn(4)
+        z_q = quantize_z(z[0], 0)
+        project(z_q, pairs[:2])
+        behind_turn(5)
+        project(z_q, pairs[2:])
         damp(z[P][:], back[1][:], P)
+        late = shared.tile([P, CHUNK], F32, name="last_x", align_bytes=64, offset=WO_RAW_BYTES + TURNED_BYTES // 2)
+        move(2, M - CHUNK, fetch(2, M - CHUNK, M, late)[:], on("late1", [P, CHUNK], F32))
         project(quantize_z(z[P], P), [(0, 3, by_scalar), (3, 6, by_scalar)])
         groups = {
             CHUNK: [(0, 1, by_scalar), (1, 3, by_scalar), (3, 5, by_scalar), (5, 6, by_scalar)],
@@ -442,6 +446,6 @@ def tile_list_latency_envelopes_kernel(
             3 * CHUNK: [pairs[0], (2, 4, by_vector), pairs[2]],
         }
         for m0 in range(CHUNK, M, CHUNK):
-            for c in range(0, CHUNK, P):
-                damp(z[m0][:, c : c + P, :], moved[m0][:, :, c : c + P], m0 + c)
+            for c0, c1 in ((0, CHUNK),) if m0 == CHUNK else ((0, FILLER), (FILLER, CHUNK)):
+                damp(z[m0][:, c0:c1, :], moved[m0][:, :, c0:c1], m0 + c0)
             project(quantize_z(z[m0], m0), groups[m0])

@@ -397,29 +397,37 @@ def tile_list_latency_envelopes_kernel(
             return z_c, z_s, m0
 
         out_rows = out.rearrange("(t p) m -> p t m", p=P)
-        result_banks = (5, 6, 7, 0, 1)
+        result_banks = (5, 6, 7, 0, 1, 2, 3, 4)
         free_tags = ["v_w%d%d" % (a, half) for a in range(PASSES) for half in range(2)]
         free_tags += ["w1_raw%d_%d" % (b, a) for b in range(3) for a in range(PASSES)]
         free_tags += ["%s_%d" % (kind, n) for kind in ("pos2", "neg3", "neg1") for n in range(2)]
         filled = []
 
+        def multiply(acc, z_q, t):
+            nc.tensor.matmul_mx(
+                out=acc, lhsT=wo_c[t], lhsT_scale=wo_s[t],
+                rhs=z_q[0][:].bitcast(FP8X4), rhs_scale=z_q[1][:], start=True, stop=True,
+            )
+
+        def result_bank(n, shape):
+            return bank(result_banks[n % len(result_banks)], shape)
+
+        def store(acc, t0, m0, copy):
+            result = on(free_tags[len(filled)], list(acc.shape), F32)
+            filled.append(result)
+            copy(result[:], acc[:])
+            nc.sync.dma_start(out_rows[:, t0 : t0 + acc.shape[1], m0 : m0 + acc.shape[2]], result[:])
+
         def project(z_q, groups):
-            z_c, z_s, m0 = z_q
-            width = z_c.shape[1]
             for t0, t1, copy in groups:
-                acc = bank(result_banks[len(filled) % len(result_banks)], (P, t1 - t0, width))
+                acc = result_bank(len(filled), (P, t1 - t0, z_q[0].shape[1]))
                 for t in range(t0, t1):
-                    nc.tensor.matmul_mx(
-                        out=acc[:, t - t0, :], lhsT=wo_c[t], lhsT_scale=wo_s[t],
-                        rhs=z_c[:].bitcast(FP8X4), rhs_scale=z_s[:], start=True, stop=True,
-                    )
-                result = on(free_tags[len(filled)], [P, t1 - t0, width], F32)
-                filled.append(result)
-                copy(result[:], acc[:])
-                nc.sync.dma_start(out_rows[:, t0:t1, m0 : m0 + width], result[:])
+                    multiply(acc[:, t - t0, :], z_q, t)
+                store(acc, t0, z_q[2], copy)
 
         by_scalar, by_vector = nc.scalar.copy, nc.vector.tensor_copy
         pairs = [(t, t + 2, by_scalar) for t in range(0, N // P, 2)]
+        end = fetch(2, M - CHUNK, M, placed(2, "x2", [P, CHUNK], F32))
         back = []
         for s in range(2):
             late = fetch(3, s * P, (s + 1) * P, on("high%d" % s, [P, P], F32))
@@ -428,6 +436,7 @@ def tile_list_latency_envelopes_kernel(
         for n, m0 in enumerate(range(CHUNK, M, CHUNK)):
             late = fetch(3, m0, m0 + CHUNK, on("late%d" % n, [P, CHUNK], F32))
             move(3, m0, late[:], on(("high0", "high1", "late0")[n], [P, CHUNK], F32))
+        move(2, M - CHUNK, end[:], on("late1", [P, CHUNK], F32))
         z = {m0: on("z%d" % m0, [P, P if m0 < CHUNK else CHUNK, PACK], BF16) for m0 in (0, P, *range(CHUNK, M, CHUNK))}
         damp(z[0][:], back[0][:], 0)
         behind_turn(3)
@@ -437,15 +446,15 @@ def tile_list_latency_envelopes_kernel(
         behind_turn(5)
         project(z_q, pairs[2:])
         damp(z[P][:], back[1][:], P)
-        late = shared.tile([P, CHUNK], F32, name="last_x", align_bytes=64, offset=WO_RAW_BYTES + TURNED_BYTES // 2)
-        move(2, M - CHUNK, fetch(2, M - CHUNK, M, late)[:], on("late1", [P, CHUNK], F32))
         project(quantize_z(z[P], P), [(0, 3, by_scalar), (3, 6, by_scalar)])
-        groups = {
-            CHUNK: [(0, 1, by_scalar), (1, 3, by_scalar), (3, 5, by_scalar), (5, 6, by_scalar)],
-            2 * CHUNK: pairs,
-            3 * CHUNK: [pairs[0], (2, 4, by_vector), pairs[2]],
-        }
-        for m0 in range(CHUNK, M, CHUNK):
-            for c0, c1 in ((0, CHUNK),) if m0 == CHUNK else ((0, FILLER), (FILLER, CHUNK)):
+        damp(z[CHUNK][:], moved[CHUNK][:], CHUNK)
+        project(quantize_z(z[CHUNK], CHUNK), [(0, 1, by_scalar), (1, 3, by_scalar), (3, 5, by_scalar), (5, 6, by_scalar)])
+        wide = [result_bank(len(filled) + t, (P, 1, BANK)) for t in range(N // P)]
+        for m0 in (BANK, M - CHUNK):
+            for c0, c1 in ((0, FILLER), (FILLER, CHUNK)):
                 damp(z[m0][:, c0:c1, :], moved[m0][:, :, c0:c1], m0 + c0)
-            project(quantize_z(z[m0], m0), groups[m0])
+            z_q = quantize_z(z[m0], m0)
+            for t, acc in enumerate(wide):
+                multiply(acc[:, 0, m0 - BANK : m0 - BANK + CHUNK], z_q, t)
+        for t, acc in enumerate(wide):
+            store(acc, t, BANK, (by_scalar, by_vector)[t % 2])

@@ -157,7 +157,7 @@ def tile_list_latency_envelopes_kernel(
         load_packed(2, PAGES)
         nc.sync.dma_start(idx3[:], offs3)
         wo_raw = {}
-        for n0, n1 in ((0, CHUNK), (CHUNK, N)):
+        for n0, n1 in ((0, CHUNK), (CHUNK, 3 * P), (3 * P, N)):
             raw = shared.tile([P, PACK, n1 - n0], F32, name="wo_raw%d" % n0, align_bytes=64, offset=4 * PACK * n0)
             nc.sync.dma_start(raw[:], wo.rearrange("(p i) n -> p i n", i=PACK)[:, :, n0:n1])
             for n in range(n0, n1, P):
@@ -368,21 +368,19 @@ def tile_list_latency_envelopes_kernel(
             h = on("h%d" % (u % 4), [P, BANK], F32)
             nc.scalar.copy(h[:], acc[:])
             if u > 5:
-                round_wo(u - 5, on("neg1_%d" % (u % 2), [P, P, PACK], BF16))
-                quantize_wo(u - 5, on("wo_c%d" % (u - 5), [P, P], U32))
+                round_wo(u - 6, on("neg1_%d" % (u % 2), [P, P, PACK], BF16))
             behind_scatter(u - 1)
             put(u, h)
 
         other_bank = 1
         for s in range(2):
             turn_in(s, 0, [x[b, 0][:, s * P : (s + 1) * P] for b in range(3)], (other_bank, sum_bank)[s])
-        for t, u, place in ((0, 4, "before"), (3, 4, "behind"), (4, 6, "before"), (5, 6, "behind")):
+        for t, u, place in ((2, 4, "before"), (3, 4, "behind"), (4, 6, "before"), (5, 6, "behind")):
             round_wo(t, placed(u, place, [P, P, PACK], BF16))
-        quantize_wo(0, on("wo_c0", [P, P], U32))
-        move(2, CHUNK, x[2, CHUNK][:], shared.tile([P, 2 * CHUNK], F32, name="behind_wo", align_bytes=64, offset=0))
+        move(2, CHUNK, x[2, CHUNK][:], shared.tile([P, 2 * CHUNK], F32, name="behind_wo", align_bytes=64, offset=4 * PACK * CHUNK))
 
         def behind_turn(t):
-            offset = WO_RAW_BYTES + 4 * P * (t - 3)
+            offset = WO_RAW_BYTES + 4 * P * t
             quantize_wo(t, shared.tile([P, P], U32, name="wo_c%d" % t, align_bytes=64, offset=offset))
 
         def damp(z, factor, m0):
@@ -398,35 +396,26 @@ def tile_list_latency_envelopes_kernel(
 
         out_rows = out.rearrange("(t p) m -> p t m", p=P)
         result_banks = (5, 6, 7, 0, 1, 2, 3, 4)
-        free_tags = ["v_w%d%d" % (a, half) for a in range(PASSES) for half in range(2)]
-        free_tags += ["w1_raw%d_%d" % (b, a) for b in range(3) for a in range(PASSES)]
-        free_tags += ["%s_%d" % (kind, n) for kind in ("pos2", "neg3", "neg1") for n in range(2)]
-        filled = []
+        results = [on(tag, [P, 2, M], F32) for tag in ("tab_w0", "tab_w1", "page0")]
+        stored = [0] * (N // P)
+        done = []
 
-        def multiply(acc, z_q, t):
-            nc.tensor.matmul_mx(
-                out=acc, lhsT=wo_c[t], lhsT_scale=wo_s[t],
-                rhs=z_q[0][:].bitcast(FP8X4), rhs_scale=z_q[1][:], start=True, stop=True,
-            )
+        def project(z_q, t0, t1, leaves, copy=nc.scalar.copy):
+            z_c, z_s, m0 = z_q
+            m1 = m0 + z_c.shape[1]
+            acc = bank(result_banks[len(done) % len(result_banks)], (P, t1 - t0, m1 - m0))
+            done.append(acc)
+            for t in range(t0, t1):
+                nc.tensor.matmul_mx(
+                    out=acc[:, t - t0, :], lhsT=wo_c[t], lhsT_scale=wo_s[t],
+                    rhs=z_c[:].bitcast(FP8X4), rhs_scale=z_s[:], start=True, stop=True,
+                )
+            rows = results[t0 // 2][:, t0 % 2 : t0 % 2 + t1 - t0, :]
+            copy(rows[:, :, m0:m1], acc[:])
+            if leaves:
+                nc.sync.dma_start(out_rows[:, t0:t1, stored[t0] : m1], rows[:, :, stored[t0] : m1])
+                stored[t0:t1] = [m1] * (t1 - t0)
 
-        def result_bank(n, shape):
-            return bank(result_banks[n % len(result_banks)], shape)
-
-        def store(acc, t0, m0, copy):
-            result = on(free_tags[len(filled)], list(acc.shape), F32)
-            filled.append(result)
-            copy(result[:], acc[:])
-            nc.sync.dma_start(out_rows[:, t0 : t0 + acc.shape[1], m0 : m0 + acc.shape[2]], result[:])
-
-        def project(z_q, groups):
-            for t0, t1, copy in groups:
-                acc = result_bank(len(filled), (P, t1 - t0, z_q[0].shape[1]))
-                for t in range(t0, t1):
-                    multiply(acc[:, t - t0, :], z_q, t)
-                store(acc, t0, z_q[2], copy)
-
-        by_scalar, by_vector = nc.scalar.copy, nc.vector.tensor_copy
-        pairs = [(t, t + 2, by_scalar) for t in range(0, N // P, 2)]
         end = fetch(2, M - CHUNK, M, placed(2, "x2", [P, CHUNK], F32))
         back = []
         for s in range(2):
@@ -439,22 +428,32 @@ def tile_list_latency_envelopes_kernel(
         move(2, M - CHUNK, end[:], on("late1", [P, CHUNK], F32))
         z = {m0: on("z%d" % m0, [P, P if m0 < CHUNK else CHUNK, PACK], BF16) for m0 in (0, P, *range(CHUNK, M, CHUNK))}
         damp(z[0][:], back[0][:], 0)
-        behind_turn(3)
-        behind_turn(4)
+        behind_turn(0)
+        behind_turn(1)
         z_q = quantize_z(z[0], 0)
-        project(z_q, pairs[:2])
-        behind_turn(5)
-        project(z_q, pairs[2:])
+        project(z_q, 0, 1, True)
+        project(z_q, 1, 2, True)
+        behind_turn(2)
+        behind_turn(3)
+        project(z_q, 2, 4, True)
         damp(z[P][:], back[1][:], P)
-        project(quantize_z(z[P], P), [(0, 3, by_scalar), (3, 6, by_scalar)])
+        behind_turn(4)
+        behind_turn(5)
+        project(z_q, 4, 6, True)
+        z_q = quantize_z(z[P], P)
+        for t0, t1, leaves in ((0, 2, True), (2, 4, True), (4, 6, True)):
+            project(z_q, t0, t1, leaves)
         damp(z[CHUNK][:], moved[CHUNK][:], CHUNK)
-        project(quantize_z(z[CHUNK], CHUNK), [(0, 1, by_scalar), (1, 3, by_scalar), (3, 5, by_scalar), (5, 6, by_scalar)])
-        wide = [result_bank(len(filled) + t, (P, 1, BANK)) for t in range(N // P)]
-        for m0 in (BANK, M - CHUNK):
-            for c0, c1 in ((0, FILLER), (FILLER, CHUNK)):
-                damp(z[m0][:, c0:c1, :], moved[m0][:, :, c0:c1], m0 + c0)
-            z_q = quantize_z(z[m0], m0)
-            for t, acc in enumerate(wide):
-                multiply(acc[:, 0, m0 - BANK : m0 - BANK + CHUNK], z_q, t)
-        for t, acc in enumerate(wide):
-            store(acc, t, BANK, (by_scalar, by_vector)[t % 2])
+        z_q = quantize_z(z[CHUNK], CHUNK)
+        for t0, t1, leaves in ((0, 1, True), (1, 2, True), (2, 4, True), (4, 6, True)):
+            project(z_q, t0, t1, leaves)
+        for c0, c1 in ((0, FILLER), (FILLER, CHUNK)):
+            damp(z[BANK][:, c0:c1, :], moved[BANK][:, :, c0:c1], BANK + c0)
+        z_q = quantize_z(z[BANK], BANK)
+        for t0, t1, leaves in ((0, 2, False), (2, 4, False), (4, 6, False)):
+            project(z_q, t0, t1, leaves)
+        for c0, c1 in ((0, FILLER), (FILLER, CHUNK)):
+            damp(z[M - CHUNK][:, c0:c1, :], moved[M - CHUNK][:, :, c0:c1], M - CHUNK + c0)
+        z_q = quantize_z(z[M - CHUNK], M - CHUNK)
+        for t0, t1, copy in ((0, 1, nc.vector.tensor_copy), (1, 2, nc.vector.tensor_copy), (2, 4, nc.vector.tensor_copy), (4, 6, nc.scalar.copy)):
+            project(z_q, t0, t1, True, copy)

@@ -132,16 +132,10 @@ def tile_list_latency_envelopes_kernel(
         nc.vector.tensor_copy(v_s[:], tab_s[:].indirect(idx1[:]))
         plane_span = P - QUADRANT + PLANE_ROWS
 
-        def move_plane(half):
-            columns = slice(half * BANK, (half + 1) * BANK)
-            nc.sync.dma_start(
-                v_s1[0:plane_span, columns].bitcast(I32),
-                v_s[SECOND_PLANE : SECOND_PLANE + plane_span, columns].bitcast(I32),
-            )
-
-        move_plane(0)
+        nc.sync.dma_start(
+            v_s1[0:plane_span, :].bitcast(I32), v_s[SECOND_PLANE : SECOND_PLANE + plane_span, :].bitcast(I32)
+        )
         load_w1(1, 0, 1)
-        move_plane(1)
         planes = [v_s[:], v_s1[:]]
         for a in range(PASSES):
             load_w1(a, 1, 2)
@@ -151,9 +145,9 @@ def tile_list_latency_envelopes_kernel(
         nc.sync.dma_start(idx2[:], offs2)
         for a in range(PASSES):
             load_w1(a, 2, 3)
+        load_w1(0, 3, PAGES)
         nc.sync.dma_start(wgs_sb[1][:], wgs[:, BANK:])
-        for a in range(PASSES):
-            load_w1(a, 3, PAGES)
+        load_w1(1, 3, PAGES)
         load_packed(2, PAGES)
         nc.sync.dma_start(idx3[:], offs3)
         wo_raw = {}
@@ -258,7 +252,7 @@ def tile_list_latency_envelopes_kernel(
             pos2[u] = copy_out({0: "w1_c10", 1: "pos2_first"}.get(u, "pos2_%d" % (u % 2)), e2(u, k), ACT.Copy, 1.0)
 
         def negate_e3(u):
-            neg3[u] = copy_out("w1_bf2" if u == 2 else "neg3_%d" % (u % 2), e3(u, 4 if u == 2 else 5), ACT.Copy, -1.0)
+            neg3[u] = copy_out("w1_bf2" if u == 2 else "neg3_%d" % (u % 2), e3(u, 5), ACT.Copy, -1.0)
 
         def negate_e1(u):
             neg1[u] = copy_out("neg1_%d" % (u % 2), e1(u, 6), ACT.Copy, -1.0)
@@ -299,13 +293,13 @@ def tile_list_latency_envelopes_kernel(
         copy_e2(0, 3)
         e3_0, e1_0 = e3(0, 5), e1(0, 6)
         copy_e2(1, 7)
-        e1_1, e3_1 = e1(1, 3), e3(1, 5)
+        e3_1, e1_1 = e3(1, 4), e1(1, 3)
 
         def bounds(u, e1_u, e3_u, tag):
-            low = on(("w1_bf01", "low1")[u], [P, BANK], F32)
+            low = on("low%d" % u, [P, BANK], F32)
             high = on(tag, [P, BANK], F32)
             steps = [(low, e3_u, ALU.min), (high, e1_u, ALU.max)]
-            for bound, estimate_u, op in steps[:: 1 - 2 * u]:
+            for bound, estimate_u, op in steps:
                 nc.vector.tensor_tensor(bound[:], estimate_u[:], pos2[u][:], op)
             return high, low
 
@@ -417,15 +411,15 @@ def tile_list_latency_envelopes_kernel(
                 stored[t0:t1] = [m1] * (t1 - t0)
 
         end = fetch(2, M - CHUNK, M, placed(2, "x2", [P, CHUNK], F32))
+        move(2, M - CHUNK, end[:], on("end_e", [P, CHUNK], F32))
         back = []
-        for s in range(2):
-            late = fetch(3, s * P, (s + 1) * P, on("high%d" % s, [P, P], F32))
-            turn_in(s, 3, [late[:]], (other_bank, sum_bank)[s])
-            back.append(turn_back(s, 3 + s))
         for n, m0 in enumerate(range(CHUNK, M, CHUNK)):
+            if n < 2:
+                late = fetch(3, n * P, (n + 1) * P, on("high%d" % n, [P, P], F32))
+                turn_in(n, 3, [late[:]], (other_bank, sum_bank)[n])
+                back.append(turn_back(n, 3 + n))
             late = fetch(3, m0, m0 + CHUNK, on("late%d" % n, [P, CHUNK], F32))
             move(3, m0, late[:], on(("high0", "high1", "late0")[n], [P, CHUNK], F32))
-        move(2, M - CHUNK, end[:], on("late1", [P, CHUNK], F32))
         z = {m0: on("z%d" % m0, [P, P if m0 < CHUNK else CHUNK, PACK], BF16) for m0 in (0, P, *range(CHUNK, M, CHUNK))}
         damp(z[0][:], back[0][:], 0)
         behind_turn(0)

from contextlib import ExitStack

import concourse.mybir as mybir
from concourse.masks import make_identity

K, H, N, T, S, T2, M = 1024, 512, 768, 2048, 1024, 2048, 1024
FLOPS = 2 * K * H * S * 3 + 2 * H * N * M

F32 = mybir.dt.float32
BF16 = mybir.dt.bfloat16
I32 = mybir.dt.int32
U32 = mybir.dt.uint32
U16 = mybir.dt.uint16
U8 = mybir.dt.uint8
FP8X4 = mybir.dt.float8_e4m3fn_x4
FP4X4 = mybir.dt.float4_e2m1fn_x4
ALU = mybir.AluOpType
ACT = mybir.ActivationFunctionType

P = 128
PACK = 4
STRIPE = 16
QUADRANT = 32
PLANE_ROWS = 4
SECOND_PLANE = 16
PASSES = K // (P * PACK)
PAGES = H // P
BANK = 512
CHUNK = 256
WO_RAW_BYTES = 4 * PACK * N
TURNED_BYTES = 4 * 2 * PACK * P
PLACES = {"above": 960, "x": 1024, "x2": 2048, "before": 1088, "behind": 3008}
REGION = 3072
FILLER = 64


def woven(planes):
    return planes.rearrange("p i (c e) -> p c i e", e=2)


def woven_out(words):
    return words.rearrange("p (c e) i -> p c i e", e=2)


def tile_list_latency_envelopes_kernel(
    tc, tab_words, tab_scales, offs, offs2, offs3, w1, w2_words, w2_scales,
    w3_words, w3_scales, wgs, load, wo, out,
):
    nc = tc.nc
    with ExitStack() as ctx:
        keep = ctx.enter_context(tc.tile_pool(name="keep", bufs=1))
        shared = ctx.enter_context(tc.tile_pool(name="shared", bufs=1))
        psum = ctx.enter_context(tc.psum_pool(name="psum", bufs=1))

        def on(tag, shape, dtype):
            return keep.tile(shape, dtype, name=tag, tag=tag, align_bytes=64)

        def bank(k, shape=(P, BANK)):
            return psum.tile(list(shape), F32, name="bank", tag="bank%d" % k)

        def placed(u, place, shape, dtype):
            offset = WO_RAW_BYTES + TURNED_BYTES + (u - 2) * REGION + PLACES[place]
            return shared.tile(shape, dtype, name="%s%d_%d" % (place, u, shape[1]), align_bytes=64, offset=offset)

        idx1 = keep.tile([P, S // STRIPE], U16, name="idx1")
        idx2 = keep.tile([P, S // STRIPE], U16, name="idx2")
        idx3 = keep.tile([P, M // STRIPE], U16, name="idx3")

        def entries(idx, j0, j1):
            return idx[:, j0 // STRIPE : j1 // STRIPE]

        tab_s = on("tab_s", [P, T], U8)
        w2_s = on("w2_s", [P, PASSES, H], U8)
        w3_s = on("w3_s", [P, PASSES, H], U8)
        v_s1 = on("v_s1", [P, S], U8)
        nc.gpsimd.memset(tab_s[:].bitcast(I32), 0)
        nc.gpsimd.memset(w2_s[:].rearrange("p a c -> p (a c)").bitcast(I32), 0)
        nc.gpsimd.memset(w3_s[:].rearrange("p a c -> p (a c)").bitcast(I32), 0)
        nc.gpsimd.memset(v_s1[:].bitcast(I32), 0)
        ident = keep.tile([P, P], F32, name="ident")
        make_identity(nc, ident[:])

        pages = {}

        def open_page(b):
            pages[b] = on(("page0", "w1_bf1", "low1", "below3")[b], [P, T2], F32)
            nc.gpsimd.memset(pages[b][:].bitcast(I32), 0)

        open_page(0)

        tab_w = [on("tab_w%d" % a, [P, T], I32) for a in range(PASSES)]
        w1_rows = w1.rearrange("(a p i) c -> a p i c", a=PASSES, i=PACK)
        w2_rows = w2_words.rearrange("a p c i -> p a (c i)")
        w3_rows = w3_words.rearrange("a p c -> p a c")
        w1_raw, w2_c, w3_c = {}, {}, {}

        def load_w1(a, b0, b1):
            raw = on("w1_raw%d_%d" % (b0, a), [P, PACK, (b1 - b0) * P], F32)
            nc.sync.dma_start(raw[:], w1_rows[a][:, :, b0 * P : b1 * P])
            for b in range(b0, b1):
                w1_raw[b, a] = raw[:, :, (b - b0) * P : (b - b0 + 1) * P]

        def load_packed(b0, b1):
            words = on("w1_bf1" if b0 == 0 else "w2_c%d" % b0, [P, PASSES, (b1 - b0) * P], U32)
            nc.sync.dma_start(words[:].bitcast(I32), w2_rows[:, :, 4 * b0 * P : 4 * b1 * P].bitcast(I32))
            nibbles = on("w3_c%d" % b0, [P, PASSES, 2 * (b1 - b0) * P], U8)
            nc.sync.dma_start(nibbles[:].bitcast(I32), w3_rows[:, :, 2 * b0 * P : 2 * b1 * P].bitcast(I32))
            for b in range(b0, b1):
                for a in range(PASSES):
                    w2_c[b, a] = words[:, a, (b - b0) * P : (b - b0 + 1) * P].bitcast(FP8X4)
                    w3_c[b, a] = nibbles[:, a, 2 * (b - b0) * P : 2 * (b - b0 + 1) * P].bitcast(FP4X4)

        def load_scale_rows(rows_of, scales):
            for row in range(PLANE_ROWS):
                nc.sync.dma_start(
                    rows_of(row).bitcast(I32),
                    scales.bitcast(I32)[:, row : 4 * PLANE_ROWS : PLANE_ROWS, :].rearrange("a q c -> q a c"),
                )

        def load_table_words(a):
            nc.sync.dma_start(tab_w[a][:], tab_words[a].rearrange("p t i -> p (t i)").bitcast(I32))

        nc.sync.dma_start(idx1[:], offs)
        load_scale_rows(lambda row: tab_s[row:P:SECOND_PLANE, :], tab_scales)
        load_packed(0, 1)
        load_table_words(0)
        load_scale_rows(lambda row: w2_s[row:P:QUADRANT, :, :], w2_scales)
        load_table_words(1)
        load_scale_rows(lambda row: w3_s[row:P:QUADRANT, :, :], w3_scales)
        load_w1(0, 0, 1)
        v_s = on("v_s", [P, S], U8)
        nc.vector.tensor_copy(v_s[:], tab_s[:].indirect(idx1[:]))
        plane_span = P - QUADRANT + PLANE_ROWS

        nc.sync.dma_start(
            v_s1[0:plane_span, :].bitcast(I32), v_s[SECOND_PLANE : SECOND_PLANE + plane_span, :].bitcast(I32)
        )
        load_w1(1, 0, 1)
        planes = [v_s[:], v_s1[:]]
        for a in range(PASSES):
            load_w1(a, 1, 2)
        wgs_sb = [keep.tile([P, BANK], F32, name="wgs%d" % half) for half in range(2)]
        load_packed(1, 2)
        nc.sync.dma_start(wgs_sb[0][:], wgs[:, :BANK])
        nc.sync.dma_start(idx2[:], offs2)
        for a in range(PASSES):
            load_w1(a, 2, 3)
        load_w1(0, 3, PAGES)
        nc.sync.dma_start(wgs_sb[1][:], wgs[:, BANK:])
        load_w1(1, 3, PAGES)
        load_packed(2, PAGES)
        nc.sync.dma_start(idx3[:], offs3)
        wo_raw = {}
        for n0, n1 in ((0, CHUNK), (CHUNK, 3 * P), (3 * P, N)):
            raw = shared.tile([P, PACK, n1 - n0], F32, name="wo_raw%d" % n0, align_bytes=64, offset=4 * PACK * n0)
            nc.sync.dma_start(raw[:], wo.rearrange("(p i) n -> p i n", i=PACK)[:, :, n0:n1])
            for n in range(n0, n1, P):
                wo_raw[n // P] = raw[:, :, n - n0 : n - n0 + P]
        load_rows = load.rearrange("(p i) m -> p i m", i=PACK)
        load_sb = keep.tile([P, PACK, M], F32, name="load_sb")
        nc.sync.dma_start(load_sb[:], load_rows)

        v_w = {}

        def gather_words(a, half):
            v_w[a, half] = on("v_w%d%d" % (a, half), [P, BANK], U32)
            nc.vector.tensor_copy(
                v_w[a, half][:], tab_w[a][:].bitcast(U32).indirect(entries(idx1, half * BANK, (half + 1) * BANK))
            )

        w1_c, w1_s = {}, {}

        def quantize_w1(b, passes, tag, cast=nc.scalar.copy):
            a0, count = passes[0], len(passes)
            rounded = on(tag, [P, count, P, PACK], BF16)
            codes = on("w1_c%d%d" % (b, a0), [P, count * P], U32)
            scales = on("w1_s%d%d" % (b, a0), [P, count * P], U8)
            for n, a in enumerate(passes):
                cast(woven_out(rounded[:, n, :, :]), woven(w1_raw[b, a]))
                w1_c[b, a] = codes[:, n * P : (n + 1) * P].bitcast(FP8X4)
                w1_s[b, a] = scales[:, n * P : (n + 1) * P]
            nc.vector.quantize_mx(
                out=codes[:].bitcast(FP8X4), scales=scales[:], in_=rounded[:].rearrange("p a c i -> p (a c i)")
            )

        def quantize_block(rounded, codes, tag):
            scales = on(tag, [P, P], U8)
            nc.vector.quantize_mx(
                out=codes[:].bitcast(FP8X4), scales=scales[:], in_=rounded[:].rearrange("p c i -> p (c i)")
            )
            return codes[:].bitcast(FP8X4), scales[:]

        gather_words(0, 0)
        quantize_w1(0, [0], "w1_bf0")
        quantize_w1(0, [1], "w1_bf01", nc.vector.tensor_copy)
        gather_words(1, 0)
        gather_words(0, 1)
        gather_words(1, 1)

        units = [(b, half) for b in range(PAGES) for half in range(2)]
        last = len(units) - 1

        def estimate(u, k, codes, scales):
            b, half = units[u]
            acc = bank(k)
            for a in range(PASSES):
                nc.tensor.matmul_mx(
                    out=acc[:], lhsT=codes[b, a], lhsT_scale=scales(b, a),
                    rhs=v_w[a, half][:].bitcast(FP8X4), rhs_scale=planes[a][:, half * BANK : (half + 1) * BANK],
                    start=(a == 0), stop=(a == PASSES - 1),
                )
            return acc

        def e1(u, k):
            return estimate(u, k, w1_c, lambda b, a: w1_s[b, a])

        def e2(u, k):
            return estimate(u, k, w2_c, lambda b, a: w2_s[:, a, b * P : (b + 1) * P])

        def e3(u, k):
            return estimate(u, k, w3_c, lambda b, a: w3_s[:, a, b * P : (b + 1) * P])

        def turned_sum(early, late, k):
            acc = bank(k)
            for tile in (early, late):
                for c0 in range(0, BANK, P):
                    nc.tensor.matmul(
                        acc[:, c0 : c0 + P], tile[:, c0 : c0 + P], ident[:],
                        start=tile is early and c0 == 0, stop=tile is late and c0 == BANK - P, is_transpose=True,
                    )
            return acc

        def copy_out(tag, acc, func, scale):
            tile = on(tag, [P, BANK], F32) if isinstance(tag, str) else placed(tag, "above", [P, BANK], F32)
            nc.scalar.activation(tile[:], acc[:], func, scale=scale)
            return tile

        def put(u, h):
            b, half = units[u]
            nc.vector.tensor_tensor(
                pages[b][:].indirect(entries(idx2, half * BANK, (half + 1) * BANK)), h[:], wgs_sb[half][:], ALU.mult
            )

        def fetch(b, m0, m1, x):
            nc.vector.tensor_copy(x[:], pages[b][:].indirect(entries(idx3, m0, m1)))
            return x

        pos2, neg1, neg3, below, above = {}, {}, {}, {}, {}
        sum_bank = 2

        def copy_e2(u, k):
            pos2[u] = copy_out({0: "w1_c10", 1: "pos2_first"}.get(u, "pos2_%d" % (u % 2)), e2(u, k), ACT.Copy, 1.0)

        def negate_e3(u):
            neg3[u] = copy_out("w1_bf2" if u == 2 else "neg3_%d" % (u % 2), e3(u, 5), ACT.Copy, -1.0)

        def negate_e1(u):
            neg1[u] = copy_out("neg1_%d" % (u % 2), e1(u, 6), ACT.Copy, -1.0)

        def lower_part(u):
            below[u] = copy_out("below%d" % u, turned_sum(neg3[u], pos2[u], 0), ACT.Relu, 1.0)

        def upper_part(u):
            above[u] = copy_out(u, turned_sum(pos2[u], neg1[u], 1), ACT.Relu, -1.0)

        moved = {m0: on("moved%d" % m0, [P, PACK, CHUNK], F32) for m0 in range(CHUNK, M, CHUNK)}

        def move(b, m0, x, e):
            nc.scalar.activation(e[:], x, ACT.Exp, scale=-1.0)
            for c in range(0, x.shape[1], CHUNK):
                nc.sync.dma_start(moved[m0 + c][QUADRANT * b : QUADRANT * (b + 1), :, :], e[:, c : c + CHUNK])

        turned = [
            shared.tile([P, PACK, P], F32, name="turned%d" % s, align_bytes=64, offset=WO_RAW_BYTES + s * TURNED_BYTES // 2)
            for s in range(2)
        ]

        def turn_in(s, b0, xs, k):
            acc = bank(k, (P, len(xs), P))
            for n, x in enumerate(xs):
                nc.tensor.transpose(acc[:, n, :], x, ident[:])
            nc.scalar.activation(
                turned[s][:, :, QUADRANT * b0 : QUADRANT * (b0 + len(xs))],
                acc[:].rearrange("m b (q i) -> m i (b q)", i=PACK), ACT.Exp, scale=-1.0,
            )

        def turn_back(s, k):
            acc = bank(k, (P, PACK, P))
            for i in range(PACK):
                nc.tensor.transpose(acc[:, i, :], turned[s][:, i, :], ident[:])
            return acc

        copy_e2(0, 3)
        e3_0, e1_0 = e3(0, 5), e1(0, 6)
        copy_e2(1, 7)
        e3_1, e1_1 = e3(1, 4), e1(1, 3)

        def bounds(u, e1_u, e3_u, tag):
            low = on("low%d" % u, [P, BANK], F32)
            high = on(tag, [P, BANK], F32)
            steps = [(low, e3_u, ALU.min), (high, e1_u, ALU.max)]
            for bound, estimate_u, op in steps:
                nc.vector.tensor_tensor(bound[:], estimate_u[:], pos2[u][:], op)
            return high, low

        def difference(u, high, low):
            h = on("h%d" % (u % 4), [P, BANK], F32)
            nc.vector.tensor_tensor(h[:], high[:], low[:], ALU.subtract)
            return h

        first = bounds(0, e1_0, e3_0, "high0")
        quantize_w1(1, [0, 1], "w1_bf1")
        h = difference(0, *first)
        second = bounds(1, e1_1, e3_1, "high1")
        open_page(1)
        put(0, h)
        h = difference(1, *second)
        open_page(2)
        negate_e3(2)
        copy_e2(2, 7)
        negate_e1(2)
        put(1, h)

        x, wo_c, wo_s = {}, {}, {}
        wo_bf = {}

        def round_wo(t, tile):
            wo_bf[t] = tile
            nc.scalar.copy(out=woven_out(tile[:]), in_=woven(wo_raw[t]))

        def quantize_wo(t, codes):
            wo_c[t], wo_s[t] = quantize_block(wo_bf[t], codes, "wo_s%d" % t)

        def behind_scatter(u):
            b = (u - 1) // 2
            if u % 2 == 0:
                x[b, CHUNK] = fetch(b, CHUNK, 3 * CHUNK, placed(u + 1, "x", [P, 2 * CHUNK], F32))
                return
            if b > 0:
                x[b - 1, 3 * CHUNK] = fetch(b - 1, 3 * CHUNK, M, placed(u + 1, "x", [P, CHUNK], F32))
            x[b, 0] = fetch(b, 0, CHUNK, placed(u + 1, "x2", [P, CHUNK], F32))

        for u in range(2, last + 1):
            lower_part(u)
            if u < last:
                negate_e3(u + 1)
            upper_part(u)
            if u == 2:
                quantize_w1(2, [0, 1], "w1_bf2")
            if u < last:
                copy_e2(u + 1, 7)
            if u < last:
                negate_e1(u + 1)
            acc = turned_sum(below[u], above[u], sum_bank)
            if u < 4:
                quantize_w1(3, [u - 2], "below%d" % u)
                if u == 3:
                    open_page(u)
            else:
                b, m0 = (u - 4) // 2, CHUNK * (1 + 2 * (u % 2))
                move(b, m0, x[b, m0][:], on("below%d" % u, list(x[b, m0].shape), F32))
            h = on("h%d" % (u % 4), [P, BANK], F32)
            nc.scalar.copy(h[:], acc[:])
            if u > 5:
                round_wo(u - 6, on("neg1_%d" % (u % 2), [P, P, PACK], BF16))
            behind_scatter(u - 1)
            put(u, h)

        other_bank = 1
        for s in range(2):
            turn_in(s, 0, [x[b, 0][:, s * P : (s + 1) * P] for b in range(3)], (other_bank, sum_bank)[s])
        for t, u, place in ((2, 4, "before"), (3, 4, "behind"), (4, 6, "before"), (5, 6, "behind")):
            round_wo(t, placed(u, place, [P, P, PACK], BF16))
        move(2, CHUNK, x[2, CHUNK][:], shared.tile([P, 2 * CHUNK], F32, name="behind_wo", align_bytes=64, offset=4 * PACK * CHUNK))

        def behind_turn(t):
            offset = WO_RAW_BYTES + 4 * P * t
            quantize_wo(t, shared.tile([P, P], U32, name="wo_c%d" % t, align_bytes=64, offset=offset))

        def damp(z, factor, m0):
            width = z.shape[1]
            nc.vector.tensor_tensor(woven_out(z), woven(factor), woven(load_sb[:, :, m0 : m0 + width]), ALU.mult)

        def quantize_z(z, m0):
            width = z.shape[1]
            z_c = on("z_c%d" % m0, [P, width], U32)
            z_s = on("z_s%d" % m0, [P, width], U8)
            nc.vector.quantize_mx(out=z_c[:].bitcast(FP8X4), scales=z_s[:], in_=z[:].rearrange("p m i -> p (m i)"))
            return z_c, z_s, m0

        out_rows = out.rearrange("(t p) m -> p t m", p=P)
        result_banks = (5, 6, 7, 0, 1, 2, 3, 4)
        results = [on(tag, [P, 2, M], F32) for tag in ("tab_w0", "tab_w1", "page0")]
        stored = [0] * (N // P)
        done = []

        def project(z_q, t0, t1, leaves, copy=nc.scalar.copy):
            z_c, z_s, m0 = z_q
            m1 = m0 + z_c.shape[1]
            acc = bank(result_banks[len(done) % len(result_banks)], (P, t1 - t0, m1 - m0))
            done.append(acc)
            for t in range(t0, t1):
                nc.tensor.matmul_mx(
                    out=acc[:, t - t0, :], lhsT=wo_c[t], lhsT_scale=wo_s[t],
                    rhs=z_c[:].bitcast(FP8X4), rhs_scale=z_s[:], start=True, stop=True,
                )
            rows = results[t0 // 2][:, t0 % 2 : t0 % 2 + t1 - t0, :]
            copy(rows[:, :, m0:m1], acc[:])
            if leaves:
                nc.sync.dma_start(out_rows[:, t0:t1, stored[t0] : m1], rows[:, :, stored[t0] : m1])
                stored[t0:t1] = [m1] * (t1 - t0)

        end = fetch(2, M - CHUNK, M, placed(2, "x2", [P, CHUNK], F32))
        move(2, M - CHUNK, end[:], on("end_e", [P, CHUNK], F32))
        back = []
        for n, m0 in enumerate(range(CHUNK, M, CHUNK)):
            if n < 2:
                late = fetch(3, n * P, (n + 1) * P, on("high%d" % n, [P, P], F32))
                turn_in(n, 3, [late[:]], (other_bank, sum_bank)[n])
                back.append(turn_back(n, 3 + n))
            late = fetch(3, m0, m0 + CHUNK, on("late%d" % n, [P, CHUNK], F32))
            move(3, m0, late[:], on(("high0", "high1", "late0")[n], [P, CHUNK], F32))
        z = {m0: on("z%d" % m0, [P, P if m0 < CHUNK else CHUNK, PACK], BF16) for m0 in (0, P, *range(CHUNK, M, CHUNK))}
        damp(z[0][:], back[0][:], 0)
        behind_turn(0)
        behind_turn(1)
        z_q = quantize_z(z[0], 0)
        project(z_q, 0, 1, True)
        project(z_q, 1, 2, True)
        behind_turn(2)
        behind_turn(3)
        project(z_q, 2, 4, True)
        damp(z[P][:], back[1][:], P)
        behind_turn(4)
        behind_turn(5)
        project(z_q, 4, 6, True)
        z_q = quantize_z(z[P], P)
        for t0, t1, leaves in ((0, 2, True), (2, 4, True), (4, 6, True)):
            project(z_q, t0, t1, leaves)
        damp(z[CHUNK][:], moved[CHUNK][:], CHUNK)
        z_q = quantize_z(z[CHUNK], CHUNK)
        for t0, t1, leaves in ((0, 1, True), (1, 2, True), (2, 4, True), (4, 6, True)):
            project(z_q, t0, t1, leaves)
        for c0, c1 in ((0, FILLER), (FILLER, CHUNK)):
            damp(z[BANK][:, c0:c1, :], moved[BANK][:, :, c0:c1], BANK + c0)
        z_q = quantize_z(z[BANK], BANK)
        for t0, t1, leaves in ((0, 2, False), (2, 4, False), (4, 6, False)):
            project(z_q, t0, t1, leaves)
        for c0, c1 in ((0, FILLER), (FILLER, CHUNK)):
            damp(z[M - CHUNK][:, c0:c1, :], moved[M - CHUNK][:, :, c0:c1], M - CHUNK + c0)
        z_q = quantize_z(z[M - CHUNK], M - CHUNK)
        for t0, t1, copy in ((0, 1, nc.vector.tensor_copy), (1, 2, nc.vector.tensor_copy), (2, 4, nc.vector.tensor_copy), (4, 6, nc.scalar.copy)):
            project(z_q, t0, t1, True, copy)
